import numpy as np
import ml_dtypes


def mxq(x, axis, fmt="e4m3"):
    dtype, down = {"e4m3": (ml_dtypes.float8_e4m3fn, 7), "e5m2": (ml_dtypes.float8_e5m2, 14)}[fmt]
    v = np.moveaxis(np.asarray(x, np.float32).astype(ml_dtypes.bfloat16).astype(np.float64), axis, -1)
    blocks = v.reshape(v.shape[:-1] + (-1, 32))
    amax = np.abs(blocks).max(-1, keepdims=True)
    byte = np.maximum(np.where(amax > 0, np.frexp(amax)[1] - 1 + 127, 0) - down, 1)
    scale = np.exp2(byte - 127.0)
    codes = (blocks / scale).astype(np.float32).astype(dtype).astype(np.float64)
    return np.moveaxis((codes * scale).reshape(v.shape), -1, axis)


WIDE = False


def mx_kscale(k):
    if not WIDE:
        return np.ones(k)
    levels = np.array([30, -30])
    if k % 512:
        return np.exp2(np.random.permutation(np.resize(levels, k // 32))).repeat(32)
    a = np.empty((k // 512, 16))
    for p in range(k // 512):
        a[p, :8] = np.random.permutation(np.resize(levels, 8))
        for g in range(8):
            far = levels[np.abs(levels - a[p, g]) >= 10]
            a[p, g + 8] = far[np.random.randint(len(far))]
    return np.exp2(a.ravel()).repeat(32)


def f64(x):
    return np.asarray(x).astype(np.float64)


def striped(idx):
    return np.tile(idx.reshape(-1, 16).T, (8, 1)).astype(np.uint16)


def unstriped(offs):
    return offs[:16].T.reshape(-1).astype(np.int64)


def relu(v):
    return np.maximum(v, 0.0)


def d_relu(v):
    return (v > 0).astype(np.float64)


K, T, E, C, H, N = 128, 2048, 4, 512, 512, 1024


def by_expert(wq, xq):
    return np.concatenate([wq[e].T @ xq[:, e * C:(e + 1) * C] for e in range(E)], axis=1)


def setup_inputs():
    n = np.random.standard_normal
    s = mx_kscale(N)[:, None]
    u = mx_kscale(H)
    return {
        "dyT": (n((N, T)) * s).astype(np.float32),
        "a1": n((H, E * C)).astype(np.float32),
        "a3": n((H, E * C)).astype(np.float32),
        "w2": (n((E, N, H)) / np.sqrt(N) / s[None] * u[None, None, :]).astype(np.float32),
        "w1": (n((E, H, K)) / np.sqrt(H) / u[None, :, None]).astype(np.float32),
        "w3": (n((E, H, K)) / np.sqrt(H) / u[None, :, None]).astype(np.float32),
        "gate": np.tile(np.random.uniform(0.2, 1.0, E * C), (N, 1)).astype(np.float32),
        "offs": striped(np.random.permutation(T)[:E * C]),
    }


def reference(dyT, a1, a3, w2, w1, w3, gate, offs):
    idx = unstriped(offs)
    gq = mxq(f64(gate) * f64(dyT)[:, idx], 0, "e5m2")
    dh = by_expert(mxq(f64(w2), 1, "e4m3"), gq)
    da1 = dh * f64(a3) * d_relu(f64(a1))
    da3 = dh * relu(f64(a1))
    dx = by_expert(mxq(f64(w1), 1, "e4m3"), mxq(da1, 0, "e5m2")) + by_expert(mxq(f64(w3), 1, "e4m3"), mxq(da3, 0, "e5m2"))
    out = np.zeros((K, T))
    out[:, idx] = dx
    return out

@@ -1,0 +1,263 @@
+from contextlib import ExitStack
+
+import concourse.mybir as mybir
+
+E, C, T, K, H, N = 4, 512, 2048, 128, 512, 1024
+P = 128
+PACK = 4
+PASSES = N // (P * PACK)
+PAIR = 2 * C
+GQ = 3
+WQ = 2
+WR = 3
+
+F32 = mybir.dt.float32
+BF16 = mybir.dt.bfloat16
+U32 = mybir.dt.uint32
+U16 = mybir.dt.uint16
+U8 = mybir.dt.uint8
+E4M3X4 = mybir.dt.float8_e4m3fn_x4
+E5M2X4 = mybir.dt.float8_e5m2_x4
+MULT = mybir.AluOpType.mult
+IS_GT = mybir.AluOpType.is_gt
+
+FLOPS = 2 * N * H * E * C + 2 * 2 * H * K * E * C
+BYTES = 4 * (N * T + 2 * H * E * C + E * N * H + 2 * E * H * K + E * C + K * T) + 2 * P * (E * C // 16)
+
+
+def tile_moe_bdx_glu_relu_kernel(tc, dyT, a1, a3, w2, w1, w3, gate, offs, out):
+    nc = tc.nc
+
+    dy_rows = dyT.rearrange("(c p t) w -> c t p w", c=PASSES, t=PACK)
+    w2_rows = w2.rearrange("e (c p j) i -> e c p j i", c=PASSES, j=PACK)
+    a1_rows = a1.rearrange("(p t) (e s) -> e p t s", t=PACK, e=E)
+    a3_rows = a3.rearrange("(p t) (e s) -> e p t s", t=PACK, e=E)
+
+    with ExitStack() as ctx:
+        held = ctx.enter_context(tc.tile_pool(name="held", bufs=1))
+        raw = ctx.enter_context(tc.tile_pool(name="raw", bufs=8))
+        wraw = ctx.enter_context(tc.tile_pool(name="wraw", bufs=WR))
+        gpool = ctx.enter_context(tc.tile_pool(name="gpool", bufs=2))
+        work = ctx.enter_context(tc.tile_pool(name="work", bufs=2))
+        codes = ctx.enter_context(tc.tile_pool(name="codes", bufs=6))
+        psum = ctx.enter_context(tc.psum_pool(name="psum", bufs=1))
+
+        def load(src, shape):
+            big = raw.tile(shape, F32, tag="big", align_bytes=64, name="big")
+            nc.sync.dma_start(big[:], src)
+            return big
+
+        def load_w(src, shape):
+            mat = wraw.tile(shape, F32, tag="mat", align_bytes=64, name="mat")
+            nc.sync.dma_start(mat[:], src)
+            return mat
+
+        def quantize(src, width, tag, dtype, bufs):
+            words = codes.tile([P, width], U32, tag=tag + "_w", bufs=bufs, align_bytes=64, name=tag + "_w")
+            scales = codes.tile([P, width], U8, tag=tag + "_s", bufs=bufs, align_bytes=64, name=tag + "_s")
+            nc.vector.quantize_mx(out=words[:].bitcast(dtype), scales=scales[:], in_=src[:])
+            return words, scales
+
+        offsets = held.tile([P, E * C // 16], U16, name="offsets")
+        nc.sync.dma_start(offsets[:], offs)
+        dy = {}
+        gates = {}
+        w2_raw = {}
+        w13_raw = {}
+        a1_raw = {}
+        a3_raw = {}
+        for pair in range(2):
+            gates[pair] = held.tile([P, PAIR], F32, name="gate%d" % pair)
+        dy[0, 0] = load(dy_rows[0, 0], [P, T])
+        nc.sync.dma_start(gates[0][:, 0:512], gate[0:P, 0:512])
+        nc.sync.dma_start(gates[0][:, 512:1024], gate[0:P, 512:1024])
+        dy[0, 1] = load(dy_rows[0, 1], [P, T])
+        dy[0, 2] = load(dy_rows[0, 2], [P, T])
+        dy[0, 3] = load(dy_rows[0, 3], [P, T])
+        dy[1, 0] = load(dy_rows[1, 0], [P, T])
+        dy[1, 1] = load(dy_rows[1, 1], [P, T])
+        dy[1, 2] = load(dy_rows[1, 2], [P, T])
+        w2_raw[0, 0] = load_w(w2_rows[0, 0], [P, PACK, H])
+        dy[1, 3] = load(dy_rows[1, 3], [P, T])
+        nc.sync.dma_start(gates[1][:, 0:1024], gate[0:P, 1024:2048])
+        w2_raw[0, 1] = load_w(w2_rows[0, 1], [P, PACK, H])
+        w13_raw[0] = load_w(w1.rearrange("e (p j) k -> p e j k", j=PACK), [P, E, PACK, K])
+        result = held.tile([P, T], F32, name="result")
+
+        g_b = {}
+        g_q = {}
+        w2_b = {}
+        w2_q = {}
+
+        def gather(pair, c, t, planes, cuts=(0, PAIR)):
+            for lo, hi in zip(cuts, cuts[1:]):
+                nc.vector.tensor_tensor(
+                    planes[:, t, lo:hi],
+                    dy[c, t][:].indirect(offsets[:, (pair * PAIR + lo) // 16 : (pair * PAIR + hi) // 16]),
+                    gates[pair][:, lo:hi],
+                    MULT,
+                )
+
+        def prepare_g(pair, c, planes):
+            gb = work.tile([P, PACK * PAIR], BF16, tag="gb", bufs=2, align_bytes=64, name="gb")
+            nc.scalar.copy(
+                out=gb[:].rearrange("p (s i t) -> p s t i", i=4, t=PACK),
+                in_=planes[:].rearrange("p t (s i) -> p s t i", i=4),
+            )
+            g_b[pair, c] = gb
+
+        def quantize_g(pair, c):
+            g_q[pair, c] = quantize(g_b[pair, c], PAIR, "g", E5M2X4, GQ)
+
+        def round_w2(e, c):
+            if c == 0:
+                w2_b[e] = work.tile([P, PASSES * PACK * H], BF16, tag="wb", bufs=2, align_bytes=64, name="wb")
+            nc.scalar.copy(
+                out=w2_b[e][:, c * PACK * H : (c + 1) * PACK * H].rearrange("p (t m j) -> p m j t", t=PACK, j=PACK),
+                in_=w2_raw[e, c][:].rearrange("p j (m t) -> p m j t", t=PACK),
+            )
+
+        def quantize_w2(e):
+            w2_q[e] = quantize(w2_b[e], PASSES * H, "w2", E4M3X4, WQ)
+
+        w13_b = {}
+
+        def round_w13(n):
+            if n == 0:
+                w13_b[0] = work.tile([P, PASSES * PACK * H], BF16, tag="wb", bufs=2, align_bytes=64, name="wb")
+            nc.scalar.copy(
+                out=w13_b[0][:, n * PACK * H : (n + 1) * PACK * H].rearrange("p (e k j) -> p e k j", e=E, j=PACK),
+                in_=w13_raw[n][:].rearrange("p e j k -> p e k j"),
+            )
+
+        def quantize_w13():
+            return quantize(w13_b[0], 2 * E * K, "w13", E4M3X4, 1)
+
+        def first_product(e):
+            dh = work.tile([P, PACK, C], F32, tag="dh", bufs=2, align_bytes=64, name="dh")
+            for t in range(PACK):
+                bank = psum.tile([P, C], F32, tag="bank", bufs=6, name="bank")
+                for c in range(PASSES):
+                    nc.tensor.matmul_mx(
+                        out=bank[:],
+                        lhsT=w2_q[e][0][:, c * H + t * P : c * H + (t + 1) * P].bitcast(E4M3X4),
+                        lhsT_scale=w2_q[e][1][:, c * H + t * P : c * H + (t + 1) * P],
+                        rhs=g_q[e // 2, c][0][:, e % 2 * C : (e % 2 + 1) * C].bitcast(E5M2X4),
+                        rhs_scale=g_q[e // 2, c][1][:, e % 2 * C : (e % 2 + 1) * C],
+                        start=(c == 0),
+                        stop=(c == PASSES - 1),
+                    )
+                nc.vector.scalar_tensor_tensor(dh[:, t, :], a1_raw[e][:, t, :], 0.0, bank[:], op0=IS_GT, op1=MULT)
+            return dh
+
+        def walk_in(x):
+            return x[:].rearrange("p t (s i) -> p s t i", i=2)
+
+        def derivative(e, dh):
+            d1 = work.tile([P, PACK * C], BF16, tag="da", bufs=2, align_bytes=64, name="d1")
+            d3 = work.tile([P, PACK * C], BF16, tag="da", bufs=2, align_bytes=64, name="d3")
+            nc.vector.tensor_tensor(
+                d1[:].rearrange("p (s i t) -> p s t i", i=2, t=PACK), walk_in(a3_raw[e]), walk_in(dh), MULT
+            )
+            nc.vector.tensor_tensor(
+                d3[:].rearrange("p (s i t) -> p s t i", i=2, t=PACK), walk_in(a1_raw[e]), walk_in(dh), MULT
+            )
+            return quantize(d1, C, "da", E5M2X4, 4), quantize(d3, C, "da", E5M2X4, 4)
+
+        def second_product(e, da):
+            bank = psum.tile([P, C], F32, tag="dx", bufs=2, name="dxbank")
+            for n, dq in enumerate(da):
+                nc.tensor.matmul_mx(
+                    out=bank[:],
+                    lhsT=w13_q[0][:, (n * E + e) * K : (n * E + e + 1) * K].bitcast(E4M3X4),
+                    lhsT_scale=w13_q[1][:, (n * E + e) * K : (n * E + e + 1) * K],
+                    rhs=dq[0][:].bitcast(E5M2X4),
+                    rhs_scale=dq[1][:],
+                    start=(n == 0),
+                    stop=(n == 1),
+                )
+            dx = work.tile([P, C], F32, tag="dx", bufs=2, align_bytes=64, name="dx")
+            nc.scalar.copy(out=dx[:], in_=bank[:])
+            return dx
+
+        def scatter(e, dx):
+            nc.vector.tensor_copy(result[:].indirect(offsets[:, e * C // 16 : (e + 1) * C // 16]), dx[:])
+
+        dh = {}
+        da = {}
+        dx = {}
+        planes = gpool.tile([P, PACK, PAIR], F32, tag="planes", align_bytes=64, name="planes")
+        gather(0, 0, 0, planes, (0, C, PAIR))
+        gather(0, 0, 1, planes)
+        gather(0, 0, 2, planes)
+        gather(0, 0, 3, planes)
+        prepare_g(0, 0, planes)
+        round_w2(0, 0)
+        w13_raw[1] = load_w(w3.rearrange("e (p j) k -> p e j k", j=PACK), [P, E, PACK, K])
+        planes = gpool.tile([P, PACK, PAIR], F32, tag="planes", align_bytes=64, name="planes")
+        gather(0, 1, 0, planes)
+        gather(0, 1, 1, planes)
+        gather(0, 1, 2, planes)
+        gather(0, 1, 3, planes)
+        prepare_g(0, 1, planes)
+        round_w2(0, 1)
+        w2_raw[1, 0] = load_w(w2_rows[1, 0], [P, PACK, H])
+        round_w13(0)
+        w2_raw[1, 1] = load_w(w2_rows[1, 1], [P, PACK, H])
+        round_w13(1)
+        planes = gpool.tile([P, PACK, PAIR], F32, tag="planes", align_bytes=64, name="planes")
+        gather(1, 0, 0, planes)
+        a1_raw[0] = load(a1_rows[0], [P, PACK, C])
+        gather(1, 0, 1, planes)
+        a3_raw[0] = load(a3_rows[0], [P, PACK, C])
+        gather(1, 0, 2, planes)
+        a1_raw[1] = load(a1_rows[1], [P, PACK, C])
+        gather(1, 0, 3, planes)
+        a3_raw[1] = load(a3_rows[1], [P, PACK, C])
+        round_w2(1, 0)
+        w2_raw[2, 0] = load_w(w2_rows[2, 0], [P, PACK, H])
+        round_w2(1, 1)
+        w2_raw[2, 1] = load_w(w2_rows[2, 1], [P, PACK, H])
+        quantize_g(0, 0)
+        quantize_g(0, 1)
+        quantize_w2(0)
+        dh[0] = first_product(0)
+        prepare_g(1, 0, planes)
+        planes = gpool.tile([P, PACK, PAIR], F32, tag="planes", align_bytes=64, name="planes")
+        gather(1, 1, 0, planes)
+        gather(1, 1, 1, planes)
+        gather(1, 1, 2, planes)
+        gather(1, 1, 3, planes)
+        prepare_g(1, 1, planes)
+        w2_raw[3, 0] = load_w(w2_rows[3, 0], [P, PACK, H])
+        da[0] = derivative(0, dh[0])
+        w13_q = quantize_w13()
+        quantize_w2(1)
+        dh[1] = first_product(1)
+        dx[0] = second_product(0, da[0])
+        da[1] = derivative(1, dh[1])
+        round_w2(2, 0)
+        w2_raw[3, 1] = load_w(w2_rows[3, 1], [P, PACK, H])
+        round_w2(2, 1)
+        a1_raw[2] = load(a1_rows[2], [P, PACK, C])
+        a3_raw[2] = load(a3_rows[2], [P, PACK, C])
+        dx[1] = second_product(1, da[1])
+        scatter(0, dx[0])
+        quantize_g(1, 0)
+        quantize_g(1, 1)
+        round_w2(3, 0)
+        round_w2(3, 1)
+        quantize_w2(2)
+        dh[2] = first_product(2)
+        a1_raw[3] = load(a1_rows[3], [P, PACK, C])
+        a3_raw[3] = load(a3_rows[3], [P, PACK, C])
+        da[2] = derivative(2, dh[2])
+        quantize_w2(3)
+        dh[3] = first_product(3)
+        dx[2] = second_product(2, da[2])
+        scatter(1, dx[1])
+        da[3] = derivative(3, dh[3])
+        dx[3] = second_product(3, da[3])
+        scatter(2, dx[2])
+        scatter(3, dx[3])
+        nc.sync.dma_start(out, result[:])

@@ -8,8 +8,7 @@ PACK = 4
 PASSES = N // (P * PACK)
 PAIR = 2 * C
 GQ = 3
-WQ = 2
-WR = 3
+WQ = 3
 
 F32 = mybir.dt.float32
 BF16 = mybir.dt.bfloat16
@@ -30,27 +29,36 @@ def tile_moe_bdx_glu_relu_kernel(tc, dyT, a1, a3, w2, w1, w3, gate, offs, out):
 
     dy_rows = dyT.rearrange("(c p t) w -> c t p w", c=PASSES, t=PACK)
     w2_rows = w2.rearrange("e (c p j) i -> e c p j i", c=PASSES, j=PACK)
-    a1_rows = a1.rearrange("(p t) (e s) -> e p t s", t=PACK, e=E)
-    a3_rows = a3.rearrange("(p t) (e s) -> e p t s", t=PACK, e=E)
+    a1_rows = a1.rearrange("(p t) s -> p t s", t=PACK)
+    a3_rows = a3.rearrange("(p t) s -> p t s", t=PACK)
 
     with ExitStack() as ctx:
         held = ctx.enter_context(tc.tile_pool(name="held", bufs=1))
-        raw = ctx.enter_context(tc.tile_pool(name="raw", bufs=8))
-        wraw = ctx.enter_context(tc.tile_pool(name="wraw", bufs=WR))
-        gpool = ctx.enter_context(tc.tile_pool(name="gpool", bufs=2))
         work = ctx.enter_context(tc.tile_pool(name="work", bufs=2))
         codes = ctx.enter_context(tc.tile_pool(name="codes", bufs=6))
         psum = ctx.enter_context(tc.psum_pool(name="psum", bufs=1))
 
-        def load(src, shape):
-            big = raw.tile(shape, F32, tag="big", align_bytes=64, name="big")
-            nc.sync.dma_start(big[:], src)
-            return big
+        def turn(tag, shape, dtype, name):
+            return held.tile(shape, dtype, tag=tag, align_bytes=64, name=name)
 
-        def load_w(src, shape):
-            mat = wraw.tile(shape, F32, tag="mat", align_bytes=64, name="mat")
-            nc.sync.dma_start(mat[:], src)
-            return mat
+        def load(tag, src, shape):
+            raw = turn(tag, shape, F32, "raw_" + tag)
+            nc.sync.dma_start(raw[:], src)
+            return raw
+
+        def load_dy(tag, c, t):
+            dy[c, t] = load(tag, dy_rows[c, t], [P, T])
+
+        def load_w2(tag, e, c):
+            w2_raw[e, c] = load(tag, w2_rows[e, c], [P, PACK, H])
+
+        def load_w13(tag, n):
+            w13_raw[n] = load(tag, (w1, w3)[n].rearrange("e (p j) k -> p e j k", j=PACK), [P, E, PACK, K])
+
+        def load_saved(tag, saved, rows, first, count):
+            raw = load(tag, rows[:, :, first * C : (first + count) * C], [P, PACK, count * C])
+            for e in range(count):
+                saved[first + e] = raw[:, :, e * C : (e + 1) * C]
 
         def quantize(src, width, tag, dtype, bufs):
             words = codes.tile([P, width], U32, tag=tag + "_w", bufs=bufs, align_bytes=64, name=tag + "_w")
@@ -61,28 +69,25 @@ def tile_moe_bdx_glu_relu_kernel(tc, dyT, a1, a3, w2, w1, w3, gate, offs, out):
         offsets = held.tile([P, E * C // 16], U16, name="offsets")
         nc.sync.dma_start(offsets[:], offs)
         dy = {}
-        gates = {}
         w2_raw = {}
         w13_raw = {}
         a1_raw = {}
         a3_raw = {}
-        for pair in range(2):
-            gates[pair] = held.tile([P, PAIR], F32, name="gate%d" % pair)
-        dy[0, 0] = load(dy_rows[0, 0], [P, T])
-        nc.sync.dma_start(gates[0][:, 0:512], gate[0:P, 0:512])
-        nc.sync.dma_start(gates[0][:, 512:1024], gate[0:P, 512:1024])
-        dy[0, 1] = load(dy_rows[0, 1], [P, T])
-        dy[0, 2] = load(dy_rows[0, 2], [P, T])
-        dy[0, 3] = load(dy_rows[0, 3], [P, T])
-        dy[1, 0] = load(dy_rows[1, 0], [P, T])
-        dy[1, 1] = load(dy_rows[1, 1], [P, T])
-        dy[1, 2] = load(dy_rows[1, 2], [P, T])
-        w2_raw[0, 0] = load_w(w2_rows[0, 0], [P, PACK, H])
-        dy[1, 3] = load(dy_rows[1, 3], [P, T])
-        nc.sync.dma_start(gates[1][:, 0:1024], gate[0:P, 1024:2048])
-        w2_raw[0, 1] = load_w(w2_rows[0, 1], [P, PACK, H])
-        w13_raw[0] = load_w(w1.rearrange("e (p j) k -> p e j k", j=PACK), [P, E, PACK, K])
-        result = held.tile([P, T], F32, name="result")
+        gates = turn("even", [P, T], F32, "gates")
+        load_dy("s0", 0, 0)
+        nc.sync.dma_start(gates[:, 0:C], gate[0:P, 0:C])
+        nc.sync.dma_start(gates[:, C:PAIR], gate[0:P, C:PAIR])
+        nc.sync.dma_start(gates[:, PAIR:T], gate[0:P, PAIR:T])
+        load_dy("s1", 0, 1)
+        load_w2("s2", 0, 0)
+        load_dy("s3", 0, 2)
+        load_w2("s4", 0, 1)
+        load_dy("s5", 0, 3)
+        load_dy("s6", 1, 0)
+        load_w2("s9", 1, 0)
+        load_dy("s7", 1, 1)
+        load_dy("s8", 1, 2)
+        load_dy("odd", 1, 3)
 
         g_b = {}
         g_q = {}
@@ -94,12 +99,12 @@ def tile_moe_bdx_glu_relu_kernel(tc, dyT, a1, a3, w2, w1, w3, gate, offs, out):
                 nc.vector.tensor_tensor(
                     planes[:, t, lo:hi],
                     dy[c, t][:].indirect(offsets[:, (pair * PAIR + lo) // 16 : (pair * PAIR + hi) // 16]),
-                    gates[pair][:, lo:hi],
+                    gates[:, pair * PAIR + lo : pair * PAIR + hi],
                     MULT,
                 )
 
-        def prepare_g(pair, c, planes):
-            gb = work.tile([P, PACK * PAIR], BF16, tag="gb", bufs=2, align_bytes=64, name="gb")
+        def prepare_g(tag, pair, c, planes):
+            gb = turn(tag, [P, PACK * PAIR], BF16, "gb")
             nc.scalar.copy(
                 out=gb[:].rearrange("p (s i t) -> p s t i", i=4, t=PACK),
                 in_=planes[:].rearrange("p t (s i) -> p s t i", i=4),
@@ -110,7 +115,7 @@ def tile_moe_bdx_glu_relu_kernel(tc, dyT, a1, a3, w2, w1, w3, gate, offs, out):
             g_q[pair, c] = quantize(g_b[pair, c], PAIR, "g", E5M2X4, GQ)
 
         def round_w2(e, c):
-            if c == 0:
+            if e not in w2_b:
                 w2_b[e] = work.tile([P, PASSES * PACK * H], BF16, tag="wb", bufs=2, align_bytes=64, name="wb")
             nc.scalar.copy(
                 out=w2_b[e][:, c * PACK * H : (c + 1) * PACK * H].rearrange("p (t m j) -> p m j t", t=PACK, j=PACK),
@@ -133,10 +138,12 @@ def tile_moe_bdx_glu_relu_kernel(tc, dyT, a1, a3, w2, w1, w3, gate, offs, out):
         def quantize_w13():
             return quantize(w13_b[0], 2 * E * K, "w13", E4M3X4, 1)
 
+        banks = {}
+
         def first_product(e):
-            dh = work.tile([P, PACK, C], F32, tag="dh", bufs=2, align_bytes=64, name="dh")
             for t in range(PACK):
-                bank = psum.tile([P, C], F32, tag="bank", bufs=6, name="bank")
+                bank = psum.tile([P, C], F32, tag="bank%d" % (e % 2 * PACK + t), name="bank")
+                banks[e, t] = bank
                 for c in range(PASSES):
                     nc.tensor.matmul_mx(
                         out=bank[:],
@@ -147,117 +154,168 @@ def tile_moe_bdx_glu_relu_kernel(tc, dyT, a1, a3, w2, w1, w3, gate, offs, out):
                         start=(c == 0),
                         stop=(c == PASSES - 1),
                     )
-                nc.vector.scalar_tensor_tensor(dh[:, t, :], a1_raw[e][:, t, :], 0.0, bank[:], op0=IS_GT, op1=MULT)
-            return dh
 
-        def walk_in(x):
-            return x[:].rearrange("p t (s i) -> p s t i", i=2)
+        def masked(e, dh):
+            for t in range(PACK):
+                nc.vector.scalar_tensor_tensor(dh[:, t, :], a1_raw[e][:, t, :], 0.0, banks[e, t][:], op0=IS_GT, op1=MULT)
 
-        def derivative(e, dh):
-            d1 = work.tile([P, PACK * C], BF16, tag="da", bufs=2, align_bytes=64, name="d1")
-            d3 = work.tile([P, PACK * C], BF16, tag="da", bufs=2, align_bytes=64, name="d3")
+        def woven_product(da, a, dh):
             nc.vector.tensor_tensor(
-                d1[:].rearrange("p (s i t) -> p s t i", i=2, t=PACK), walk_in(a3_raw[e]), walk_in(dh), MULT
+                da[:].rearrange("p (s i t) -> p s t i", i=2, t=PACK),
+                a.rearrange("p t (s i) -> p s t i", i=2),
+                dh.rearrange("p t (s i) -> p s t i", i=2),
+                MULT,
             )
-            nc.vector.tensor_tensor(
-                d3[:].rearrange("p (s i t) -> p s t i", i=2, t=PACK), walk_in(a1_raw[e]), walk_in(dh), MULT
-            )
-            return quantize(d1, C, "da", E5M2X4, 4), quantize(d3, C, "da", E5M2X4, 4)
 
-        def second_product(e, da):
-            bank = psum.tile([P, C], F32, tag="dx", bufs=2, name="dxbank")
-            for n, dq in enumerate(da):
+        def rows_on_gpsimd(e, count):
+            rows = turn("rows", [P, PACK, C], BF16, "rows")
+            for t in range(count):
+                nc.gpsimd.tensor_tensor(rows[:, t, :], a3_raw[e][:, t, :], dh[e][:, t, :], MULT)
+            return rows
+
+        def weave(da, rows):
+            nc.scalar.copy(
+                out=da[:].rearrange("p (s i t) -> p s t i", i=4, t=PACK),
+                in_=rows[:].rearrange("p t (s i) -> p s t i", i=4),
+            )
+
+        def new_da():
+            return work.tile([P, PACK * C], BF16, tag="da", bufs=3, align_bytes=64, name="da")
+
+        def quantize_da(da):
+            return quantize(da, C, "da", E5M2X4, 4)
+
+        def second_product(e, q1, q3, where, dx):
+            bank = psum.tile([P, C], F32, tag="bank%d" % where, name="dxbank")
+            for n, dq in ((1, q3), (0, q1)):
                 nc.tensor.matmul_mx(
                     out=bank[:],
                     lhsT=w13_q[0][:, (n * E + e) * K : (n * E + e + 1) * K].bitcast(E4M3X4),
                     lhsT_scale=w13_q[1][:, (n * E + e) * K : (n * E + e + 1) * K],
                     rhs=dq[0][:].bitcast(E5M2X4),
                     rhs_scale=dq[1][:],
-                    start=(n == 0),
-                    stop=(n == 1),
+                    start=(n == 1),
+                    stop=(n == 0),
                 )
-            dx = work.tile([P, C], F32, tag="dx", bufs=2, align_bytes=64, name="dx")
-            nc.scalar.copy(out=dx[:], in_=bank[:])
-            return dx
+            nc.scalar.copy(out=dx, in_=bank[:])
 
         def scatter(e, dx):
-            nc.vector.tensor_copy(result[:].indirect(offsets[:, e * C // 16 : (e + 1) * C // 16]), dx[:])
+            nc.vector.tensor_copy(result[:].indirect(offsets[:, e * C // 16 : (e + 1) * C // 16]), dx)
+
+        def new_planes(tag):
+            return turn(tag, [P, PACK, PAIR], F32, "planes")
+
+        def as_rows(x):
+            return x[:, 0 : PACK * C].rearrange("p (t s) -> p t s", t=PACK)
 
         dh = {}
-        da = {}
-        dx = {}
-        planes = gpool.tile([P, PACK, PAIR], F32, tag="planes", align_bytes=64, name="planes")
-        gather(0, 0, 0, planes, (0, C, PAIR))
-        gather(0, 0, 1, planes)
-        gather(0, 0, 2, planes)
-        gather(0, 0, 3, planes)
-        prepare_g(0, 0, planes)
+        planes = {(0, 0): new_planes("p0"), (1, 0): new_planes("p1")}
+        gather(0, 0, 0, planes[0, 0], (0, C, PAIR))
+        gather(1, 0, 0, planes[1, 0])
         round_w2(0, 0)
-        w13_raw[1] = load_w(w3.rearrange("e (p j) k -> p e j k", j=PACK), [P, E, PACK, K])
-        planes = gpool.tile([P, PACK, PAIR], F32, tag="planes", align_bytes=64, name="planes")
-        gather(0, 1, 0, planes)
-        gather(0, 1, 1, planes)
-        gather(0, 1, 2, planes)
-        gather(0, 1, 3, planes)
-        prepare_g(0, 1, planes)
+        gather(0, 0, 1, planes[0, 0])
+        gather(1, 0, 1, planes[1, 0])
         round_w2(0, 1)
-        w2_raw[1, 0] = load_w(w2_rows[1, 0], [P, PACK, H])
-        round_w13(0)
-        w2_raw[1, 1] = load_w(w2_rows[1, 1], [P, PACK, H])
-        round_w13(1)
-        planes = gpool.tile([P, PACK, PAIR], F32, tag="planes", align_bytes=64, name="planes")
-        gather(1, 0, 0, planes)
-        a1_raw[0] = load(a1_rows[0], [P, PACK, C])
-        gather(1, 0, 1, planes)
-        a3_raw[0] = load(a3_rows[0], [P, PACK, C])
-        gather(1, 0, 2, planes)
-        a1_raw[1] = load(a1_rows[1], [P, PACK, C])
-        gather(1, 0, 3, planes)
-        a3_raw[1] = load(a3_rows[1], [P, PACK, C])
+        load_w2("s0", 1, 1)
+        load_w2("s1", 2, 0)
+        gather(0, 0, 2, planes[0, 0])
+        gather(1, 0, 2, planes[1, 0])
+        load_w2("s3", 2, 1)
+        gather(0, 0, 3, planes[0, 0])
+        gather(1, 0, 3, planes[1, 0])
+        prepare_g("s2", 0, 0, planes[0, 0])
+        load_saved("p0", a3_raw, a3_rows, 0, 2)
         round_w2(1, 0)
-        w2_raw[2, 0] = load_w(w2_rows[2, 0], [P, PACK, H])
+        planes[0, 1] = new_planes("p2")
+        for t in range(PACK):
+            gather(0, 1, t, planes[0, 1])
+        prepare_g("s5", 1, 0, planes[1, 0])
+        prepare_g("s4", 0, 1, planes[0, 1])
+        load_saved("p2", a1_raw, a1_rows, 0, 2)
         round_w2(1, 1)
-        w2_raw[2, 1] = load_w(w2_rows[2, 1], [P, PACK, H])
-        quantize_g(0, 0)
-        quantize_g(0, 1)
-        quantize_w2(0)
-        dh[0] = first_product(0)
-        prepare_g(1, 0, planes)
-        planes = gpool.tile([P, PACK, PAIR], F32, tag="planes", align_bytes=64, name="planes")
-        gather(1, 1, 0, planes)
-        gather(1, 1, 1, planes)
-        gather(1, 1, 2, planes)
-        gather(1, 1, 3, planes)
-        prepare_g(1, 1, planes)
-        w2_raw[3, 0] = load_w(w2_rows[3, 0], [P, PACK, H])
-        da[0] = derivative(0, dh[0])
-        w13_q = quantize_w13()
-        quantize_w2(1)
-        dh[1] = first_product(1)
-        dx[0] = second_product(0, da[0])
-        da[1] = derivative(1, dh[1])
         round_w2(2, 0)
-        w2_raw[3, 1] = load_w(w2_rows[3, 1], [P, PACK, H])
+        load_w13("s1", 0)
         round_w2(2, 1)
-        a1_raw[2] = load(a1_rows[2], [P, PACK, C])
-        a3_raw[2] = load(a3_rows[2], [P, PACK, C])
-        dx[1] = second_product(1, da[1])
-        scatter(0, dx[0])
+        quantize_w2(0)
+        quantize_g(0, 0)
         quantize_g(1, 0)
-        quantize_g(1, 1)
-        round_w2(3, 0)
-        round_w2(3, 1)
+        quantize_g(0, 1)
+        load_w13("s4", 1)
+        first_product(0)
+        quantize_w2(1)
+        first_product(1)
+        planes[1, 1] = new_planes("p1")
+        for t in range(PACK):
+            gather(1, 1, t, planes[1, 1])
+        prepare_g("s3", 1, 1, planes[1, 1])
         quantize_w2(2)
-        dh[2] = first_product(2)
-        a1_raw[3] = load(a1_rows[3], [P, PACK, C])
-        a3_raw[3] = load(a3_rows[3], [P, PACK, C])
-        da[2] = derivative(2, dh[2])
+        result = turn("p1", [P, T], F32, "result")
+
+        dh[0] = as_rows(turn("even", [P, PACK * C], F32, "dh0"))
+        dh[1] = as_rows(turn("odd", [P, PACK * C], F32, "dh1"))
+        masked(0, dh[0])
+        rows = rows_on_gpsimd(0, PACK - 1)
+        masked(1, dh[1])
+        nc.vector.tensor_tensor(rows[:, PACK - 1, :], a3_raw[0][:, PACK - 1, :], dh[0][:, PACK - 1, :], MULT)
+        woven = new_da()
+        weave(woven, rows)
+        d3 = new_da()
+        woven_product(d3, a1_raw[0], dh[0])
+        quantize_g(1, 1)
+        load_w2("s3", 3, 1)
+        first_product(2)
+        q3 = quantize_da(d3)
+        round_w13(0)
+        load_w2("s1", 3, 0)
+        round_w13(1)
+        load_saved("s4", a1_raw, a1_rows, 2, 1)
+        d1 = new_da()
+        woven_product(d1, a3_raw[1], dh[1])
+        load_saved("p0", a3_raw, a3_rows, 2, 1)
+        first = (quantize_da(woven), q3)
+        w13_q = quantize_w13()
+        round_w2(3, 1)
+        load_saved("s3", a3_raw, a3_rows, 3, 1)
+        round_w2(3, 0)
+        load_saved("s1", a1_raw, a1_rows, 3, 1)
+        d3 = turn("even", [P, PACK * C], BF16, "d3")
+        woven_product(d3, a1_raw[1], dh[1])
+        q1 = quantize_da(d1)
+        q3 = quantize_da(d3)
+        second = (q1, q3)
         quantize_w2(3)
-        dh[3] = first_product(3)
-        dx[2] = second_product(2, da[2])
-        scatter(1, dx[1])
-        da[3] = derivative(3, dh[3])
-        dx[3] = second_product(3, da[3])
-        scatter(2, dx[2])
-        scatter(3, dx[3])
+
+        both = turn("even", [P, PACK * C + C], F32, "both")
+        dh[2] = as_rows(both)
+        second_product(0, first[0], first[1], 7, both[:, PACK * C :])
+        first_product(3)
+        masked(2, dh[2])
+        rows = rows_on_gpsimd(2, PACK)
+        scatter(0, both[:, PACK * C :])
+        d1 = turn("odd", [P, PACK * C], BF16, "d1")
+        weave(d1, rows)
+        d3 = new_da()
+        woven_product(d3, a1_raw[2], dh[2])
+        q3 = quantize_da(d3)
+        q1 = quantize_da(d1)
+        third = (q1, q3)
+
+        both = turn("odd", [P, PACK * C + C], F32, "both")
+        dh[3] = as_rows(both)
+        second_product(1, second[0], second[1], 0, both[:, PACK * C :])
+        masked(3, dh[3])
+        rows = rows_on_gpsimd(3, PACK)
+        scatter(1, both[:, PACK * C :])
+        d1 = new_da()
+        weave(d1, rows)
+        d3 = new_da()
+        woven_product(d3, a1_raw[3], dh[3])
+        dx = turn("rows", [P, C], F32, "dx")
+        second_product(2, third[0], third[1], 1, dx[:])
+        q3 = quantize_da(d3)
+        q1 = quantize_da(d1)
+        last = turn("last", [P, C], F32, "last")
+        second_product(3, q1, q3, 2, last[:])
+        scatter(2, dx[:])
+        scatter(3, last[:])
         nc.sync.dma_start(out, result[:])

@@ -19,6 +19,8 @@ E4M3X4 = mybir.dt.float8_e4m3fn_x4
 E5M2X4 = mybir.dt.float8_e5m2_x4
 MULT = mybir.AluOpType.mult
 IS_GT = mybir.AluOpType.is_gt
+RELU = mybir.ActivationFunctionType.Relu
+SIGN = mybir.ActivationFunctionType.Sign
 
 FLOPS = 2 * N * H * E * C + 2 * 2 * H * K * E * C
 BYTES = 4 * (N * T + 2 * H * E * C + E * N * H + 2 * E * H * K + E * C + K * T) + 2 * P * (E * C // 16)
@@ -167,17 +169,28 @@ def tile_moe_bdx_glu_relu_kernel(tc, dyT, a1, a3, w2, w1, w3, gate, offs, out):
                 MULT,
             )
 
-        def rows_on_gpsimd(e, count):
-            rows = turn("rows", [P, PACK, C], BF16, "rows")
-            for t in range(count):
-                nc.gpsimd.tensor_tensor(rows[:, t, :], a3_raw[e][:, t, :], dh[e][:, t, :], MULT)
-            return rows
+        def plain(e, dh):
+            for t in range(PACK):
+                nc.scalar.copy(out=dh[:, t, :], in_=banks[e, t][:])
 
-        def weave(da, rows):
-            nc.scalar.copy(
-                out=da[:].rearrange("p (s i t) -> p s t i", i=4, t=PACK),
-                in_=rows[:].rearrange("p t (s i) -> p s t i", i=4),
+        def relu_and_mask(e, tag):
+            nc.scalar.activation(a1_raw[e], a1_raw[e], RELU)
+            mask = turn(tag, [P, PACK * C], BF16, "mask")
+            nc.scalar.activation(
+                mask[:].rearrange("p (s i t) -> p s t i", i=4, t=PACK),
+                a1_raw[e].rearrange("p t (s i) -> p s t i", i=4),
+                SIGN,
             )
+            return mask
+
+        def derivative_masked_late(e, mask):
+            d1 = new_da()
+            woven_product(d1, a3_raw[e], dh[e])
+            d3 = new_da()
+            woven_product(d3, a1_raw[e], dh[e])
+            nc.vector.tensor_tensor(d1[:], d1[:], mask[:], MULT)
+            q3 = quantize_da(d3)
+            return quantize_da(d1), q3
 
         def new_da():
             return work.tile([P, PACK * C], BF16, tag="da", bufs=3, align_bytes=64, name="da")
@@ -224,23 +237,27 @@ def tile_moe_bdx_glu_relu_kernel(tc, dyT, a1, a3, w2, w1, w3, gate, offs, out):
         gather(0, 0, 3, planes[0, 0])
         gather(1, 0, 3, planes[1, 0])
         prepare_g("s2", 0, 0, planes[0, 0])
-        load_saved("p0", a3_raw, a3_rows, 0, 2)
+        load_saved("p0", a1_raw, a1_rows, 0, 2)
         round_w2(1, 0)
+        load_w13("s9", 0)
         planes[0, 1] = new_planes("p2")
         for t in range(PACK):
             gather(0, 1, t, planes[0, 1])
         prepare_g("s5", 1, 0, planes[1, 0])
         prepare_g("s4", 0, 1, planes[0, 1])
-        load_saved("p2", a1_raw, a1_rows, 0, 2)
+        load_saved("p2", a3_raw, a3_rows, 0, 2)
         round_w2(1, 1)
         round_w2(2, 0)
-        load_w13("s1", 0)
         round_w2(2, 1)
         quantize_w2(0)
         quantize_g(0, 0)
+        load_w13("s2", 1)
         quantize_g(1, 0)
+        load_w2("s5", 3, 0)
+        load_w2("s0", 3, 1)
+        load_saved("s1", a1_raw, a1_rows, 2, 1)
         quantize_g(0, 1)
-        load_w13("s4", 1)
+        load_saved("s4", a3_raw, a3_rows, 2, 1)
         first_product(0)
         quantize_w2(1)
         first_product(1)
@@ -254,67 +271,47 @@ def tile_moe_bdx_glu_relu_kernel(tc, dyT, a1, a3, w2, w1, w3, gate, offs, out):
         dh[0] = as_rows(turn("even", [P, PACK * C], F32, "dh0"))
         dh[1] = as_rows(turn("odd", [P, PACK * C], F32, "dh1"))
         masked(0, dh[0])
-        rows = rows_on_gpsimd(0, PACK - 1)
         masked(1, dh[1])
-        nc.vector.tensor_tensor(rows[:, PACK - 1, :], a3_raw[0][:, PACK - 1, :], dh[0][:, PACK - 1, :], MULT)
-        woven = new_da()
-        weave(woven, rows)
         d3 = new_da()
         woven_product(d3, a1_raw[0], dh[0])
         quantize_g(1, 1)
-        load_w2("s3", 3, 1)
+        load_saved("s3", a1_raw, a1_rows, 3, 1)
         first_product(2)
-        q3 = quantize_da(d3)
         round_w13(0)
-        load_w2("s1", 3, 0)
         round_w13(1)
-        load_saved("s4", a1_raw, a1_rows, 2, 1)
+        d1 = new_da()
+        woven_product(d1, a3_raw[0], dh[0])
+        q3 = quantize_da(d3)
+        first = (quantize_da(d1), q3)
         d1 = new_da()
         woven_product(d1, a3_raw[1], dh[1])
-        load_saved("p0", a3_raw, a3_rows, 2, 1)
-        first = (quantize_da(woven), q3)
+        load_saved("p2", a3_raw, a3_rows, 3, 1)
         w13_q = quantize_w13()
-        round_w2(3, 1)
-        load_saved("s3", a3_raw, a3_rows, 3, 1)
         round_w2(3, 0)
-        load_saved("s1", a1_raw, a1_rows, 3, 1)
-        d3 = turn("even", [P, PACK * C], BF16, "d3")
+        round_w2(3, 1)
+        d3 = new_da()
         woven_product(d3, a1_raw[1], dh[1])
         q1 = quantize_da(d1)
-        q3 = quantize_da(d3)
-        second = (q1, q3)
+        second = (q1, quantize_da(d3))
+        dx = turn("dx0", [P, C], F32, "dx0")
+        second_product(0, first[0], first[1], 7, dx[:])
         quantize_w2(3)
-
-        both = turn("even", [P, PACK * C + C], F32, "both")
-        dh[2] = as_rows(both)
-        second_product(0, first[0], first[1], 7, both[:, PACK * C :])
         first_product(3)
-        masked(2, dh[2])
-        rows = rows_on_gpsimd(2, PACK)
-        scatter(0, both[:, PACK * C :])
-        d1 = turn("odd", [P, PACK * C], BF16, "d1")
-        weave(d1, rows)
-        d3 = new_da()
-        woven_product(d3, a1_raw[2], dh[2])
-        q3 = quantize_da(d3)
-        q1 = quantize_da(d1)
-        third = (q1, q3)
-
-        both = turn("odd", [P, PACK * C + C], F32, "both")
-        dh[3] = as_rows(both)
-        second_product(1, second[0], second[1], 0, both[:, PACK * C :])
-        masked(3, dh[3])
-        rows = rows_on_gpsimd(3, PACK)
-        scatter(1, both[:, PACK * C :])
-        d1 = new_da()
-        weave(d1, rows)
-        d3 = new_da()
-        woven_product(d3, a1_raw[3], dh[3])
-        dx = turn("rows", [P, C], F32, "dx")
+        mask = relu_and_mask(2, "s2")
+        dh[2] = as_rows(turn("s8", [P, PACK * C], F32, "dh2"))
+        plain(2, dh[2])
+        scatter(0, dx[:])
+        third = derivative_masked_late(2, mask)
+        mask = relu_and_mask(3, "s5")
+        dh[3] = as_rows(turn("s9", [P, PACK * C], F32, "dh3"))
+        plain(3, dh[3])
+        dx = turn("dx1", [P, C], F32, "dx1")
+        second_product(1, second[0], second[1], 0, dx[:])
+        scatter(1, dx[:])
+        q1, q3 = derivative_masked_late(3, mask)
+        dx = turn("s3", [P, C], F32, "dx2")
         second_product(2, third[0], third[1], 1, dx[:])
-        q3 = quantize_da(d3)
-        q1 = quantize_da(d1)
-        last = turn("last", [P, C], F32, "last")
+        last = turn("dx0", [P, C], F32, "dx3")
         second_product(3, q1, q3, 2, last[:])
         scatter(2, dx[:])
         scatter(3, last[:])

@@ -8,7 +8,8 @@ PACK = 4
 PASSES = N // (P * PACK)
 PAIR = 2 * C
 GQ = 3
-WQ = 3
+WQ = 2
+GPSIMD_ROWS = 3
 
 F32 = mybir.dt.float32
 BF16 = mybir.dt.bfloat16
@@ -62,8 +63,11 @@ def tile_moe_bdx_glu_relu_kernel(tc, dyT, a1, a3, w2, w1, w3, gate, offs, out):
             for e in range(count):
                 saved[first + e] = raw[:, :, e * C : (e + 1) * C]
 
-        def quantize(src, width, tag, dtype, bufs):
-            words = codes.tile([P, width], U32, tag=tag + "_w", bufs=bufs, align_bytes=64, name=tag + "_w")
+        def quantize(src, width, tag, dtype, bufs, slot=None):
+            if slot is None:
+                words = codes.tile([P, width], U32, tag=tag + "_w", bufs=bufs, align_bytes=64, name=tag + "_w")
+            else:
+                words = turn(slot, [P, width], U32, tag + "_w")
             scales = codes.tile([P, width], U8, tag=tag + "_s", bufs=bufs, align_bytes=64, name=tag + "_s")
             nc.vector.quantize_mx(out=words[:].bitcast(dtype), scales=scales[:], in_=src[:])
             return words, scales
@@ -85,11 +89,9 @@ def tile_moe_bdx_glu_relu_kernel(tc, dyT, a1, a3, w2, w1, w3, gate, offs, out):
         load_dy("s3", 0, 2)
         load_w2("s4", 0, 1)
         load_dy("s5", 0, 3)
-        load_dy("s6", 1, 0)
         load_w2("s9", 1, 0)
+        load_dy("s6", 1, 0)
         load_dy("s7", 1, 1)
-        load_dy("s8", 1, 2)
-        load_dy("odd", 1, 3)
 
         g_b = {}
         g_q = {}
@@ -118,23 +120,23 @@ def tile_moe_bdx_glu_relu_kernel(tc, dyT, a1, a3, w2, w1, w3, gate, offs, out):
 
         def round_w2(e, c):
             if e not in w2_b:
-                w2_b[e] = work.tile([P, PASSES * PACK * H], BF16, tag="wb", bufs=2, align_bytes=64, name="wb")
+                w2_b[e] = work.tile([P, PASSES * PACK * H], BF16, tag="wb", bufs=3, align_bytes=64, name="wb")
             nc.scalar.copy(
                 out=w2_b[e][:, c * PACK * H : (c + 1) * PACK * H].rearrange("p (t m j) -> p m j t", t=PACK, j=PACK),
                 in_=w2_raw[e, c][:].rearrange("p j (m t) -> p m j t", t=PACK),
             )
 
-        def quantize_w2(e):
-            w2_q[e] = quantize(w2_b[e], PASSES * H, "w2", E4M3X4, WQ)
+        def quantize_w2(e, slot=None):
+            w2_q[e] = quantize(w2_b[e], PASSES * H, "w2", E4M3X4, WQ, slot)
 
         w13_b = {}
 
         def round_w13(n):
             if n == 0:
-                w13_b[0] = work.tile([P, PASSES * PACK * H], BF16, tag="wb", bufs=2, align_bytes=64, name="wb")
+                w13_b[0] = work.tile([P, PASSES * PACK * H], BF16, tag="wb", bufs=3, align_bytes=64, name="wb")
             nc.scalar.copy(
-                out=w13_b[0][:, n * PACK * H : (n + 1) * PACK * H].rearrange("p (e k j) -> p e k j", e=E, j=PACK),
-                in_=w13_raw[n][:].rearrange("p e j k -> p e k j"),
+                out=w13_b[0][:, n * PACK * H : (n + 1) * PACK * H].rearrange("p (e k i j) -> p e k j i", e=E, i=4, j=PACK),
+                in_=w13_raw[n][:].rearrange("p e j (k i) -> p e k j i", i=4),
             )
 
         def quantize_w13():
@@ -173,14 +175,19 @@ def tile_moe_bdx_glu_relu_kernel(tc, dyT, a1, a3, w2, w1, w3, gate, offs, out):
             for t in range(PACK):
                 nc.scalar.copy(out=dh[:, t, :], in_=banks[e, t][:])
 
-        def relu_and_mask(e, tag):
-            nc.scalar.activation(a1_raw[e], a1_raw[e], RELU)
+        def relu(e):
+            for lo in (0, C // 2):
+                half = a1_raw[e][:, :, lo : lo + C // 2]
+                nc.scalar.activation(half, half, RELU)
+
+        def make_mask(e, tag):
             mask = turn(tag, [P, PACK * C], BF16, "mask")
-            nc.scalar.activation(
-                mask[:].rearrange("p (s i t) -> p s t i", i=4, t=PACK),
-                a1_raw[e].rearrange("p t (s i) -> p s t i", i=4),
-                SIGN,
-            )
+            for lo in (0, C // 2):
+                nc.scalar.activation(
+                    mask[:, PACK * lo : PACK * (lo + C // 2)].rearrange("p (s i t) -> p s t i", i=4, t=PACK),
+                    a1_raw[e][:, :, lo : lo + C // 2].rearrange("p t (s i) -> p s t i", i=4),
+                    SIGN,
+                )
             return mask
 
         def derivative_masked_late(e, mask):
@@ -225,69 +232,79 @@ def tile_moe_bdx_glu_relu_kernel(tc, dyT, a1, a3, w2, w1, w3, gate, offs, out):
         planes = {(0, 0): new_planes("p0"), (1, 0): new_planes("p1")}
         gather(0, 0, 0, planes[0, 0], (0, C, PAIR))
         gather(1, 0, 0, planes[1, 0])
+        load_w2("s0", 1, 1)
+        load_dy("s8", 1, 2)
+        load_dy("odd", 1, 3)
         round_w2(0, 0)
         gather(0, 0, 1, planes[0, 0])
         gather(1, 0, 1, planes[1, 0])
         round_w2(0, 1)
-        load_w2("s0", 1, 1)
         load_w2("s1", 2, 0)
         gather(0, 0, 2, planes[0, 0])
         gather(1, 0, 2, planes[1, 0])
         load_w2("s3", 2, 1)
+        load_saved("s2", a3_raw, a3_rows, 0, 1)
         gather(0, 0, 3, planes[0, 0])
         gather(1, 0, 3, planes[1, 0])
-        prepare_g("s2", 0, 0, planes[0, 0])
-        load_saved("p0", a1_raw, a1_rows, 0, 2)
         round_w2(1, 0)
-        load_w13("s9", 0)
+        prepare_g("s9", 0, 0, planes[0, 0])
+        load_saved("p0", a1_raw, a1_rows, 0, 2)
         planes[0, 1] = new_planes("p2")
         for t in range(PACK):
             gather(0, 1, t, planes[0, 1])
-        prepare_g("s5", 1, 0, planes[1, 0])
-        prepare_g("s4", 0, 1, planes[0, 1])
-        load_saved("p2", a3_raw, a3_rows, 0, 2)
         round_w2(1, 1)
+        prepare_g("s0", 1, 0, planes[1, 0])
         round_w2(2, 0)
+        prepare_g("s1", 0, 1, planes[0, 1])
+        load_saved("p2", a3_raw, a3_rows, 1, 1)
         round_w2(2, 1)
         quantize_w2(0)
         quantize_g(0, 0)
-        load_w13("s2", 1)
+        load_w13("s9", 0)
         quantize_g(1, 0)
-        load_w2("s5", 3, 0)
-        load_w2("s0", 3, 1)
-        load_saved("s1", a1_raw, a1_rows, 2, 1)
+        load_w13("s0", 1)
+        load_w2("s3", 3, 0)
+        round_w13(0)
         quantize_g(0, 1)
-        load_saved("s4", a3_raw, a3_rows, 2, 1)
         first_product(0)
-        quantize_w2(1)
+        quantize_w2(1, "s1")
         first_product(1)
         planes[1, 1] = new_planes("p1")
         for t in range(PACK):
             gather(1, 1, t, planes[1, 1])
-        prepare_g("s3", 1, 1, planes[1, 1])
-        quantize_w2(2)
-        result = turn("p1", [P, T], F32, "result")
+        prepare_g("s9", 1, 1, planes[1, 1])
+        round_w13(1)
+        load_saved("s7", a1_raw, a1_rows, 2, 1)
+        load_w2("s8", 3, 1)
+        result = turn("s4", [P, T], F32, "result")
 
         dh[0] = as_rows(turn("even", [P, PACK * C], F32, "dh0"))
         dh[1] = as_rows(turn("odd", [P, PACK * C], F32, "dh1"))
         masked(0, dh[0])
+        rows = turn("rows", [P, PACK, C], BF16, "rows")
+        for t in range(GPSIMD_ROWS):
+            nc.gpsimd.tensor_tensor(rows[:, t, :], a3_raw[0][:, t, :], dh[0][:, t, :], MULT)
         masked(1, dh[1])
+        nc.vector.tensor_tensor(rows[:, GPSIMD_ROWS:, :], a3_raw[0][:, GPSIMD_ROWS:, :], dh[0][:, GPSIMD_ROWS:, :], MULT)
+        woven = turn("p1", [P, PACK * C], BF16, "woven")
+        nc.scalar.copy(
+            out=woven[:].rearrange("p (s i t) -> p s t i", i=4, t=PACK),
+            in_=rows[:].rearrange("p t (s i) -> p s t i", i=4),
+        )
         d3 = new_da()
         woven_product(d3, a1_raw[0], dh[0])
+        quantize_w2(2, "s2")
         quantize_g(1, 1)
-        load_saved("s3", a1_raw, a1_rows, 3, 1)
+        load_saved("s9", a3_raw, a3_rows, 2, 1)
         first_product(2)
-        round_w13(0)
-        round_w13(1)
-        d1 = new_da()
-        woven_product(d1, a3_raw[0], dh[0])
         q3 = quantize_da(d3)
-        first = (quantize_da(d1), q3)
         d1 = new_da()
         woven_product(d1, a3_raw[1], dh[1])
+        first = (quantize_da(woven), q3)
         load_saved("p2", a3_raw, a3_rows, 3, 1)
         w13_q = quantize_w13()
         round_w2(3, 0)
+        load_saved("s3", a1_raw, a1_rows, 3, 1)
         round_w2(3, 1)
         d3 = new_da()
         woven_product(d3, a1_raw[1], dh[1])
@@ -297,16 +314,18 @@ def tile_moe_bdx_glu_relu_kernel(tc, dyT, a1, a3, w2, w1, w3, gate, offs, out):
         second_product(0, first[0], first[1], 7, dx[:])
         quantize_w2(3)
         first_product(3)
-        mask = relu_and_mask(2, "s2")
-        dh[2] = as_rows(turn("s8", [P, PACK * C], F32, "dh2"))
+        relu(2)
+        dh[2] = as_rows(turn("s5", [P, PACK * C], F32, "dh2"))
         plain(2, dh[2])
+        mask = make_mask(2, "s8")
         scatter(0, dx[:])
         third = derivative_masked_late(2, mask)
-        mask = relu_and_mask(3, "s5")
-        dh[3] = as_rows(turn("s9", [P, PACK * C], F32, "dh3"))
-        plain(3, dh[3])
         dx = turn("dx1", [P, C], F32, "dx1")
         second_product(1, second[0], second[1], 0, dx[:])
+        relu(3)
+        dh[3] = as_rows(turn("s6", [P, PACK * C], F32, "dh3"))
+        plain(3, dh[3])
+        mask = make_mask(3, "s0")
         scatter(1, dx[:])
         q1, q3 = derivative_masked_late(3, mask)
         dx = turn("s3", [P, C], F32, "dx2")

@@ -20,8 +20,7 @@ E4M3X4 = mybir.dt.float8_e4m3fn_x4
 E5M2X4 = mybir.dt.float8_e5m2_x4
 MULT = mybir.AluOpType.mult
 IS_GT = mybir.AluOpType.is_gt
-RELU = mybir.ActivationFunctionType.Relu
-SIGN = mybir.ActivationFunctionType.Sign
+MAX = mybir.AluOpType.max
 
 FLOPS = 2 * N * H * E * C + 2 * 2 * H * K * E * C
 BYTES = 4 * (N * T + 2 * H * E * C + E * N * H + 2 * E * H * K + E * C + K * T) + 2 * P * (E * C // 16)
@@ -139,8 +138,8 @@ def tile_moe_bdx_glu_relu_kernel(tc, dyT, a1, a3, w2, w1, w3, gate, offs, out):
                 in_=w13_raw[n][:].rearrange("p e j (k i) -> p e k j i", i=4),
             )
 
-        def quantize_w13():
-            return quantize(w13_b[0], 2 * E * K, "w13", E4M3X4, 1)
+        def quantize_w13(slot):
+            return quantize(w13_b[0], 2 * E * K, "w13", E4M3X4, 1, slot)
 
         banks = {}
 
@@ -159,76 +158,56 @@ def tile_moe_bdx_glu_relu_kernel(tc, dyT, a1, a3, w2, w1, w3, gate, offs, out):
                         stop=(c == PASSES - 1),
                     )
 
-        def masked(e, dh):
+        def read_banks(e, dh_slot, rows_slot, on_gpsimd):
+            dh = turn(dh_slot, [P, PACK, C], F32, "dh")
+            rows[e] = turn(rows_slot, [P, 2 * PACK, C], BF16, "rows")
             for t in range(PACK):
                 nc.vector.scalar_tensor_tensor(dh[:, t, :], a1_raw[e][:, t, :], 0.0, banks[e, t][:], op0=IS_GT, op1=MULT)
-
-        def woven_product(da, a, dh):
-            nc.vector.tensor_tensor(
-                da[:].rearrange("p (s i t) -> p s t i", i=2, t=PACK),
-                a.rearrange("p t (s i) -> p s t i", i=2),
-                dh.rearrange("p t (s i) -> p s t i", i=2),
-                MULT,
-            )
-
-        def plain(e, dh):
+            for t in range(on_gpsimd):
+                nc.gpsimd.tensor_tensor(rows[e][:, t, :], a3_raw[e][:, t, :], dh[:, t, :], MULT)
             for t in range(PACK):
-                nc.scalar.copy(out=dh[:, t, :], in_=banks[e, t][:])
-
-        def relu(e):
-            for lo in (0, C // 2):
-                half = a1_raw[e][:, :, lo : lo + C // 2]
-                nc.scalar.activation(half, half, RELU)
-
-        def make_mask(e, tag):
-            mask = turn(tag, [P, PACK * C], BF16, "mask")
-            for lo in (0, C // 2):
-                nc.scalar.activation(
-                    mask[:, PACK * lo : PACK * (lo + C // 2)].rearrange("p (s i t) -> p s t i", i=4, t=PACK),
-                    a1_raw[e][:, :, lo : lo + C // 2].rearrange("p t (s i) -> p s t i", i=4),
-                    SIGN,
+                nc.vector.scalar_tensor_tensor(
+                    rows[e][:, PACK + t, :], a1_raw[e][:, t, :], 0.0, banks[e, t][:], op0=MAX, op1=MULT
                 )
-            return mask
+            if on_gpsimd < PACK:
+                nc.vector.tensor_tensor(
+                    rows[e][:, on_gpsimd:PACK, :], a3_raw[e][:, on_gpsimd:, :], dh[:, on_gpsimd:, :], MULT
+                )
 
-        def derivative_masked_late(e, mask):
-            d1 = new_da()
-            woven_product(d1, a3_raw[e], dh[e])
-            d3 = new_da()
-            woven_product(d3, a1_raw[e], dh[e])
-            nc.vector.tensor_tensor(d1[:], d1[:], mask[:], MULT)
-            q3 = quantize_da(d3)
-            return quantize_da(d1), q3
+        def weave(e, slot):
+            da_b[e] = turn(slot, [P, 2 * PACK * C], BF16, "da")
+            for n in (1, 0):
+                nc.scalar.copy(
+                    out=da_b[e][:, n * PACK * C : (n + 1) * PACK * C].rearrange("p (s i t) -> p s t i", i=4, t=PACK),
+                    in_=rows[e][:, n * PACK : (n + 1) * PACK, :].rearrange("p t (s i) -> p s t i", i=4),
+                )
 
-        def new_da():
-            return work.tile([P, PACK * C], BF16, tag="da", bufs=3, align_bytes=64, name="da")
+        def quantize_da(e, slot=None):
+            da_q[e] = quantize(da_b[e], 2 * C, "da", E5M2X4, 3, slot)
 
-        def quantize_da(da):
-            return quantize(da, C, "da", E5M2X4, 4)
-
-        def second_product(e, q1, q3, where, dx):
-            bank = psum.tile([P, C], F32, tag="bank%d" % where, name="dxbank")
-            for n, dq in ((1, q3), (0, q1)):
+        def second_product(e, dx):
+            bank = psum.tile([P, C], F32, tag="bank%d" % e, name="dxbank")
+            for n in range(2):
                 nc.tensor.matmul_mx(
                     out=bank[:],
                     lhsT=w13_q[0][:, (n * E + e) * K : (n * E + e + 1) * K].bitcast(E4M3X4),
                     lhsT_scale=w13_q[1][:, (n * E + e) * K : (n * E + e + 1) * K],
-                    rhs=dq[0][:].bitcast(E5M2X4),
-                    rhs_scale=dq[1][:],
-                    start=(n == 1),
-                    stop=(n == 0),
+                    rhs=da_q[e][0][:, n * C : (n + 1) * C].bitcast(E5M2X4),
+                    rhs_scale=da_q[e][1][:, n * C : (n + 1) * C],
+                    start=(n == 0),
+                    stop=(n == 1),
                 )
             nc.scalar.copy(out=dx, in_=bank[:])
 
-        def scatter(e, dx):
-            nc.vector.tensor_copy(result[:].indirect(offsets[:, e * C // 16 : (e + 1) * C // 16]), dx)
+        def scatter(first, count, dx):
+            nc.vector.tensor_copy(result[:].indirect(offsets[:, first * C // 16 : (first + count) * C // 16]), dx[:])
 
         def new_planes(tag):
             return turn(tag, [P, PACK, PAIR], F32, "planes")
 
-        def as_rows(x):
-            return x[:, 0 : PACK * C].rearrange("p (t s) -> p t s", t=PACK)
-
-        dh = {}
+        rows = {}
+        da_b = {}
+        da_q = {}
         planes = {(0, 0): new_planes("p0"), (1, 0): new_planes("p1")}
         gather(0, 0, 0, planes[0, 0], (0, C, PAIR))
         gather(1, 0, 0, planes[1, 0])
@@ -243,7 +222,8 @@ def tile_moe_bdx_glu_relu_kernel(tc, dyT, a1, a3, w2, w1, w3, gate, offs, out):
         gather(0, 0, 2, planes[0, 0])
         gather(1, 0, 2, planes[1, 0])
         load_w2("s3", 2, 1)
-        load_saved("s2", a3_raw, a3_rows, 0, 1)
+        load_w2("s4", 3, 1)
+        load_w2("s2", 3, 0)
         gather(0, 0, 3, planes[0, 0])
         gather(1, 0, 3, planes[1, 0])
         round_w2(1, 0)
@@ -256,15 +236,16 @@ def tile_moe_bdx_glu_relu_kernel(tc, dyT, a1, a3, w2, w1, w3, gate, offs, out):
         prepare_g("s0", 1, 0, planes[1, 0])
         round_w2(2, 0)
         prepare_g("s1", 0, 1, planes[0, 1])
-        load_saved("p2", a3_raw, a3_rows, 1, 1)
+        load_saved("p2", a1_raw, a1_rows, 2, 1)
         round_w2(2, 1)
         quantize_w2(0)
         quantize_g(0, 0)
-        load_w13("s9", 0)
+        load_saved("s9", a3_raw, a3_rows, 0, 1)
         quantize_g(1, 0)
-        load_w13("s0", 1)
-        load_w2("s3", 3, 0)
-        round_w13(0)
+        load_saved("s0", a3_raw, a3_rows, 1, 1)
+        load_saved("s3", a1_raw, a1_rows, 3, 1)
+        round_w2(3, 1)
+        round_w2(3, 0)
         quantize_g(0, 1)
         first_product(0)
         quantize_w2(1, "s1")
@@ -272,66 +253,41 @@ def tile_moe_bdx_glu_relu_kernel(tc, dyT, a1, a3, w2, w1, w3, gate, offs, out):
         planes[1, 1] = new_planes("p1")
         for t in range(PACK):
             gather(1, 1, t, planes[1, 1])
-        prepare_g("s9", 1, 1, planes[1, 1])
-        round_w13(1)
-        load_saved("s7", a1_raw, a1_rows, 2, 1)
-        load_w2("s8", 3, 1)
-        result = turn("s4", [P, T], F32, "result")
+        prepare_g("s2", 1, 1, planes[1, 1])
+        load_w13("s6", 0)
+        load_w13("s8", 1)
 
-        dh[0] = as_rows(turn("even", [P, PACK * C], F32, "dh0"))
-        dh[1] = as_rows(turn("odd", [P, PACK * C], F32, "dh1"))
-        masked(0, dh[0])
-        rows = turn("rows", [P, PACK, C], BF16, "rows")
-        for t in range(GPSIMD_ROWS):
-            nc.gpsimd.tensor_tensor(rows[:, t, :], a3_raw[0][:, t, :], dh[0][:, t, :], MULT)
-        masked(1, dh[1])
-        nc.vector.tensor_tensor(rows[:, GPSIMD_ROWS:, :], a3_raw[0][:, GPSIMD_ROWS:, :], dh[0][:, GPSIMD_ROWS:, :], MULT)
-        woven = turn("p1", [P, PACK * C], BF16, "woven")
-        nc.scalar.copy(
-            out=woven[:].rearrange("p (s i t) -> p s t i", i=4, t=PACK),
-            in_=rows[:].rearrange("p t (s i) -> p s t i", i=4),
-        )
-        d3 = new_da()
-        woven_product(d3, a1_raw[0], dh[0])
-        quantize_w2(2, "s2")
+        read_banks(0, "even", "s5", PACK)
+        load_saved("s1", a3_raw, a3_rows, 2, 1)
+        load_saved("s9", a3_raw, a3_rows, 3, 1)
+        read_banks(1, "odd", "s7", GPSIMD_ROWS)
+        quantize_w2(2, "p0")
         quantize_g(1, 1)
-        load_saved("s9", a3_raw, a3_rows, 2, 1)
         first_product(2)
-        q3 = quantize_da(d3)
-        d1 = new_da()
-        woven_product(d1, a3_raw[1], dh[1])
-        first = (quantize_da(woven), q3)
-        load_saved("p2", a3_raw, a3_rows, 3, 1)
-        w13_q = quantize_w13()
-        round_w2(3, 0)
-        load_saved("s3", a1_raw, a1_rows, 3, 1)
-        round_w2(3, 1)
-        d3 = new_da()
-        woven_product(d3, a1_raw[1], dh[1])
-        q1 = quantize_da(d1)
-        second = (q1, quantize_da(d3))
-        dx = turn("dx0", [P, C], F32, "dx0")
-        second_product(0, first[0], first[1], 7, dx[:])
-        quantize_w2(3)
+        quantize_w2(3, "s0")
         first_product(3)
-        relu(2)
-        dh[2] = as_rows(turn("s5", [P, PACK * C], F32, "dh2"))
-        plain(2, dh[2])
-        mask = make_mask(2, "s8")
-        scatter(0, dx[:])
-        third = derivative_masked_late(2, mask)
-        dx = turn("dx1", [P, C], F32, "dx1")
-        second_product(1, second[0], second[1], 0, dx[:])
-        relu(3)
-        dh[3] = as_rows(turn("s6", [P, PACK * C], F32, "dh3"))
-        plain(3, dh[3])
-        mask = make_mask(3, "s0")
-        scatter(1, dx[:])
-        q1, q3 = derivative_masked_late(3, mask)
-        dx = turn("s3", [P, C], F32, "dx2")
-        second_product(2, third[0], third[1], 1, dx[:])
-        last = turn("dx0", [P, C], F32, "dx3")
-        second_product(3, q1, q3, 2, last[:])
-        scatter(2, dx[:])
-        scatter(3, last[:])
+        weave(0, "p1")
+        weave(1, "s4")
+        round_w13(0)
+        round_w13(1)
+        read_banks(2, "even", "rows2", PACK)
+        read_banks(3, "odd", "rows3", GPSIMD_ROWS)
+        weave(2, "s2")
+        w13_q = quantize_w13("s3")
+        quantize_da(0)
+        dx0 = turn("dx0", [P, C], F32, "dx0")
+        second_product(0, dx0[:])
+        weave(3, "p0")
+        quantize_da(1)
+        result = turn("s4", [P, T], F32, "result")
+        dx1 = turn("dx1", [P, C], F32, "dx1")
+        second_product(1, dx1[:])
+        quantize_da(2)
+        scatter(0, 1, dx0)
+        quantize_da(3, "dx0")
+        dx23 = turn("s5", [P, PAIR], F32, "dx23")
+        second_product(2, dx23[:, 0:C])
+        second_product(3, dx23[:, C:])
+        scatter(1, 1, dx1)
+        scatter(2, 2, dx23)
         nc.sync.dma_start(out, result[:])

@@ -9,7 +9,8 @@ PASSES = N // (P * PACK)
 PAIR = 2 * C
 GQ = 3
 WQ = 2
-GPSIMD_ROWS = 3
+FIRST_ROWS = (0, 1, 2, 4)
+SECOND_ROWS = (0, 1, 3)
 
 F32 = mybir.dt.float32
 BF16 = mybir.dt.bfloat16
@@ -114,8 +115,8 @@ def tile_moe_bdx_glu_relu_kernel(tc, dyT, a1, a3, w2, w1, w3, gate, offs, out):
             )
             g_b[pair, c] = gb
 
-        def quantize_g(pair, c):
-            g_q[pair, c] = quantize(g_b[pair, c], PAIR, "g", E5M2X4, GQ)
+        def quantize_g(pair, c, slot=None):
+            g_q[pair, c] = quantize(g_b[pair, c], PAIR, "g", E5M2X4, GQ, slot)
 
         def round_w2(e, c):
             if e not in w2_b:
@@ -158,21 +159,22 @@ def tile_moe_bdx_glu_relu_kernel(tc, dyT, a1, a3, w2, w1, w3, gate, offs, out):
                         stop=(c == PASSES - 1),
                     )
 
-        def read_banks(e, dh_slot, rows_slot, on_gpsimd):
+        def read_banks(e, dh_slot, rows_slot, cuts):
             dh = turn(dh_slot, [P, PACK, C], F32, "dh")
             rows[e] = turn(rows_slot, [P, 2 * PACK, C], BF16, "rows")
             for t in range(PACK):
                 nc.vector.scalar_tensor_tensor(dh[:, t, :], a1_raw[e][:, t, :], 0.0, banks[e, t][:], op0=IS_GT, op1=MULT)
-            for t in range(on_gpsimd):
-                nc.gpsimd.tensor_tensor(rows[e][:, t, :], a3_raw[e][:, t, :], dh[:, t, :], MULT)
+            for lo, hi in zip(cuts, cuts[1:]):
+                nc.gpsimd.tensor_tensor(rows[e][:, lo:hi, :], a3_raw[e][:, lo:hi, :], dh[:, lo:hi, :], MULT)
             for t in range(PACK):
                 nc.vector.scalar_tensor_tensor(
                     rows[e][:, PACK + t, :], a1_raw[e][:, t, :], 0.0, banks[e, t][:], op0=MAX, op1=MULT
                 )
-            if on_gpsimd < PACK:
-                nc.vector.tensor_tensor(
-                    rows[e][:, on_gpsimd:PACK, :], a3_raw[e][:, on_gpsimd:, :], dh[:, on_gpsimd:, :], MULT
-                )
+            masked[e] = dh
+
+        def last_row(e):
+            t = SECOND_ROWS[-1]
+            nc.vector.tensor_tensor(rows[e][:, t:PACK, :], a3_raw[e][:, t:, :], masked[e][:, t:, :], MULT)
 
         def weave(e, slot):
             da_b[e] = turn(slot, [P, 2 * PACK * C], BF16, "da")
@@ -206,6 +208,7 @@ def tile_moe_bdx_glu_relu_kernel(tc, dyT, a1, a3, w2, w1, w3, gate, offs, out):
             return turn(tag, [P, PACK, PAIR], F32, "planes")
 
         rows = {}
+        masked = {}
         da_b = {}
         da_q = {}
         planes = {(0, 0): new_planes("p0"), (1, 0): new_planes("p1")}
@@ -257,28 +260,30 @@ def tile_moe_bdx_glu_relu_kernel(tc, dyT, a1, a3, w2, w1, w3, gate, offs, out):
         load_w13("s6", 0)
         load_w13("s8", 1)
 
-        read_banks(0, "even", "s5", PACK)
+        read_banks(0, "even", "s5", FIRST_ROWS)
         load_saved("s1", a3_raw, a3_rows, 2, 1)
-        load_saved("s9", a3_raw, a3_rows, 3, 1)
-        read_banks(1, "odd", "s7", GPSIMD_ROWS)
-        quantize_w2(2, "p0")
-        quantize_g(1, 1)
-        first_product(2)
-        quantize_w2(3, "s0")
-        first_product(3)
+        read_banks(1, "odd", "s7", SECOND_ROWS)
+        load_saved("p0", a3_raw, a3_rows, 3, 1)
+        quantize_w2(2, "s9")
+        last_row(1)
         weave(0, "p1")
+        quantize_da(0)
+        quantize_g(1, 1, "p1")
+        first_product(2)
+        quantize_w2(3, "s2")
+        first_product(3)
         weave(1, "s4")
         round_w13(0)
         round_w13(1)
-        read_banks(2, "even", "rows2", PACK)
-        read_banks(3, "odd", "rows3", GPSIMD_ROWS)
-        weave(2, "s2")
-        w13_q = quantize_w13("s3")
-        quantize_da(0)
+        read_banks(2, "even", "rows2", FIRST_ROWS)
+        read_banks(3, "odd", "rows3", SECOND_ROWS)
+        w13_q = quantize_w13("p2")
         dx0 = turn("dx0", [P, C], F32, "dx0")
         second_product(0, dx0[:])
-        weave(3, "p0")
         quantize_da(1)
+        last_row(3)
+        weave(2, "s0")
+        weave(3, "s9")
         result = turn("s4", [P, T], F32, "result")
         dx1 = turn("dx1", [P, C], F32, "dx1")
         second_product(1, dx1[:])

@@ -7,10 +7,11 @@ P = 128
 PACK = 4
 PASSES = N // (P * PACK)
 PAIR = 2 * C
+FIRST = 384
 GQ = 3
 WQ = 2
-FIRST_ROWS = (0, 1, 2, 4)
-SECOND_ROWS = (0, 1, 3)
+FIRST_CUTS = (0, C, 2 * C, PACK * C)
+SECOND_CUTS = (0, C, 5 * C // 2)
 
 F32 = mybir.dt.float32
 BF16 = mybir.dt.bfloat16
@@ -81,8 +82,8 @@ def tile_moe_bdx_glu_relu_kernel(tc, dyT, a1, a3, w2, w1, w3, gate, offs, out):
         a3_raw = {}
         gates = turn("even", [P, T], F32, "gates")
         load_dy("s0", 0, 0)
-        nc.sync.dma_start(gates[:, 0:C], gate[0:P, 0:C])
-        nc.sync.dma_start(gates[:, C:PAIR], gate[0:P, C:PAIR])
+        nc.sync.dma_start(gates[:, 0:FIRST], gate[0:P, 0:FIRST])
+        nc.sync.dma_start(gates[:, FIRST:PAIR], gate[0:P, FIRST:PAIR])
         nc.sync.dma_start(gates[:, PAIR:T], gate[0:P, PAIR:T])
         load_dy("s1", 0, 1)
         load_w2("s2", 0, 0)
@@ -159,13 +160,16 @@ def tile_moe_bdx_glu_relu_kernel(tc, dyT, a1, a3, w2, w1, w3, gate, offs, out):
                         stop=(c == PASSES - 1),
                     )
 
+        def flat(x):
+            return x[:, :, :].rearrange("p t s -> p (t s)")
+
         def read_banks(e, dh_slot, rows_slot, cuts):
             dh = turn(dh_slot, [P, PACK, C], F32, "dh")
             rows[e] = turn(rows_slot, [P, 2 * PACK, C], BF16, "rows")
             for t in range(PACK):
                 nc.vector.scalar_tensor_tensor(dh[:, t, :], a1_raw[e][:, t, :], 0.0, banks[e, t][:], op0=IS_GT, op1=MULT)
             for lo, hi in zip(cuts, cuts[1:]):
-                nc.gpsimd.tensor_tensor(rows[e][:, lo:hi, :], a3_raw[e][:, lo:hi, :], dh[:, lo:hi, :], MULT)
+                nc.gpsimd.tensor_tensor(flat(rows[e])[:, lo:hi], flat(a3_raw[e])[:, lo:hi], flat(dh)[:, lo:hi], MULT)
             for t in range(PACK):
                 nc.vector.scalar_tensor_tensor(
                     rows[e][:, PACK + t, :], a1_raw[e][:, t, :], 0.0, banks[e, t][:], op0=MAX, op1=MULT
@@ -173,31 +177,37 @@ def tile_moe_bdx_glu_relu_kernel(tc, dyT, a1, a3, w2, w1, w3, gate, offs, out):
             masked[e] = dh
 
         def last_row(e):
-            t = SECOND_ROWS[-1]
-            nc.vector.tensor_tensor(rows[e][:, t:PACK, :], a3_raw[e][:, t:, :], masked[e][:, t:, :], MULT)
+            lo, hi = SECOND_CUTS[-1], PACK * C
+            nc.vector.tensor_tensor(flat(rows[e])[:, lo:hi], flat(a3_raw[e])[:, lo:hi], flat(masked[e])[:, lo:hi], MULT)
 
-        def weave(e, slot):
-            da_b[e] = turn(slot, [P, 2 * PACK * C], BF16, "da")
-            for n in (1, 0):
+        def weave(e, slot, halves=(1, 0)):
+            da = turn(slot, [P, len(halves) * PACK * C], BF16, "da")
+            for n in halves:
+                lo = (n - min(halves)) * PACK * C
                 nc.scalar.copy(
-                    out=da_b[e][:, n * PACK * C : (n + 1) * PACK * C].rearrange("p (s i t) -> p s t i", i=4, t=PACK),
+                    out=da[:, lo : lo + PACK * C].rearrange("p (s i t) -> p s t i", i=4, t=PACK),
                     in_=rows[e][:, n * PACK : (n + 1) * PACK, :].rearrange("p t (s i) -> p s t i", i=4),
                 )
+            da_b[e, halves] = da
 
-        def quantize_da(e, slot=None):
-            da_q[e] = quantize(da_b[e], 2 * C, "da", E5M2X4, 3, slot)
+        def quantize_da(e, halves=(1, 0)):
+            count = len(halves)
+            words, scales = quantize(da_b[e, halves], count * C, "da%d" % count, E5M2X4, 3 if count == 2 else 2)
+            for n in halves:
+                lo = (n - min(halves)) * C
+                da_q[e, n] = (words[:, lo : lo + C], scales[:, lo : lo + C])
 
         def second_product(e, dx):
             bank = psum.tile([P, C], F32, tag="bank%d" % e, name="dxbank")
-            for n in range(2):
+            for n in (1, 0):
                 nc.tensor.matmul_mx(
                     out=bank[:],
                     lhsT=w13_q[0][:, (n * E + e) * K : (n * E + e + 1) * K].bitcast(E4M3X4),
                     lhsT_scale=w13_q[1][:, (n * E + e) * K : (n * E + e + 1) * K],
-                    rhs=da_q[e][0][:, n * C : (n + 1) * C].bitcast(E5M2X4),
-                    rhs_scale=da_q[e][1][:, n * C : (n + 1) * C],
-                    start=(n == 0),
-                    stop=(n == 1),
+                    rhs=da_q[e, n][0].bitcast(E5M2X4),
+                    rhs_scale=da_q[e, n][1],
+                    start=(n == 1),
+                    stop=(n == 0),
                 )
             nc.scalar.copy(out=dx, in_=bank[:])
 
@@ -212,7 +222,7 @@ def tile_moe_bdx_glu_relu_kernel(tc, dyT, a1, a3, w2, w1, w3, gate, offs, out):
         da_b = {}
         da_q = {}
         planes = {(0, 0): new_planes("p0"), (1, 0): new_planes("p1")}
-        gather(0, 0, 0, planes[0, 0], (0, C, PAIR))
+        gather(0, 0, 0, planes[0, 0], (0, FIRST, PAIR))
         gather(1, 0, 0, planes[1, 0])
         load_w2("s0", 1, 1)
         load_dy("s8", 1, 2)
@@ -260,9 +270,9 @@ def tile_moe_bdx_glu_relu_kernel(tc, dyT, a1, a3, w2, w1, w3, gate, offs, out):
         load_w13("s6", 0)
         load_w13("s8", 1)
 
-        read_banks(0, "even", "s5", FIRST_ROWS)
+        read_banks(0, "even", "s5", FIRST_CUTS)
         load_saved("s1", a3_raw, a3_rows, 2, 1)
-        read_banks(1, "odd", "s7", SECOND_ROWS)
+        read_banks(1, "odd", "s7", SECOND_CUTS)
         load_saved("p0", a3_raw, a3_rows, 3, 1)
         quantize_w2(2, "s9")
         last_row(1)
@@ -275,24 +285,27 @@ def tile_moe_bdx_glu_relu_kernel(tc, dyT, a1, a3, w2, w1, w3, gate, offs, out):
         weave(1, "s4")
         round_w13(0)
         round_w13(1)
-        read_banks(2, "even", "rows2", FIRST_ROWS)
-        read_banks(3, "odd", "rows3", SECOND_ROWS)
+        read_banks(2, "even", "rows2", FIRST_CUTS)
+        read_banks(3, "odd", "rows3", SECOND_CUTS)
         w13_q = quantize_w13("p2")
-        dx0 = turn("dx0", [P, C], F32, "dx0")
-        second_product(0, dx0[:])
-        quantize_da(1)
-        last_row(3)
+        dx01 = turn("dx0", [P, PAIR], F32, "dx01")
+        second_product(0, dx01[:, 0:C])
         weave(2, "s0")
-        weave(3, "s9")
+        weave(3, "rows2", (1,))
+        quantize_da(1)
+        second_product(1, dx01[:, C:])
+        last_row(3)
         result = turn("s4", [P, T], F32, "result")
-        dx1 = turn("dx1", [P, C], F32, "dx1")
-        second_product(1, dx1[:])
         quantize_da(2)
-        scatter(0, 1, dx0)
-        quantize_da(3, "dx0")
-        dx23 = turn("s5", [P, PAIR], F32, "dx23")
-        second_product(2, dx23[:, 0:C])
-        second_product(3, dx23[:, C:])
-        scatter(1, 1, dx1)
-        scatter(2, 2, dx23)
-        nc.sync.dma_start(out, result[:])
+        weave(3, "s0", (0,))
+        quantize_da(3, (1,))
+        scatter(0, 2, dx01)
+        quantize_da(3, (0,))
+        dx2 = turn("rows3", [P, C], F32, "dx2")
+        second_product(2, dx2[:])
+        dx3 = turn("s5", [P, C], F32, "dx3")
+        second_product(3, dx3[:])
+        scatter(2, 1, dx2)
+        scatter(3, 1, dx3)
+        nc.sync.dma_start(out[:, 0:PAIR], result[:, 0:PAIR])
+        nc.scalar.dma_start(out[:, PAIR:T], result[:, PAIR:T])

@@ -1,17 +1,16 @@
 from contextlib import ExitStack
 
 import concourse.mybir as mybir
+from concourse.masks import make_identity
 
 E, C, T, K, H, N = 4, 512, 2048, 128, 512, 1024
 P = 128
 PACK = 4
 PASSES = N // (P * PACK)
 PAIR = 2 * C
-FIRST = 384
-GQ = 3
-WQ = 2
-FIRST_CUTS = (0, C, 2 * C, PACK * C)
-SECOND_CUTS = (0, C, 5 * C // 2)
+BLOCKS = C // P
+RUN = PAIR // P
+ROOM = 8192
 
 F32 = mybir.dt.float32
 BF16 = mybir.dt.bfloat16
@@ -23,6 +22,7 @@ E5M2X4 = mybir.dt.float8_e5m2_x4
 MULT = mybir.AluOpType.mult
 IS_GT = mybir.AluOpType.is_gt
 MAX = mybir.AluOpType.max
+COPY = mybir.ActivationFunctionType.Copy
 
 FLOPS = 2 * N * H * E * C + 2 * 2 * H * K * E * C
 BYTES = 4 * (N * T + 2 * H * E * C + E * N * H + 2 * E * H * K + E * C + K * T) + 2 * P * (E * C // 16)
@@ -38,274 +38,403 @@ def tile_moe_bdx_glu_relu_kernel(tc, dyT, a1, a3, w2, w1, w3, gate, offs, out):
 
     with ExitStack() as ctx:
         held = ctx.enter_context(tc.tile_pool(name="held", bufs=1))
-        work = ctx.enter_context(tc.tile_pool(name="work", bufs=2))
-        codes = ctx.enter_context(tc.tile_pool(name="codes", bufs=6))
+        rooms = ctx.enter_context(tc.tile_pool(name="rooms", bufs=1))
         psum = ctx.enter_context(tc.psum_pool(name="psum", bufs=1))
 
-        def turn(tag, shape, dtype, name):
-            return held.tile(shape, dtype, tag=tag, align_bytes=64, name=name)
+        def room(number, shape, dtype, name, quarter=0):
+            at = number * ROOM + int(quarter * (ROOM // 4))
+            return rooms.tile(shape, dtype, tag="%s_at%d" % (name, at), offset=at, align_bytes=64, name=name)
 
-        def load(tag, src, shape):
-            raw = turn(tag, shape, F32, "raw_" + tag)
-            nc.sync.dma_start(raw[:], src)
-            return raw
+        def small(shape, dtype, name):
+            return held.tile(shape, dtype, align_bytes=64, name=name)
+
+        def bank(b, shape, name):
+            return psum.tile(shape, F32, tag="bank%d" % b, name=name)
+
+        dy, w2_raw, w13_raw, a1_raw, a3_raw = {}, {}, {}, {}, {}
+        w2_b, w2_q, g_q, gates = {}, {}, {}, {}
+        dh_banks, masked, rows, da_b, da_q = {}, {}, {}, {}, {}
+        word_banks, a1_row, w13_b, pairs = {}, {}, {}, {}
+
+        def load(dst, src):
+            nc.sync.dma_start(dst, src)
+            return dst
 
         def load_dy(tag, c, t):
-            dy[c, t] = load(tag, dy_rows[c, t], [P, T])
+            dy[c, t] = load(room(tag, [P, T], F32, "dy")[:], dy_rows[c, t])
 
         def load_w2(tag, e, c):
-            w2_raw[e, c] = load(tag, w2_rows[e, c], [P, PACK, H])
+            w2_raw[e, c] = load(room(tag, [P, PACK, H], F32, "w2_raw")[:], w2_rows[e, c])
 
-        def load_w13(tag, n):
-            w13_raw[n] = load(tag, (w1, w3)[n].rearrange("e (p j) k -> p e j k", j=PACK), [P, E, PACK, K])
+        def load_w13(at, n):
+            src = (w1, w3)[n].rearrange("e (p j) k -> p e j k", j=PACK)
+            w13_raw[n] = load(room(at, [P, E, PACK, K], F32, "w13_raw")[:], src)
 
-        def load_saved(tag, saved, rows, first, count):
-            raw = load(tag, rows[:, :, first * C : (first + count) * C], [P, PACK, count * C])
-            for e in range(count):
-                saved[first + e] = raw[:, :, e * C : (e + 1) * C]
+        def load_saved(tag, saved, src, e):
+            saved[e] = load(room(tag, [P, PACK, C], F32, "saved")[:], src[:, :, e * C : (e + 1) * C])
 
-        def quantize(src, width, tag, dtype, bufs, slot=None):
-            if slot is None:
-                words = codes.tile([P, width], U32, tag=tag + "_w", bufs=bufs, align_bytes=64, name=tag + "_w")
+        def load_a1_apart(at, e):
+            a1_raw[e] = load(room(at, [P, 2, C], F32, "a1_low")[:], a1_rows[:, 0:2, e * C : (e + 1) * C])
+            for t in range(2):
+                a1_row[e, t] = a1_raw[e][:, t, :]
+            for t in range(2, PACK):
+                a1_row[e, t] = load(room(at, [P, C], F32, "a1_row", t)[:], a1_rows[:, t, e * C : (e + 1) * C])
+
+        def load_a1_last(at, e):
+            a1_raw[e] = load(room(at, [P, 1, C], F32, "a1_first")[:], a1_rows[:, 0:1, e * C : (e + 1) * C])
+            a1_row[e, 0] = a1_raw[e][:, 0, :]
+            middle = load(room(at, [P, 2, C], F32, "a1_middle", 2)[:], a1_rows[:, 1:3, e * C : (e + 1) * C])
+            a1_row[e, 1], a1_row[e, 2] = middle[:, 0, :], middle[:, 1, :]
+            a1_row[e, 3] = load(room(at, [P, C], F32, "a1_row", 1)[:], a1_rows[:, 3, e * C : (e + 1) * C])
+
+        def load_a1(at, e):
+            load_saved(at, a1_raw, a1_rows, e)
+            for t in range(PACK):
+                a1_row[e, t] = a1_raw[e][:, t, :]
+
+        def codes(at, quarter, width, name, scales_at=None):
+            words = room(at, [P, width], U32, name, quarter)
+            if scales_at:
+                scales = room(scales_at[0], [P, width], U8, name + "_s", scales_at[1])
             else:
-                words = turn(slot, [P, width], U32, tag + "_w")
-            scales = codes.tile([P, width], U8, tag=tag + "_s", bufs=bufs, align_bytes=64, name=tag + "_s")
-            nc.vector.quantize_mx(out=words[:].bitcast(dtype), scales=scales[:], in_=src[:])
-            return words, scales
+                scales = small([P, width], U8, name + "_s")
+            return words[:], scales[:]
 
-        offsets = held.tile([P, E * C // 16], U16, name="offsets")
-        nc.sync.dma_start(offsets[:], offs)
-        dy = {}
-        w2_raw = {}
-        w13_raw = {}
-        a1_raw = {}
-        a3_raw = {}
-        gates = turn("even", [P, T], F32, "gates")
-        load_dy("s0", 0, 0)
-        nc.sync.dma_start(gates[:, 0:FIRST], gate[0:P, 0:FIRST])
-        nc.sync.dma_start(gates[:, FIRST:PAIR], gate[0:P, FIRST:PAIR])
-        nc.sync.dma_start(gates[:, PAIR:T], gate[0:P, PAIR:T])
-        load_dy("s1", 0, 1)
-        load_w2("s2", 0, 0)
-        load_dy("s3", 0, 2)
-        load_w2("s4", 0, 1)
-        load_dy("s5", 0, 3)
-        load_w2("s9", 1, 0)
-        load_dy("s6", 1, 0)
-        load_dy("s7", 1, 1)
+        def part(pair, lo, hi):
+            return pair[0][:, lo:hi], pair[1][:, lo:hi]
 
-        g_b = {}
-        g_q = {}
-        w2_b = {}
-        w2_q = {}
+        def quantize(dst, src, dtype):
+            nc.vector.quantize_mx(out=dst[0].bitcast(dtype), scales=dst[1], in_=src)
 
-        def gather(pair, c, t, planes, cuts=(0, PAIR)):
-            for lo, hi in zip(cuts, cuts[1:]):
-                nc.vector.tensor_tensor(
-                    planes[:, t, lo:hi],
-                    dy[c, t][:].indirect(offsets[:, (pair * PAIR + lo) // 16 : (pair * PAIR + hi) // 16]),
-                    gates[:, pair * PAIR + lo : pair * PAIR + hi],
-                    MULT,
+        def woven(x):
+            return x.rearrange("p (s i t) -> p s t i", i=4, t=PACK)
+
+        def planes_of(x):
+            return x.rearrange("p t (s i) -> p s t i", i=4)
+
+        def slots(lo, hi):
+            return offsets[:, lo // 16 : hi // 16]
+
+        def spread_gates(pair, first_bank):
+            for half in range(RUN // 4):
+                spread = bank(first_bank + half, [P, 4, P], "spread")
+                for j in range(4):
+                    col = half * 4 + j
+                    nc.tensor.transpose(spread[:, j, :], gate_runs[:, pair, col : col + 1].to_broadcast([P, P]), ident[:])
+                nc.scalar.copy(
+                    out=gates[pair].rearrange("q (p h j) -> q p h j", h=RUN // 4, j=4)[:, :, half, :],
+                    in_=spread[:].rearrange("q j p -> q p j"),
                 )
 
-        def prepare_g(tag, pair, c, planes):
-            gb = turn(tag, [P, PACK * PAIR], BF16, "gb")
-            nc.scalar.copy(
-                out=gb[:].rearrange("p (s i t) -> p s t i", i=4, t=PACK),
-                in_=planes[:].rearrange("p t (s i) -> p s t i", i=4),
-            )
-            g_b[pair, c] = gb
+        def turn_gates(e):
+            cols = bank(2 + e, [P, BLOCKS, P], "cols")
+            for b in range(BLOCKS):
+                lo = e % 2 * C + b * P
+                nc.tensor.transpose(cols[:, b, :], gates[1][:, lo : lo + P], ident[:])
+            nc.scalar.copy(out=gate_cols[:, e - 2, :], in_=cols[:, :, 0])
 
-        def quantize_g(pair, c, slot=None):
-            g_q[pair, c] = quantize(g_b[pair, c], PAIR, "g", E5M2X4, GQ, slot)
-
-        def round_w2(e, c):
-            if e not in w2_b:
-                w2_b[e] = work.tile([P, PASSES * PACK * H], BF16, tag="wb", bufs=3, align_bytes=64, name="wb")
-            nc.scalar.copy(
-                out=w2_b[e][:, c * PACK * H : (c + 1) * PACK * H].rearrange("p (t m j) -> p m j t", t=PACK, j=PACK),
-                in_=w2_raw[e, c][:].rearrange("p j (m t) -> p m j t", t=PACK),
+        def gather(dst, c, t, first, count):
+            lo = first % 2 * C
+            nc.vector.tensor_tensor(
+                dst, dy[c, t].indirect(slots(first * C, (first + count) * C)), gates[first // 2][:, lo : lo + count * C], MULT
             )
 
-        def quantize_w2(e, slot=None):
-            w2_q[e] = quantize(w2_b[e], PASSES * H, "w2", E4M3X4, WQ, slot)
+        def weave(dst, src):
+            nc.scalar.copy(out=woven(dst), in_=planes_of(src))
 
-        w13_b = {}
-
-        def round_w13(n):
-            if n == 0:
-                w13_b[0] = work.tile([P, PASSES * PACK * H], BF16, tag="wb", bufs=3, align_bytes=64, name="wb")
-            nc.scalar.copy(
-                out=w13_b[0][:, n * PACK * H : (n + 1) * PACK * H].rearrange("p (e k i j) -> p e k j i", e=E, i=4, j=PACK),
-                in_=w13_raw[n][:].rearrange("p e j (k i) -> p e k j i", i=4),
-            )
-
-        def quantize_w13(slot):
-            return quantize(w13_b[0], 2 * E * K, "w13", E4M3X4, 1, slot)
-
-        banks = {}
-
-        def first_product(e):
-            for t in range(PACK):
-                bank = psum.tile([P, C], F32, tag="bank%d" % (e % 2 * PACK + t), name="bank")
-                banks[e, t] = bank
-                for c in range(PASSES):
-                    nc.tensor.matmul_mx(
-                        out=bank[:],
-                        lhsT=w2_q[e][0][:, c * H + t * P : c * H + (t + 1) * P].bitcast(E4M3X4),
-                        lhsT_scale=w2_q[e][1][:, c * H + t * P : c * H + (t + 1) * P],
-                        rhs=g_q[e // 2, c][0][:, e % 2 * C : (e % 2 + 1) * C].bitcast(E5M2X4),
-                        rhs_scale=g_q[e // 2, c][1][:, e % 2 * C : (e % 2 + 1) * C],
-                        start=(c == 0),
-                        stop=(c == PASSES - 1),
+        def pick_and_turn(ring, e, u, places):
+            there = [bank(4 + 2 * (e % 2) + h, [P, 2, 2, P], "there") for h in range(2)]
+            for k in range(2):
+                picked = room(ring, [P, C], F32, "picked", 2 * (1 - u) + k)
+                nc.vector.tensor_copy(picked[:], dy[1, 2 * u + k].indirect(slots(e * C, (e + 1) * C)))
+                for b in range(BLOCKS):
+                    nc.tensor.transpose(there[b // 2][:, b % 2, k, :], picked[:, b * P : (b + 1) * P], ident[:])
+            for h, (at, quarter) in enumerate(places):
+                pairs[e, u, h] = room(at, [P, 2, 2 * P], BF16, "pairs", quarter)
+                for b in range(2):
+                    nc.scalar.activation(
+                        pairs[e, u, h][:, b, :].rearrange("s (q k) -> s q k", k=2),
+                        there[h][:, b, :, :].rearrange("s k q -> s q k"),
+                        COPY,
+                        scale=gate_cols[:, e - 2, 2 * h + b : 2 * h + b + 1],
                     )
 
-        def flat(x):
-            return x[:, :, :].rearrange("p t s -> p (t s)")
+        def turn_back(e):
+            word_banks[e] = [bank(6 - 2 * (e % 2) + h, [P, 2, 2 * P], "back") for h in range(2)]
+            for h in range(2):
+                for u in range(2):
+                    for b in range(2):
+                        nc.tensor.transpose(
+                            word_banks[e][h][:, u, b * P : (b + 1) * P], pairs[e, u, h][:, b, :].bitcast(F32), ident[:]
+                        )
 
-        def read_banks(e, dh_slot, rows_slot, cuts):
-            dh = turn(dh_slot, [P, PACK, C], F32, "dh")
-            rows[e] = turn(rows_slot, [P, 2 * PACK, C], BF16, "rows")
-            for t in range(PACK):
-                nc.vector.scalar_tensor_tensor(dh[:, t, :], a1_raw[e][:, t, :], 0.0, banks[e, t][:], op0=IS_GT, op1=MULT)
-            for lo, hi in zip(cuts, cuts[1:]):
-                nc.gpsimd.tensor_tensor(flat(rows[e])[:, lo:hi], flat(a3_raw[e])[:, lo:hi], flat(dh)[:, lo:hi], MULT)
-            for t in range(PACK):
-                nc.vector.scalar_tensor_tensor(
-                    rows[e][:, PACK + t, :], a1_raw[e][:, t, :], 0.0, banks[e, t][:], op0=MAX, op1=MULT
-                )
-            masked[e] = dh
-
-        def last_row(e):
-            lo, hi = SECOND_CUTS[-1], PACK * C
-            nc.vector.tensor_tensor(flat(rows[e])[:, lo:hi], flat(a3_raw[e])[:, lo:hi], flat(masked[e])[:, lo:hi], MULT)
-
-        def weave(e, slot, halves=(1, 0)):
-            da = turn(slot, [P, len(halves) * PACK * C], BF16, "da")
-            for n in halves:
-                lo = (n - min(halves)) * PACK * C
+        def join(at, quarter, e):
+            gb = room(at, [P, PACK * C], BF16, "joined", quarter)
+            for h in range(2):
                 nc.scalar.copy(
-                    out=da[:, lo : lo + PACK * C].rearrange("p (s i t) -> p s t i", i=4, t=PACK),
-                    in_=rows[e][:, n * PACK : (n + 1) * PACK, :].rearrange("p t (s i) -> p s t i", i=4),
+                    out=gb[:, h * 2 * C : (h + 1) * 2 * C].bitcast(F32).rearrange("p (s u) -> p s u", u=2),
+                    in_=word_banks[e][h][:].rearrange("p u s -> p s u"),
                 )
-            da_b[e, halves] = da
+            return gb
 
-        def quantize_da(e, halves=(1, 0)):
-            count = len(halves)
-            words, scales = quantize(da_b[e, halves], count * C, "da%d" % count, E5M2X4, 3 if count == 2 else 2)
-            for n in halves:
-                lo = (n - min(halves)) * C
-                da_q[e, n] = (words[:, lo : lo + C], scales[:, lo : lo + C])
+        def round_w2(tag, e, c):
+            if e not in w2_b:
+                w2_b[e] = room(tag, [P, PASSES * PACK * H], BF16, "w2_b")
+            nc.scalar.copy(
+                out=w2_b[e][:, c * PACK * H : (c + 1) * PACK * H].rearrange("p (t m j) -> p m j t", t=PACK, j=PACK),
+                in_=w2_raw[e, c].rearrange("p j (m t) -> p m j t", t=PACK),
+            )
 
-        def second_product(e, dx):
-            bank = psum.tile([P, C], F32, tag="bank%d" % e, name="dxbank")
-            for n in (1, 0):
+        def quantize_w2(dst, e):
+            w2_q[e] = dst
+            quantize(dst, w2_b[e][:], E4M3X4)
+
+        def round_w13(copy, at, quarter, n):
+            w13_b[n] = room(at, [P, PACK * H], BF16, "w13_b", quarter)[:]
+            copy(
+                w13_b[n].rearrange("p (e k i j) -> p e k j i", e=E, i=4, j=PACK),
+                w13_raw[n].rearrange("p e j (k i) -> p e k j i", i=4),
+            )
+
+        def first_product(e, banks, by_bank=None):
+            steps = [(c, t) for c in range(PASSES) for t in range(PACK)]
+            if by_bank:
+                steps = [(c, t) for t in range(PACK) for c in by_bank]
+            first = steps[0][0]
+            for c, t in steps:
+                if c == first:
+                    dh_banks[e, t] = bank(banks[t], [P, C], "dh")
+                words, scales = part(w2_q[e], c * H + t * P, c * H + (t + 1) * P)
                 nc.tensor.matmul_mx(
-                    out=bank[:],
-                    lhsT=w13_q[0][:, (n * E + e) * K : (n * E + e + 1) * K].bitcast(E4M3X4),
-                    lhsT_scale=w13_q[1][:, (n * E + e) * K : (n * E + e + 1) * K],
-                    rhs=da_q[e, n][0].bitcast(E5M2X4),
-                    rhs_scale=da_q[e, n][1],
-                    start=(n == 1),
-                    stop=(n == 0),
+                    out=dh_banks[e, t][:],
+                    lhsT=words.bitcast(E4M3X4),
+                    lhsT_scale=scales,
+                    rhs=g_q[e, c][0].bitcast(E5M2X4),
+                    rhs_scale=g_q[e, c][1],
+                    start=(c == first),
+                    stop=(c != first),
                 )
-            nc.scalar.copy(out=dx, in_=bank[:])
+
+        def mask(at, e, lo=0, hi=PACK):
+            if lo == 0:
+                masked[e] = room(at, [P, PACK, C], F32, "masked")
+            for t in range(lo, hi):
+                nc.vector.scalar_tensor_tensor(
+                    masked[e][:, t, :], a1_row[e, t], 0.0, dh_banks[e, t][:], op0=IS_GT, op1=MULT
+                )
+
+        def da3_from_banks(e, lo, hi):
+            for t in range(lo, hi):
+                nc.vector.scalar_tensor_tensor(
+                    rows[e, 1][:, t, :], a1_row[e, t], 0.0, dh_banks[e, t][:], op0=MAX, op1=MULT
+                )
+
+        def flat(x):
+            return x.rearrange("p t s -> p (t s)")
+
+        def from_masked(e, n, lo, hi, first=0, last=C):
+            factor = (a3_raw, a1_raw)[n][e]
+            nc.gpsimd.tensor_tensor(
+                rows[e, n][:, lo:hi, first:last], factor[:, lo:hi, first:last], masked[e][:, lo:hi, first:last], MULT
+            )
+
+        def new_rows(at, e, quarter=0):
+            for n in range(2):
+                rows[e, n] = room(at, [P, PACK, C], BF16, "rows", quarter + 2 * n)[:]
+
+        def weave_da(e, n, first=0, last=C):
+            weave(da_b[e, n][:, first * PACK : last * PACK], rows[e, n][:, :, first:last])
+
+        def new_da(at, e):
+            da_b[e] = room(at, [P, 2 * PACK * C], BF16, "da_b")[:]
+            for n in range(2):
+                da_b[e, n] = da_b[e][:, n * PACK * C : (n + 1) * PACK * C]
+
+        def new_da_half(at, quarter, e, n):
+            da_b[e, n] = room(at, [P, PACK * C], BF16, "da_half", quarter)[:]
+
+        def quantize_da(dst, e):
+            da_q[e] = dst
+            if e in da_b:
+                quantize(dst, da_b[e], E5M2X4)
+            else:
+                for n in (1, 0):
+                    quantize(part(dst, n * C, (n + 1) * C), da_b[e, n], E5M2X4)
+
+        def second_product(e, b, dx):
+            acc = bank(b, [P, C], "dx")
+            for n in range(2):
+                words, scales = part(w13_q, (n * E + e) * K, (n * E + e + 1) * K)
+                moving = part(da_q[e], n * C, (n + 1) * C)
+                nc.tensor.matmul_mx(
+                    out=acc[:],
+                    lhsT=words.bitcast(E4M3X4),
+                    lhsT_scale=scales,
+                    rhs=moving[0].bitcast(E5M2X4),
+                    rhs_scale=moving[1],
+                    start=(n == 0),
+                    stop=(n == 1),
+                )
+            nc.scalar.copy(out=dx, in_=acc[:])
 
         def scatter(first, count, dx):
-            nc.vector.tensor_copy(result[:].indirect(offsets[:, first * C // 16 : (first + count) * C // 16]), dx[:])
+            nc.vector.tensor_copy(result[:].indirect(slots(first * C, (first + count) * C)), dx)
 
-        def new_planes(tag):
-            return turn(tag, [P, PACK, PAIR], F32, "planes")
+        def window(e, mask_tag, rows_tag):
+            mask(mask_tag, e)
+            new_rows(rows_tag, e)
+            da3_from_banks(e, 2, PACK)
+            from_masked(e, 1, 0, 1)
+            from_masked(e, 1, 1, 2)
+            from_masked(e, 0, 0, PACK)
 
-        rows = {}
-        masked = {}
-        da_b = {}
-        da_q = {}
-        planes = {(0, 0): new_planes("p0"), (1, 0): new_planes("p1")}
-        gather(0, 0, 0, planes[0, 0], (0, FIRST, PAIR))
-        gather(1, 0, 0, planes[1, 0])
-        load_w2("s0", 1, 1)
-        load_dy("s8", 1, 2)
-        load_dy("odd", 1, 3)
-        round_w2(0, 0)
-        gather(0, 0, 1, planes[0, 0])
-        gather(1, 0, 1, planes[1, 0])
-        round_w2(0, 1)
-        load_w2("s1", 2, 0)
-        gather(0, 0, 2, planes[0, 0])
-        gather(1, 0, 2, planes[1, 0])
-        load_w2("s3", 2, 1)
-        load_w2("s4", 3, 1)
-        load_w2("s2", 3, 0)
-        gather(0, 0, 3, planes[0, 0])
-        gather(1, 0, 3, planes[1, 0])
-        round_w2(1, 0)
-        prepare_g("s9", 0, 0, planes[0, 0])
-        load_saved("p0", a1_raw, a1_rows, 0, 2)
-        planes[0, 1] = new_planes("p2")
+        gate_runs = room(15, [P, 2, RUN], F32, "gate_runs")
+        load(gate_runs[:], gate[0:1, :].rearrange("o (r p j) -> p (o r) j", r=2, j=RUN))
+        offsets = held.tile([P, E * C // 16], U16, name="offsets")
+        nc.sync.dma_start(offsets[:], offs)
+        load_dy(0, 0, 0)
+        load_dy(2, 0, 1)
+        load_w2(1, 0, 0)
+        load_w2(3, 0, 1)
+        load_dy(8, 0, 2)
+        load_w2(6, 1, 0)
+        load_dy(5, 0, 3)
+        load_w2(7, 1, 1)
+        load_dy(4, 1, 0)
+
+        ident = small([P, P], F32, "ident")
+        make_identity(nc, ident[:])
+        gates[0] = room(24, [P, PAIR], F32, "gates")[:]
+        gates[1] = room(24, [P, PAIR], F32, "gates", 2)[:]
+        gate_cols = small([P, 2, BLOCKS], F32, "gate_cols")
+        spread_gates(0, 0)
+        spread_gates(1, 2)
+        for e in range(2, E):
+            turn_gates(e)
+
+        planes = [room(9, [P, PACK, PAIR], F32, "planes"), room(11, [P, PACK, PAIR], F32, "planes")]
         for t in range(PACK):
-            gather(0, 1, t, planes[0, 1])
-        round_w2(1, 1)
-        prepare_g("s0", 1, 0, planes[1, 0])
-        round_w2(2, 0)
-        prepare_g("s1", 0, 1, planes[0, 1])
-        load_saved("p2", a1_raw, a1_rows, 2, 1)
-        round_w2(2, 1)
-        quantize_w2(0)
-        quantize_g(0, 0)
-        load_saved("s9", a3_raw, a3_rows, 0, 1)
-        quantize_g(1, 0)
-        load_saved("s0", a3_raw, a3_rows, 1, 1)
-        load_saved("s3", a1_raw, a1_rows, 3, 1)
-        round_w2(3, 1)
-        round_w2(3, 0)
-        quantize_g(0, 1)
-        first_product(0)
-        quantize_w2(1, "s1")
-        first_product(1)
-        planes[1, 1] = new_planes("p1")
-        for t in range(PACK):
-            gather(1, 1, t, planes[1, 1])
-        prepare_g("s2", 1, 1, planes[1, 1])
-        load_w13("s6", 0)
-        load_w13("s8", 1)
+            for pair in range(2):
+                gather(planes[pair][:, t, :], 0, t, 2 * pair, 2)
+        for e in range(2):
+            for c in range(PASSES):
+                round_w2(15 + e, e, c)
+        load_w2(0, 2, 0)
+        for t in range(1, PACK):
+            load_dy(t, 1, t)
+        load_a1_apart(8, 0)
+        load_w2(5, 2, 1)
+        quantize_w2(codes(25, 0, PAIR, "w2_q0"), 0)
 
-        read_banks(0, "even", "s5", FIRST_CUTS)
-        load_saved("s1", a3_raw, a3_rows, 2, 1)
-        read_banks(1, "odd", "s7", SECOND_CUTS)
-        load_saved("p0", a3_raw, a3_rows, 3, 1)
-        quantize_w2(2, "s9")
-        last_row(1)
-        weave(0, "p1")
-        quantize_da(0)
-        quantize_g(1, 1, "p1")
-        first_product(2)
-        quantize_w2(3, "s2")
-        first_product(3)
-        weave(1, "s4")
-        round_w13(0)
-        round_w13(1)
-        read_banks(2, "even", "rows2", FIRST_CUTS)
-        read_banks(3, "odd", "rows3", SECOND_CUTS)
-        w13_q = quantize_w13("p2")
-        dx01 = turn("dx0", [P, PAIR], F32, "dx01")
-        second_product(0, dx01[:, 0:C])
-        weave(2, "s0")
-        weave(3, "rows2", (1,))
-        quantize_da(1)
-        second_product(1, dx01[:, C:])
-        last_row(3)
-        result = turn("s4", [P, T], F32, "result")
-        quantize_da(2)
-        weave(3, "s0", (0,))
-        quantize_da(3, (1,))
-        scatter(0, 2, dx01)
-        quantize_da(3, (0,))
-        dx2 = turn("rows3", [P, C], F32, "dx2")
-        second_product(2, dx2[:])
-        dx3 = turn("s5", [P, C], F32, "dx3")
-        second_product(3, dx3[:])
-        scatter(2, 1, dx2)
-        scatter(3, 1, dx3)
+        first_pass = room(6, [P, E, PACK * C], BF16, "first_pass")
+        for e in range(E):
+            weave(first_pass[:, e, :], planes[e // 2][:, :, e % 2 * C : (e % 2 + 1) * C])
+        round_w2(17, 2, 0)
+        load_w2(10, 3, 0)
+        load_w2(9, 3, 1)
+        load_saved(11, a3_raw, a3_rows, 0)
+        load_a1_apart(12, 1)
+        load_w13(0, 0)
+        g_a = codes(25, 2, PAIR, "g_a")
+        g_q[0, 0], g_q[1, 0] = part(g_a, 0, C), part(g_a, C, PAIR)
+        for e in range(2):
+            quantize(g_q[e, 0], first_pass[:, e, :], E5M2X4)
+
+        own = room(13, [P, PACK, PAIR], F32, "own")
+        for t in range(PACK - 1):
+            gather(own[:, t, :], 1, t, 0, 2)
+        for e in range(2):
+            gather(own[:, PACK - 1, e * C : (e + 1) * C], 1, PACK - 1, e, 1)
+        gb01 = room(26, [P, PACK * C], BF16, "gb01")
+        weave(gb01[:], own[:, :, 0:C])
+        gb11 = room(22, [P, PACK * C], BF16, "gb11", 3)
+        weave(gb11[:], own[:, :, C:])
+        round_w2(17, 2, 1)
+        quantize_w2(codes(24, 0, PAIR, "w2_q1"), 1)
+        load_saved(16, a3_raw, a3_rows, 1)
+        g_q[0, 1] = codes(24, 2, C, "g01")
+        quantize(g_q[0, 1], gb01[:], E5M2X4)
+        first_product(0, (0, 1, 2, 3))
+        g_b = codes(26, 0, PAIR, "g_b")
+        g_q[2, 0], g_q[3, 0] = part(g_b, 0, C), part(g_b, C, PAIR)
+        quantize(g_b, flat(first_pass[:, 2:E, :]), E5M2X4)
+        g_q[1, 1] = codes(24, 3, C, "g11")
+        quantize(g_q[1, 1], gb11[:], E5M2X4)
+        load_a1(13, 2)
+        load_saved(14, a3_raw, a3_rows, 2)
+        load_a1_last(6, 3)
+        load_saved(5, a3_raw, a3_rows, 3)
+        load_w13(7, 1)
+
+        window(0, 23, 22)
+        first_product(1, (0, 1, 2, 3), (1, 0))
+        round_w2(19, 3, 0)
+        round_w2(19, 3, 1)
+        new_da_half(9, 0, 0, 1)
+        weave_da(0, 1)
+        pick_and_turn(8, 2, 0, ((22, 2), (22, 2.5)))
+        pick_and_turn(8, 2, 1, ((21, 0), (21, 1)))
+        turn_back(2)
+        gb21 = join(25, 0, 2)
+        new_da_half(21, 1, 0, 0)
+        weave_da(0, 0)
+
+        window(1, 20, 18)
+        pick_and_turn(12, 3, 0, ((26, 2), (26, 3)))
+        pick_and_turn(12, 3, 1, ((11, 0), (9, 3.75)))
+        turn_back(3)
+        gb31 = join(24, 2, 3)
+        quantize_w2(codes(20, 0, PAIR, "w2_q3"), 3)
+        quantize_da(codes(16, 0, PAIR, "da_q0"), 0)
+        g_q[2, 1] = codes(20, 2, C, "g21")
+        quantize(g_q[2, 1], gb21[:], E5M2X4)
+        quantize_w2(codes(10, 0, PAIR, "w2_q2", (20, 3)), 2)
+        first_product(2, (0, 1, 2, 3), (0, 1))
+        g_q[3, 1] = codes(16, 2, C, "g31")
+        quantize(g_q[3, 1], gb31[:], E5M2X4)
+        first_product(3, (4, 5, 6, 7), (1, 0))
+        round_w13(nc.vector.tensor_copy, 17, 0, 0)
+        new_da(9, 1)
+        weave_da(1, 1)
+        weave_da(1, 0)
+        round_w13(nc.scalar.copy, 17, 2, 1)
+
+        new_rows(23, 2)
+        for t in range(PACK):
+            mask(24, 2, t, t + 1)
+            da3_from_banks(2, t, t + 1)
+        from_masked(2, 0, 0, 1)
+        from_masked(2, 0, 1, 2)
+        from_masked(2, 0, 2, PACK)
+        mask(12, 3)
+        new_da_half(7, 2, 2, 1)
+        weave_da(2, 1)
+        new_da_half(23, 2, 2, 0)
+        weave_da(2, 0)
+        w13_q = codes(14, 0, PAIR, "w13_q")
+        for n in range(2):
+            quantize(part(w13_q, n * E * K, (n + 1) * E * K), w13_b[n], E4M3X4)
+        dx01 = room(22, [P, PAIR], F32, "dx01", 3)
+        second_product(0, 0, dx01[:, 0:C])
+        quantize_da(codes(14, 2, PAIR, "da_q1"), 1)
+        second_product(1, 1, dx01[:, C:])
+        quantize_da(codes(24, 2, PAIR, "da_q2"), 2)
+        new_rows(23, 3, 1)
+        new_da(2, 3)
+        da3_from_banks(3, 1, PACK)
+        from_masked(3, 1, 0, 1)
+        weave_da(3, 1)
+        for half in range(2):
+            from_masked(3, 0, 0, PACK, half * C // 2, (half + 1) * C // 2)
+            weave_da(3, 0, half * C // 2, (half + 1) * C // 2)
+        result = room(6, [P, T], F32, "result", 2)
+        scatter(0, 2, dx01[:])
+        quantize_da(codes(1, 0, PAIR, "da_q3"), 3)
+        dx = room(23, [P, C], F32, "dx", 1)
+        second_product(2, 2, dx[:])
+        scatter(2, 1, dx[:])
+        dx = room(3, [P, C], F32, "dx")
+        second_product(3, 3, dx[:])
+        scatter(3, 1, dx[:])
         nc.sync.dma_start(out[:, 0:PAIR], result[:, 0:PAIR])
         nc.scalar.dma_start(out[:, PAIR:T], result[:, PAIR:T])

@@ -107,10 +107,10 @@ def tile_moe_bdx_glu_relu_kernel(tc, dyT, a1, a3, w2, w1, w3, gate, offs, out):
             nc.vector.quantize_mx(out=dst[0].bitcast(dtype), scales=dst[1], in_=src)
 
         def woven(x):
-            return x.rearrange("p (s i t) -> p s t i", i=4, t=PACK)
+            return x.rearrange("p (s i u k) -> p s u i k", i=4, u=2, k=2)
 
         def planes_of(x):
-            return x.rearrange("p t (s i) -> p s t i", i=4)
+            return x.rearrange("p (u k) (s i) -> p s u i k", i=4, k=2)
 
         def slots(lo, hi):
             return offsets[:, lo // 16 : hi // 16]
@@ -181,8 +181,8 @@ def tile_moe_bdx_glu_relu_kernel(tc, dyT, a1, a3, w2, w1, w3, gate, offs, out):
             if e not in w2_b:
                 w2_b[e] = room(tag, [P, PASSES * PACK * H], BF16, "w2_b")
             nc.scalar.copy(
-                out=w2_b[e][:, c * PACK * H : (c + 1) * PACK * H].rearrange("p (t m j) -> p m j t", t=PACK, j=PACK),
-                in_=w2_raw[e, c].rearrange("p j (m t) -> p m j t", t=PACK),
+                out=w2_b[e][:, c * PACK * H : (c + 1) * PACK * H].rearrange("p (t m u k) -> p m u t k", t=PACK, u=2, k=2),
+                in_=w2_raw[e, c].rearrange("p (u k) (m t) -> p m u t k", t=PACK, k=2),
             )
 
         def quantize_w2(dst, e):
@@ -397,7 +397,9 @@ def tile_moe_bdx_glu_relu_kernel(tc, dyT, a1, a3, w2, w1, w3, gate, offs, out):
         new_da(9, 1)
         weave_da(1, 1)
         weave_da(1, 0)
-        round_w13(nc.scalar.copy, 17, 2, 1)
+        w13_b[1] = room(17, [P, PACK * H], BF16, "w13_b", 2)[:]
+        for e in range(E):
+            weave(w13_b[1][:, e * H : (e + 1) * H], w13_raw[1][:, e, :, :])
 
         new_rows(23, 2)
         for t in range(PACK):

@@ -11,6 +11,7 @@ PAIR = 2 * C
 BLOCKS = C // P
 RUN = PAIR // P
 ROOM = 8192
+CUTS = (C + C // 4, 2 * C + C // 2)
 
 F32 = mybir.dt.float32
 BF16 = mybir.dt.bfloat16
@@ -54,7 +55,7 @@ def tile_moe_bdx_glu_relu_kernel(tc, dyT, a1, a3, w2, w1, w3, gate, offs, out):
         dy, w2_raw, w13_raw, a1_raw, a3_raw = {}, {}, {}, {}, {}
         w2_b, w2_q, g_q, gates = {}, {}, {}, {}
         dh_banks, masked, rows, da_b, da_q = {}, {}, {}, {}, {}
-        word_banks, a1_row, w13_b, pairs = {}, {}, {}, {}
+        word_banks, a1_row, w13_q, pairs, sums = {}, {}, {}, {}, {}
 
         def load(dst, src):
             nc.sync.dma_start(dst, src)
@@ -68,7 +69,9 @@ def tile_moe_bdx_glu_relu_kernel(tc, dyT, a1, a3, w2, w1, w3, gate, offs, out):
 
         def load_w13(at, n):
             src = (w1, w3)[n].rearrange("e (p j) k -> p e j k", j=PACK)
-            w13_raw[n] = load(room(at, [P, E, PACK, K], F32, "w13_raw")[:], src)
+            for pair in range(2):
+                dst = room(at, [P, 2, PACK, K], F32, "w13_raw", 2 * pair)
+                w13_raw[n, pair] = load(dst[:], src[:, 2 * pair : 2 * pair + 2, :, :])
 
         def load_saved(tag, saved, src, e):
             saved[e] = load(room(tag, [P, PACK, C], F32, "saved")[:], src[:, :, e * C : (e + 1) * C])
@@ -79,13 +82,6 @@ def tile_moe_bdx_glu_relu_kernel(tc, dyT, a1, a3, w2, w1, w3, gate, offs, out):
                 a1_row[e, t] = a1_raw[e][:, t, :]
             for t in range(2, PACK):
                 a1_row[e, t] = load(room(at, [P, C], F32, "a1_row", t)[:], a1_rows[:, t, e * C : (e + 1) * C])
-
-        def load_a1_last(at, e):
-            a1_raw[e] = load(room(at, [P, 1, C], F32, "a1_first")[:], a1_rows[:, 0:1, e * C : (e + 1) * C])
-            a1_row[e, 0] = a1_raw[e][:, 0, :]
-            middle = load(room(at, [P, 2, C], F32, "a1_middle", 2)[:], a1_rows[:, 1:3, e * C : (e + 1) * C])
-            a1_row[e, 1], a1_row[e, 2] = middle[:, 0, :], middle[:, 1, :]
-            a1_row[e, 3] = load(room(at, [P, C], F32, "a1_row", 1)[:], a1_rows[:, 3, e * C : (e + 1) * C])
 
         def load_a1(at, e):
             load_saved(at, a1_raw, a1_rows, e)
@@ -189,12 +185,19 @@ def tile_moe_bdx_glu_relu_kernel(tc, dyT, a1, a3, w2, w1, w3, gate, offs, out):
             w2_q[e] = dst
             quantize(dst, w2_b[e][:], E4M3X4)
 
-        def round_w13(copy, at, quarter, n):
-            w13_b[n] = room(at, [P, PACK * H], BF16, "w13_b", quarter)[:]
-            copy(
-                w13_b[n].rearrange("p (e k i j) -> p e k j i", e=E, i=4, j=PACK),
-                w13_raw[n].rearrange("p e j (k i) -> p e k j i", i=4),
-            )
+        def round_w13(at, quarter, pair, which):
+            rounded = room(at, [P, len(which), 2, H], BF16, "w13_b%d" % len(which), quarter)
+            for place, n in enumerate(which):
+                for e in range(2):
+                    weave(rounded[:, place, e, :], w13_raw[n, pair][:, e, :, :])
+            return rounded[:].rearrange("p n e x -> p (n e x)")
+
+        def quantize_w13(at, quarter, pair, which, rounded):
+            dst = codes(at, quarter, len(which) * 2 * K, "w13_q%d%d" % (pair, which[0]))
+            quantize(dst, rounded, E4M3X4)
+            for place, n in enumerate(which):
+                for e in range(2):
+                    w13_q[2 * pair + e, n] = part(dst, (2 * place + e) * K, (2 * place + e + 1) * K)
 
         def first_product(e, banks, by_bank=None):
             steps = [(c, t) for c in range(PASSES) for t in range(PACK)]
@@ -232,61 +235,60 @@ def tile_moe_bdx_glu_relu_kernel(tc, dyT, a1, a3, w2, w1, w3, gate, offs, out):
         def flat(x):
             return x.rearrange("p t s -> p (t s)")
 
-        def from_masked(e, n, lo, hi, first=0, last=C):
+        def from_masked(e, n, lo, hi):
+            factor = (a3_raw, a1_raw)[n][e]
+            nc.gpsimd.tensor_tensor(rows[e, n][:, lo:hi, :], factor[:, lo:hi, :], masked[e][:, lo:hi, :], MULT)
+
+        def woven_from_masked(at, quarter, e, n):
+            da_b[e, n] = room(at, [P, PACK * C], BF16, "da_b", quarter)[:]
             factor = (a3_raw, a1_raw)[n][e]
             nc.gpsimd.tensor_tensor(
-                rows[e, n][:, lo:hi, first:last], factor[:, lo:hi, first:last], masked[e][:, lo:hi, first:last], MULT
+                da_b[e, n].rearrange("p (s i t) -> p s t i", i=4, t=PACK),
+                factor.rearrange("p t (s i) -> p s t i", i=4),
+                masked[e][:].rearrange("p t (s i) -> p s t i", i=4),
+                MULT,
             )
 
-        def new_rows(at, e, quarter=0):
-            for n in range(2):
-                rows[e, n] = room(at, [P, PACK, C], BF16, "rows", quarter + 2 * n)[:]
+        def new_rows(at, quarter, e, n):
+            rows[e, n] = room(at, [P, PACK, C], BF16, "rows", quarter)[:]
 
-        def weave_da(e, n, first=0, last=C):
-            weave(da_b[e, n][:, first * PACK : last * PACK], rows[e, n][:, :, first:last])
+        def weave_da(at, quarter, e, n):
+            da_b[e, n] = room(at, [P, PACK * C], BF16, "da_b", quarter)[:]
+            weave(da_b[e, n], rows[e, n])
 
-        def new_da(at, e):
-            da_b[e] = room(at, [P, 2 * PACK * C], BF16, "da_b")[:]
-            for n in range(2):
-                da_b[e, n] = da_b[e][:, n * PACK * C : (n + 1) * PACK * C]
+        def quantize_da(at, quarter, e, n):
+            da_q[e, n] = codes(at, quarter, C, "da_q%d%d" % (e, n))
+            quantize(da_q[e, n], da_b[e, n], E5M2X4)
 
-        def new_da_half(at, quarter, e, n):
-            da_b[e, n] = room(at, [P, PACK * C], BF16, "da_half", quarter)[:]
-
-        def quantize_da(dst, e):
-            da_q[e] = dst
-            if e in da_b:
-                quantize(dst, da_b[e], E5M2X4)
-            else:
-                for n in (1, 0):
-                    quantize(part(dst, n * C, (n + 1) * C), da_b[e, n], E5M2X4)
-
-        def second_product(e, b, dx):
+        def second_product(e, b, order):
             acc = bank(b, [P, C], "dx")
-            for n in range(2):
-                words, scales = part(w13_q, (n * E + e) * K, (n * E + e + 1) * K)
-                moving = part(da_q[e], n * C, (n + 1) * C)
+            for n in order:
+                words, scales = w13_q[e, n]
                 nc.tensor.matmul_mx(
                     out=acc[:],
                     lhsT=words.bitcast(E4M3X4),
                     lhsT_scale=scales,
-                    rhs=moving[0].bitcast(E5M2X4),
-                    rhs_scale=moving[1],
-                    start=(n == 0),
-                    stop=(n == 1),
+                    rhs=da_q[e, n][0].bitcast(E5M2X4),
+                    rhs_scale=da_q[e, n][1],
+                    start=(n == order[0]),
+                    stop=(n == order[1]),
                 )
-            nc.scalar.copy(out=dx, in_=acc[:])
+            sums[e] = acc
 
-        def scatter(first, count, dx):
-            nc.vector.tensor_copy(result[:].indirect(slots(first * C, (first + count) * C)), dx)
+        def put_back(at, quarter, lo, hi):
+            dx = room(at, [P, hi - lo], F32, "dx%d" % (hi - lo), quarter)
+            for e in range(lo // C, (hi - 1) // C + 1):
+                first, last = max(lo, e * C), min(hi, (e + 1) * C)
+                nc.scalar.copy(out=dx[:, first - lo : last - lo], in_=sums[e][:, first - e * C : last - e * C])
+            nc.vector.tensor_copy(result[:].indirect(slots(lo, hi)), dx[:])
 
-        def window(e, mask_tag, rows_tag):
-            mask(mask_tag, e)
-            new_rows(rows_tag, e)
+        def window(e, mask_at, rows_at):
+            mask(mask_at, e)
+            new_rows(rows_at, 2, e, 1)
             da3_from_banks(e, 2, PACK)
             from_masked(e, 1, 0, 1)
             from_masked(e, 1, 1, 2)
-            from_masked(e, 0, 0, PACK)
+            woven_from_masked(rows_at, 0, e, 0)
 
         gate_runs = room(15, [P, 2, RUN], F32, "gate_runs")
         load(gate_runs[:], gate[0:1, :].rearrange("o (r p j) -> p (o r) j", r=2, j=RUN))
@@ -360,83 +362,73 @@ def tile_moe_bdx_glu_relu_kernel(tc, dyT, a1, a3, w2, w1, w3, gate, offs, out):
         quantize(g_b, flat(first_pass[:, 2:E, :]), E5M2X4)
         g_q[1, 1] = codes(24, 3, C, "g11")
         quantize(g_q[1, 1], gb11[:], E5M2X4)
-        load_a1(13, 2)
-        load_saved(14, a3_raw, a3_rows, 2)
-        load_a1_last(6, 3)
-        load_saved(5, a3_raw, a3_rows, 3)
         load_w13(7, 1)
+        load_a1_apart(13, 2)
+        load_saved(14, a3_raw, a3_rows, 2)
+        load_a1(6, 3)
+        load_saved(5, a3_raw, a3_rows, 3)
 
         window(0, 23, 22)
         first_product(1, (0, 1, 2, 3), (1, 0))
         round_w2(19, 3, 0)
         round_w2(19, 3, 1)
-        new_da_half(9, 0, 0, 1)
-        weave_da(0, 1)
+        weave_da(9, 0, 0, 1)
         pick_and_turn(8, 2, 0, ((22, 2), (22, 2.5)))
         pick_and_turn(8, 2, 1, ((21, 0), (21, 1)))
         turn_back(2)
         gb21 = join(25, 0, 2)
-        new_da_half(21, 1, 0, 0)
-        weave_da(0, 0)
 
         window(1, 20, 18)
-        pick_and_turn(12, 3, 0, ((26, 2), (26, 3)))
-        pick_and_turn(12, 3, 1, ((11, 0), (9, 3.75)))
+        weave_da(21, 1, 1, 1)
+        pick_and_turn(12, 3, 0, ((18, 2), (18, 2.5)))
+        pick_and_turn(12, 3, 1, ((11, 0), (23, 3.75)))
         turn_back(3)
         gb31 = join(24, 2, 3)
-        quantize_w2(codes(20, 0, PAIR, "w2_q3"), 3)
-        quantize_da(codes(16, 0, PAIR, "da_q0"), 0)
-        g_q[2, 1] = codes(20, 2, C, "g21")
+        w1_first = round_w13(18, 3, 0, (0,))
+        w3_first = round_w13(24, 0, 0, (1,))
+        quantize_w2(codes(20, 0, PAIR, "w2_q2"), 2)
+        quantize_w2(codes(20, 2, PAIR, "w2_q3"), 3)
+        quantize_da(16, 0, 0, 1)
+        quantize_da(16, 1, 0, 0)
+        g_q[2, 1] = codes(16, 2, C, "g21", (23, 3.75))
         quantize(g_q[2, 1], gb21[:], E5M2X4)
-        quantize_w2(codes(10, 0, PAIR, "w2_q2", (20, 3)), 2)
-        first_product(2, (0, 1, 2, 3), (0, 1))
-        g_q[3, 1] = codes(16, 2, C, "g31")
+        first_product(2, (0, 1, 2, 3), (1, 0))
+        w13_second = round_w13(25, 0, 1, (0, 1))
+        quantize_da(16, 3, 1, 1)
+        g_q[3, 1] = codes(22, 0, C, "g31")
         quantize(g_q[3, 1], gb31[:], E5M2X4)
         first_product(3, (4, 5, 6, 7), (1, 0))
-        round_w13(nc.vector.tensor_copy, 17, 0, 0)
-        new_da(9, 1)
-        weave_da(1, 1)
-        weave_da(1, 0)
-        w13_b[1] = room(17, [P, PACK * H], BF16, "w13_b", 2)[:]
-        for e in range(E):
-            weave(w13_b[1][:, e * H : (e + 1) * H], w13_raw[1][:, e, :, :])
+        quantize_w13(21, 1, 0, (0,), w1_first)
+        quantize_w13(21, 2, 0, (1,), w3_first)
+        quantize_da(7, 0, 1, 0)
 
-        new_rows(23, 2)
-        for t in range(PACK):
-            mask(24, 2, t, t + 1)
-            da3_from_banks(2, t, t + 1)
+        mask(24, 2)
+        new_rows(22, 2, 2, 0)
+        new_rows(18, 0, 2, 1)
+        da3_from_banks(2, 0, 1)
+        mask(19, 3)
+        da3_from_banks(2, 1, PACK)
         from_masked(2, 0, 0, 1)
         from_masked(2, 0, 1, 2)
         from_masked(2, 0, 2, PACK)
-        mask(12, 3)
-        new_da_half(7, 2, 2, 1)
-        weave_da(2, 1)
-        new_da_half(23, 2, 2, 0)
-        weave_da(2, 0)
-        w13_q = codes(14, 0, PAIR, "w13_q")
-        for n in range(2):
-            quantize(part(w13_q, n * E * K, (n + 1) * E * K), w13_b[n], E4M3X4)
-        dx01 = room(22, [P, PAIR], F32, "dx01", 3)
-        second_product(0, 0, dx01[:, 0:C])
-        quantize_da(codes(14, 2, PAIR, "da_q1"), 1)
-        second_product(1, 1, dx01[:, C:])
-        quantize_da(codes(24, 2, PAIR, "da_q2"), 2)
-        new_rows(23, 3, 1)
-        new_da(2, 3)
-        da3_from_banks(3, 1, PACK)
-        from_masked(3, 1, 0, 1)
-        weave_da(3, 1)
-        for half in range(2):
-            from_masked(3, 0, 0, PACK, half * C // 2, (half + 1) * C // 2)
-            weave_da(3, 0, half * C // 2, (half + 1) * C // 2)
-        result = room(6, [P, T], F32, "result", 2)
-        scatter(0, 2, dx01[:])
-        quantize_da(codes(1, 0, PAIR, "da_q3"), 3)
-        dx = room(23, [P, C], F32, "dx", 1)
-        second_product(2, 2, dx[:])
-        scatter(2, 1, dx[:])
-        dx = room(3, [P, C], F32, "dx")
-        second_product(3, 3, dx[:])
-        scatter(3, 1, dx[:])
+        woven_from_masked(10, 0, 3, 1)
+        result = room(12, [P, T], F32, "result", 3)
+        second_product(0, 0, (0, 1))
+        second_product(1, 4, (0, 1))
+        put_back(8, 0, 0, CUTS[0])
+        weave_da(15, 0, 2, 0)
+        weave_da(22, 2, 2, 1)
+        quantize_w13(6, 0, 1, (0, 1), w13_second)
+        quantize_da(1, 0, 3, 1)
+        quantize_da(6, 1, 2, 0)
+        quantize_da(6, 2, 2, 1)
+        woven_from_masked(15, 0, 3, 0)
+        put_back(25, 0, CUTS[0], PAIR)
+        second_product(2, 2, (0, 1))
+        put_back(8, 2, PAIR, CUTS[1])
+        quantize_da(1, 1, 3, 0)
+        put_back(19, 0, CUTS[1], 3 * C)
+        second_product(3, 3, (1, 0))
+        put_back(2, 0, 3 * C, E * C)
         nc.sync.dma_start(out[:, 0:PAIR], result[:, 0:PAIR])
         nc.scalar.dma_start(out[:, PAIR:T], result[:, PAIR:T])

@@ -192,8 +192,8 @@ def tile_moe_bdx_glu_relu_kernel(tc, dyT, a1, a3, w2, w1, w3, gate, offs, out):
                     weave(rounded[:, place, e, :], w13_raw[n, pair][:, e, :, :])
             return rounded[:].rearrange("p n e x -> p (n e x)")
 
-        def quantize_w13(at, quarter, pair, which, rounded):
-            dst = codes(at, quarter, len(which) * 2 * K, "w13_q%d%d" % (pair, which[0]))
+        def quantize_w13(at, quarter, pair, which, rounded, scales_at=None):
+            dst = codes(at, quarter, len(which) * 2 * K, "w13_q%d%d" % (pair, which[0]), scales_at)
             quantize(dst, rounded, E4M3X4)
             for place, n in enumerate(which):
                 for e in range(2):
@@ -256,8 +256,8 @@ def tile_moe_bdx_glu_relu_kernel(tc, dyT, a1, a3, w2, w1, w3, gate, offs, out):
             da_b[e, n] = room(at, [P, PACK * C], BF16, "da_b", quarter)[:]
             weave(da_b[e, n], rows[e, n])
 
-        def quantize_da(at, quarter, e, n):
-            da_q[e, n] = codes(at, quarter, C, "da_q%d%d" % (e, n))
+        def quantize_da(at, quarter, e, n, scales_at=None):
+            da_q[e, n] = codes(at, quarter, C, "da_q%d%d" % (e, n), scales_at)
             quantize(da_q[e, n], da_b[e, n], E5M2X4)
 
         def second_product(e, b, order):
@@ -306,7 +306,7 @@ def tile_moe_bdx_glu_relu_kernel(tc, dyT, a1, a3, w2, w1, w3, gate, offs, out):
 
         ident = small([P, P], F32, "ident")
         make_identity(nc, ident[:])
-        gates[0] = room(24, [P, PAIR], F32, "gates")[:]
+        gates[0] = room(26, [P, PAIR], F32, "gates", 2)[:]
         gates[1] = room(24, [P, PAIR], F32, "gates", 2)[:]
         gate_cols = small([P, 2, BLOCKS], F32, "gate_cols")
         spread_gates(0, 0)
@@ -337,10 +337,8 @@ def tile_moe_bdx_glu_relu_kernel(tc, dyT, a1, a3, w2, w1, w3, gate, offs, out):
         load_saved(11, a3_raw, a3_rows, 0)
         load_a1_apart(12, 1)
         load_w13(0, 0)
-        g_a = codes(25, 2, PAIR, "g_a")
-        g_q[0, 0], g_q[1, 0] = part(g_a, 0, C), part(g_a, C, PAIR)
-        for e in range(2):
-            quantize(g_q[e, 0], first_pass[:, e, :], E5M2X4)
+        g_q[0, 0] = codes(25, 2, C, "g00")
+        quantize(g_q[0, 0], first_pass[:, 0, :], E5M2X4)
 
         own = room(13, [P, PACK, PAIR], F32, "own")
         for t in range(PACK - 1):
@@ -352,14 +350,16 @@ def tile_moe_bdx_glu_relu_kernel(tc, dyT, a1, a3, w2, w1, w3, gate, offs, out):
         gb11 = room(22, [P, PACK * C], BF16, "gb11", 3)
         weave(gb11[:], own[:, :, C:])
         round_w2(17, 2, 1)
-        quantize_w2(codes(24, 0, PAIR, "w2_q1"), 1)
+        quantize_w2(codes(24, 0, PAIR, "w2_q1", (26, 2)), 1)
         load_saved(16, a3_raw, a3_rows, 1)
+        g_b = codes(15, 0, PAIR, "g_b", (26, 2.5))
+        g_q[2, 0], g_q[3, 0] = part(g_b, 0, C), part(g_b, C, PAIR)
+        quantize(g_b, flat(first_pass[:, 2:E, :]), E5M2X4)
         g_q[0, 1] = codes(24, 2, C, "g01")
         quantize(g_q[0, 1], gb01[:], E5M2X4)
         first_product(0, (0, 1, 2, 3))
-        g_b = codes(26, 0, PAIR, "g_b")
-        g_q[2, 0], g_q[3, 0] = part(g_b, 0, C), part(g_b, C, PAIR)
-        quantize(g_b, flat(first_pass[:, 2:E, :]), E5M2X4)
+        g_q[1, 0] = codes(25, 3, C, "g10", (26, 3))
+        quantize(g_q[1, 0], first_pass[:, 1, :], E5M2X4)
         g_q[1, 1] = codes(24, 3, C, "g11")
         quantize(g_q[1, 1], gb11[:], E5M2X4)
         load_w13(7, 1)
@@ -414,16 +414,16 @@ def tile_moe_bdx_glu_relu_kernel(tc, dyT, a1, a3, w2, w1, w3, gate, offs, out):
         woven_from_masked(10, 0, 3, 1)
         result = room(12, [P, T], F32, "result", 3)
         second_product(0, 0, (0, 1))
-        second_product(1, 4, (0, 1))
+        second_product(1, 4, (1, 0))
         put_back(8, 0, 0, CUTS[0])
-        weave_da(15, 0, 2, 0)
-        weave_da(22, 2, 2, 1)
-        quantize_w13(6, 0, 1, (0, 1), w13_second)
-        quantize_da(1, 0, 3, 1)
+        weave_da(7, 0, 2, 0)
+        weave_da(22, 3, 2, 1)
         quantize_da(6, 1, 2, 0)
+        quantize_w13(6, 0, 1, (0, 1), w13_second, (22, 2))
+        quantize_da(1, 0, 3, 1, (22, 2.25))
         quantize_da(6, 2, 2, 1)
-        woven_from_masked(15, 0, 3, 0)
-        put_back(25, 0, CUTS[0], PAIR)
+        woven_from_masked(10, 0, 3, 0)
+        put_back(18, 0, CUTS[0], PAIR)
         second_product(2, 2, (0, 1))
         put_back(8, 2, PAIR, CUTS[1])
         quantize_da(1, 1, 3, 0)

@@ -9,9 +9,9 @@ PACK = 4
 PASSES = N // (P * PACK)
 PAIR = 2 * C
 BLOCKS = C // P
-RUN = PAIR // P
-ROOM = 8192
-CUTS = (C + C // 4, 2 * C + C // 2)
+LINE = 4
+HALF = C // 2
+KB = 1024
 
 F32 = mybir.dt.float32
 BF16 = mybir.dt.bfloat16
@@ -22,11 +22,24 @@ E4M3X4 = mybir.dt.float8_e4m3fn_x4
 E5M2X4 = mybir.dt.float8_e5m2_x4
 MULT = mybir.AluOpType.mult
 IS_GT = mybir.AluOpType.is_gt
-MAX = mybir.AluOpType.max
 COPY = mybir.ActivationFunctionType.Copy
 
 FLOPS = 2 * N * H * E * C + 2 * 2 * H * K * E * C
 BYTES = 4 * (N * T + 2 * H * E * C + E * N * H + 2 * E * H * K + E * C + K * T) + 2 * P * (E * C // 16)
+
+DY = [8 * i for i in range(8)]
+IDENT = 65
+PIECES_V = ((0, 0, PAIR, 66), (1, 0, C, 98), (1, C, C + HALF, 106))
+PIECES_S = ((0, PAIR, T, 82), (1, C + HALF, T, 110))
+FRESH = [130, 138, 146, 154]
+GATES = [162, 166]
+RESULT = 170
+MASKED = 178
+G_WORDS = 186
+G_SCALES = 202
+G_ROUND = [205, 209]
+W2_ROUND = [213, 221]
+W2_CODES = [229, 234]
 
 
 def tile_moe_bdx_glu_relu_kernel(tc, dyT, a1, a3, w2, w1, w3, gate, offs, out):
@@ -34,67 +47,42 @@ def tile_moe_bdx_glu_relu_kernel(tc, dyT, a1, a3, w2, w1, w3, gate, offs, out):
 
     dy_rows = dyT.rearrange("(c p t) w -> c t p w", c=PASSES, t=PACK)
     w2_rows = w2.rearrange("e (c p j) i -> e c p j i", c=PASSES, j=PACK)
-    a1_rows = a1.rearrange("(p t) s -> p t s", t=PACK)
-    a3_rows = a3.rearrange("(p t) s -> p t s", t=PACK)
+    saved_rows = [a.rearrange("(p t) s -> p t s", t=PACK) for a in (a1, a3)]
+    w13_rows = [w.rearrange("e (p j) k -> e p j k", j=PACK) for w in (w1, w3)]
 
     with ExitStack() as ctx:
         held = ctx.enter_context(tc.tile_pool(name="held", bufs=1))
         rooms = ctx.enter_context(tc.tile_pool(name="rooms", bufs=1))
         psum = ctx.enter_context(tc.psum_pool(name="psum", bufs=1))
 
-        def room(number, shape, dtype, name, quarter=0):
-            at = number * ROOM + int(quarter * (ROOM // 4))
-            return rooms.tile(shape, dtype, tag="%s_at%d" % (name, at), offset=at, align_bytes=64, name=name)
-
-        def small(shape, dtype, name):
-            return held.tile(shape, dtype, align_bytes=64, name=name)
+        def room(kib, shape, dtype, name):
+            at = int(kib * KB)
+            return rooms.tile(shape, dtype, tag="%s_at%d" % (name, at), offset=at, align_bytes=64, name=name)[:]
 
         def bank(b, shape, name):
-            return psum.tile(shape, F32, tag="bank%d" % b, name=name)
+            return psum.tile(shape, F32, tag="bank%d" % b, name=name)[:]
 
-        dy, w2_raw, w13_raw, a1_raw, a3_raw = {}, {}, {}, {}, {}
-        w2_b, w2_q, g_q, gates = {}, {}, {}, {}
-        dh_banks, masked, rows, da_b, da_q = {}, {}, {}, {}, {}
-        word_banks, a1_row, w13_q, pairs, sums = {}, {}, {}, {}, {}
+        dy, planes, gates, gate_bank = {}, {}, {}, {}
+        w2_raw, w2_b, w2_q, g_b, g_q = {}, {}, {}, {}, {}
+        saved, w13_raw, w13_b, w13_q = {}, {}, {}, {}
+        dh, masked, da_b, da_q = {}, {}, {}, {}
 
         def load(dst, src):
             nc.sync.dma_start(dst, src)
             return dst
 
-        def load_dy(tag, c, t):
-            dy[c, t] = load(room(tag, [P, T], F32, "dy")[:], dy_rows[c, t])
+        def load_w2(kib, e, c):
+            w2_raw[e, c] = load(room(kib, [P, PACK, H], F32, "w2_raw"), w2_rows[e, c])
 
-        def load_w2(tag, e, c):
-            w2_raw[e, c] = load(room(tag, [P, PACK, H], F32, "w2_raw")[:], w2_rows[e, c])
+        def load_saved(kib, n, e):
+            saved[n, e] = load(room(kib, [P, PACK, C], F32, "saved"), saved_rows[n][:, :, e * C : (e + 1) * C])
 
-        def load_w13(at, n):
-            src = (w1, w3)[n].rearrange("e (p j) k -> p e j k", j=PACK)
-            for pair in range(2):
-                dst = room(at, [P, 2, PACK, K], F32, "w13_raw", 2 * pair)
-                w13_raw[n, pair] = load(dst[:], src[:, 2 * pair : 2 * pair + 2, :, :])
+        def load_w13(kib, e):
+            for n in range(2):
+                w13_raw[e, n] = load(room(kib + 2 * n, [P, PACK, K], F32, "w13_raw"), w13_rows[n][e])
 
-        def load_saved(tag, saved, src, e):
-            saved[e] = load(room(tag, [P, PACK, C], F32, "saved")[:], src[:, :, e * C : (e + 1) * C])
-
-        def load_a1_apart(at, e):
-            a1_raw[e] = load(room(at, [P, 2, C], F32, "a1_low")[:], a1_rows[:, 0:2, e * C : (e + 1) * C])
-            for t in range(2):
-                a1_row[e, t] = a1_raw[e][:, t, :]
-            for t in range(2, PACK):
-                a1_row[e, t] = load(room(at, [P, C], F32, "a1_row", t)[:], a1_rows[:, t, e * C : (e + 1) * C])
-
-        def load_a1(at, e):
-            load_saved(at, a1_raw, a1_rows, e)
-            for t in range(PACK):
-                a1_row[e, t] = a1_raw[e][:, t, :]
-
-        def codes(at, quarter, width, name, scales_at=None):
-            words = room(at, [P, width], U32, name, quarter)
-            if scales_at:
-                scales = room(scales_at[0], [P, width], U8, name + "_s", scales_at[1])
-            else:
-                scales = small([P, width], U8, name + "_s")
-            return words[:], scales[:]
+        def codes(words_at, scales_at, width, name):
+            return room(words_at, [P, width], U32, name), room(scales_at, [P, width], U8, name + "_s")
 
         def part(pair, lo, hi):
             return pair[0][:, lo:hi], pair[1][:, lo:hi]
@@ -103,332 +91,238 @@ def tile_moe_bdx_glu_relu_kernel(tc, dyT, a1, a3, w2, w1, w3, gate, offs, out):
             nc.vector.quantize_mx(out=dst[0].bitcast(dtype), scales=dst[1], in_=src)
 
         def woven(x):
-            return x.rearrange("p (s i u k) -> p s u i k", i=4, u=2, k=2)
+            return x.rearrange("p (s i t) -> p s t i", i=LINE, t=PACK)
 
-        def planes_of(x):
-            return x.rearrange("p (u k) (s i) -> p s u i k", i=4, k=2)
+        def by_lines(x):
+            return x.rearrange("p t (s i) -> p s t i", i=LINE)
 
         def slots(lo, hi):
             return offsets[:, lo // 16 : hi // 16]
 
-        def spread_gates(pair, first_bank):
-            for half in range(RUN // 4):
-                spread = bank(first_bank + half, [P, 4, P], "spread")
-                for j in range(4):
-                    col = half * 4 + j
-                    nc.tensor.transpose(spread[:, j, :], gate_runs[:, pair, col : col + 1].to_broadcast([P, P]), ident[:])
-                nc.scalar.copy(
-                    out=gates[pair].rearrange("q (p h j) -> q p h j", h=RUN // 4, j=4)[:, :, half, :],
-                    in_=spread[:].rearrange("q j p -> q p j"),
+        def gathered(c, lo, hi):
+            for key, tile in planes.items():
+                if key[0] == c and key[1] <= lo and hi <= key[2]:
+                    return tile[:, :, lo - key[1] : hi - key[1]]
+
+        def unit(c, e):
+            return gathered(c, e * C, (e + 1) * C)
+
+        def over_rows(x):
+            return x.unsqueeze(2).to_broadcast([P, x.shape[1], PACK, LINE])
+
+        def spread_gates(e, b):
+            gate_bank[e] = bank(b, [P, LINE, P], "spread")
+            for i in range(LINE):
+                nc.tensor.transpose(gate_bank[e][:, i, :], gate_runs[:, e, i : i + 1].to_broadcast([P, P]), ident)
+
+        def gates_out(e):
+            lo = e % 2 * C
+            return gates[e // 2][:, lo : lo + C].rearrange("q (s i) -> q s i", i=LINE)
+
+        def gates_in(e):
+            return gate_bank[e].rearrange("q i s -> q s i")
+
+        def gate_on_vector(kib, e):
+            g_b[e, 1] = room(kib, [P, PACK * C], BF16, "g_b")
+            cuts = (0, HALF, C) if e == 1 else (0, C)
+            for lo, hi in zip(cuts, cuts[1:]):
+                nc.vector.tensor_tensor(
+                    woven(g_b[e, 1][:, lo * PACK : hi * PACK]),
+                    by_lines(gathered(1, e * C + lo, e * C + hi)),
+                    over_rows(gates_in(e)[:, lo // LINE : hi // LINE, :]),
+                    MULT,
                 )
 
-        def turn_gates(e):
-            cols = bank(2 + e, [P, BLOCKS, P], "cols")
-            for b in range(BLOCKS):
-                lo = e % 2 * C + b * P
-                nc.tensor.transpose(cols[:, b, :], gates[1][:, lo : lo + P], ident[:])
-            nc.scalar.copy(out=gate_cols[:, e - 2, :], in_=cols[:, :, 0])
+        def quantize_g(e, c):
+            place = 2 * e + c if e < 2 else e + 2
+            g_q[e, c] = codes(G_WORDS + 2 * place, G_SCALES + 0.5 * place, C, "g_q")
+            quantize(g_q[e, c], g_b[e, c], E5M2X4)
 
-        def gather(dst, c, t, first, count):
-            lo = first % 2 * C
-            nc.vector.tensor_tensor(
-                dst, dy[c, t].indirect(slots(first * C, (first + count) * C)), gates[first // 2][:, lo : lo + count * C], MULT
-            )
-
-        def weave(dst, src):
-            nc.scalar.copy(out=woven(dst), in_=planes_of(src))
-
-        def pick_and_turn(ring, e, u, places):
-            there = [bank(4 + 2 * (e % 2) + h, [P, 2, 2, P], "there") for h in range(2)]
-            for k in range(2):
-                picked = room(ring, [P, C], F32, "picked", 2 * (1 - u) + k)
-                nc.vector.tensor_copy(picked[:], dy[1, 2 * u + k].indirect(slots(e * C, (e + 1) * C)))
-                for b in range(BLOCKS):
-                    nc.tensor.transpose(there[b // 2][:, b % 2, k, :], picked[:, b * P : (b + 1) * P], ident[:])
-            for h, (at, quarter) in enumerate(places):
-                pairs[e, u, h] = room(at, [P, 2, 2 * P], BF16, "pairs", quarter)
-                for b in range(2):
-                    nc.scalar.activation(
-                        pairs[e, u, h][:, b, :].rearrange("s (q k) -> s q k", k=2),
-                        there[h][:, b, :, :].rearrange("s k q -> s q k"),
-                        COPY,
-                        scale=gate_cols[:, e - 2, 2 * h + b : 2 * h + b + 1],
-                    )
-
-        def turn_back(e):
-            word_banks[e] = [bank(6 - 2 * (e % 2) + h, [P, 2, 2 * P], "back") for h in range(2)]
-            for h in range(2):
-                for u in range(2):
-                    for b in range(2):
-                        nc.tensor.transpose(
-                            word_banks[e][h][:, u, b * P : (b + 1) * P], pairs[e, u, h][:, b, :].bitcast(F32), ident[:]
-                        )
-
-        def join(at, quarter, e):
-            gb = room(at, [P, PACK * C], BF16, "joined", quarter)
-            for h in range(2):
-                nc.scalar.copy(
-                    out=gb[:, h * 2 * C : (h + 1) * 2 * C].bitcast(F32).rearrange("p (s u) -> p s u", u=2),
-                    in_=word_banks[e][h][:].rearrange("p u s -> p s u"),
-                )
-            return gb
-
-        def round_w2(tag, e, c):
-            if e not in w2_b:
-                w2_b[e] = room(tag, [P, PASSES * PACK * H], BF16, "w2_b")
-            nc.scalar.copy(
+        def round_w2(e, c, copy=nc.scalar.copy):
+            if c == 0:
+                w2_b[e] = room(W2_ROUND[e % 2], [P, PASSES * PACK * H], BF16, "w2_b")
+            copy(
                 out=w2_b[e][:, c * PACK * H : (c + 1) * PACK * H].rearrange("p (t m u k) -> p m u t k", t=PACK, u=2, k=2),
                 in_=w2_raw[e, c].rearrange("p (u k) (m t) -> p m u t k", t=PACK, k=2),
             )
 
-        def quantize_w2(dst, e):
-            w2_q[e] = dst
-            quantize(dst, w2_b[e][:], E4M3X4)
-
-        def round_w13(at, quarter, pair, which):
-            rounded = room(at, [P, len(which), 2, H], BF16, "w13_b%d" % len(which), quarter)
-            for place, n in enumerate(which):
-                for e in range(2):
-                    weave(rounded[:, place, e, :], w13_raw[n, pair][:, e, :, :])
-            return rounded[:].rearrange("p n e x -> p (n e x)")
-
-        def quantize_w13(at, quarter, pair, which, rounded, scales_at=None):
-            dst = codes(at, quarter, len(which) * 2 * K, "w13_q%d%d" % (pair, which[0]), scales_at)
-            quantize(dst, rounded, E4M3X4)
-            for place, n in enumerate(which):
-                for e in range(2):
-                    w13_q[2 * pair + e, n] = part(dst, (2 * place + e) * K, (2 * place + e + 1) * K)
-
-        def first_product(e, banks, by_bank=None):
-            steps = [(c, t) for c in range(PASSES) for t in range(PACK)]
-            if by_bank:
-                steps = [(c, t) for t in range(PACK) for c in by_bank]
-            first = steps[0][0]
-            for c, t in steps:
-                if c == first:
-                    dh_banks[e, t] = bank(banks[t], [P, C], "dh")
-                words, scales = part(w2_q[e], c * H + t * P, c * H + (t + 1) * P)
-                nc.tensor.matmul_mx(
-                    out=dh_banks[e, t][:],
-                    lhsT=words.bitcast(E4M3X4),
-                    lhsT_scale=scales,
-                    rhs=g_q[e, c][0].bitcast(E5M2X4),
-                    rhs_scale=g_q[e, c][1],
-                    start=(c == first),
-                    stop=(c != first),
-                )
-
-        def mask(at, e, lo=0, hi=PACK):
+        def quantize_w2(e, lo, hi):
             if lo == 0:
-                masked[e] = room(at, [P, PACK, C], F32, "masked")
-            for t in range(lo, hi):
+                w2_q[e] = codes(W2_CODES[e % 2], W2_CODES[e % 2] + 4, PASSES * H, "w2_q")
+            quantize(part(w2_q[e], lo * H, hi * H), w2_b[e][:, lo * PACK * H : hi * PACK * H], E4M3X4)
+
+        def round_w13(e):
+            w13_b[e] = room((79, 163)[e % 2], [P, 2, PACK * K], BF16, "w13_b")
+            for n in range(2):
+                nc.scalar.copy(out=woven(w13_b[e][:, n, :]), in_=by_lines(w13_raw[e, n]))
+
+        def quantize_w13(e):
+            w13_q[e] = codes(81, 162, 2 * K, "w13_q")
+            quantize(w13_q[e], w13_b[e].rearrange("p n x -> p (n x)"), E4M3X4)
+
+        def first_product(e):
+            for b in range(BLOCKS):
+                dh[e, b] = bank(b, [P, PACK, P], "dh")
+                for t in range(PACK):
+                    for c in range(PASSES):
+                        words, scales = part(w2_q[e], c * H + t * P, c * H + (t + 1) * P)
+                        moving, moving_scales = part(g_q[e, c], b * P, (b + 1) * P)
+                        nc.tensor.matmul_mx(
+                            out=dh[e, b][:, t, :],
+                            lhsT=words.bitcast(E4M3X4),
+                            lhsT_scale=scales,
+                            rhs=moving.bitcast(E5M2X4),
+                            rhs_scale=moving_scales,
+                            start=(c == 0),
+                            stop=(c == PASSES - 1),
+                        )
+
+        def mask(e):
+            for b in range(BLOCKS):
+                masked[e, b] = room(MASKED + 2 * b, [P, PACK, P], F32, "masked")
                 nc.vector.scalar_tensor_tensor(
-                    masked[e][:, t, :], a1_row[e, t], 0.0, dh_banks[e, t][:], op0=IS_GT, op1=MULT
+                    masked[e, b], saved[0, e][:, :, b * P : (b + 1) * P], 0.0, dh[e, b], op0=IS_GT, op1=MULT
                 )
 
-        def da3_from_banks(e, lo, hi):
-            for t in range(lo, hi):
-                nc.vector.scalar_tensor_tensor(
-                    rows[e, 1][:, t, :], a1_row[e, t], 0.0, dh_banks[e, t][:], op0=MAX, op1=MULT
+        def derivative(engine, e, n, blocks):
+            if (e, n) not in da_b:
+                da_b[e, n] = room(70 - 4 * n, [P, PACK * C], BF16, "da_b")
+            for b in blocks:
+                engine.tensor_tensor(
+                    woven(da_b[e, n][:, b * PACK * P : (b + 1) * PACK * P]),
+                    by_lines(saved[1 - n, e][:, :, b * P : (b + 1) * P]),
+                    by_lines(masked[e, b]),
+                    MULT,
                 )
 
-        def flat(x):
-            return x.rearrange("p t s -> p (t s)")
+        def quantize_da(e, n, lo, hi):
+            if lo == 0:
+                da_q[e, n] = codes(74 + 2 * n, 78 + 0.5 * n, C, "da_q")
+            quantize(part(da_q[e, n], lo, hi), da_b[e, n][:, lo * PACK : hi * PACK], E5M2X4)
 
-        def from_masked(e, n, lo, hi):
-            factor = (a3_raw, a1_raw)[n][e]
-            nc.gpsimd.tensor_tensor(rows[e, n][:, lo:hi, :], factor[:, lo:hi, :], masked[e][:, lo:hi, :], MULT)
-
-        def woven_from_masked(at, quarter, e, n):
-            da_b[e, n] = room(at, [P, PACK * C], BF16, "da_b", quarter)[:]
-            factor = (a3_raw, a1_raw)[n][e]
-            nc.gpsimd.tensor_tensor(
-                da_b[e, n].rearrange("p (s i t) -> p s t i", i=4, t=PACK),
-                factor.rearrange("p t (s i) -> p s t i", i=4),
-                masked[e][:].rearrange("p t (s i) -> p s t i", i=4),
-                MULT,
-            )
-
-        def new_rows(at, quarter, e, n):
-            rows[e, n] = room(at, [P, PACK, C], BF16, "rows", quarter)[:]
-
-        def weave_da(at, quarter, e, n):
-            da_b[e, n] = room(at, [P, PACK * C], BF16, "da_b", quarter)[:]
-            weave(da_b[e, n], rows[e, n])
-
-        def quantize_da(at, quarter, e, n, scales_at=None):
-            da_q[e, n] = codes(at, quarter, C, "da_q%d%d" % (e, n), scales_at)
-            quantize(da_q[e, n], da_b[e, n], E5M2X4)
-
-        def second_product(e, b, order):
-            acc = bank(b, [P, C], "dx")
-            for n in order:
-                words, scales = w13_q[e, n]
+        def put_back(e, b, kib, lo, hi, copy):
+            sums = bank(b, [P, hi - lo], "dx")
+            for n in (1, 0):
+                words, scales = part(w13_q[e], n * K, (n + 1) * K)
+                moving, moving_scales = part(da_q[e, n], lo, hi)
                 nc.tensor.matmul_mx(
-                    out=acc[:],
+                    out=sums,
                     lhsT=words.bitcast(E4M3X4),
                     lhsT_scale=scales,
-                    rhs=da_q[e, n][0].bitcast(E5M2X4),
-                    rhs_scale=da_q[e, n][1],
-                    start=(n == order[0]),
-                    stop=(n == order[1]),
+                    rhs=moving.bitcast(E5M2X4),
+                    rhs_scale=moving_scales,
+                    start=(n == 1),
+                    stop=(n == 0),
                 )
-            sums[e] = acc
+            dx = room(kib, [P, hi - lo], F32, "dx")
+            copy(out=dx, in_=sums)
+            for at in range(lo, hi, HALF):
+                nc.scalar.activation(result.indirect(slots(e * C + at, e * C + at + HALF)), dx[:, at - lo : at - lo + HALF], COPY)
 
-        def put_back(at, quarter, lo, hi):
-            dx = room(at, [P, hi - lo], F32, "dx%d" % (hi - lo), quarter)
-            for e in range(lo // C, (hi - 1) // C + 1):
-                first, last = max(lo, e * C), min(hi, (e + 1) * C)
-                nc.scalar.copy(out=dx[:, first - lo : last - lo], in_=sums[e][:, first - e * C : last - e * C])
-            nc.vector.tensor_copy(result[:].indirect(slots(lo, hi)), dx[:])
-
-        def window(e, mask_at, rows_at):
-            mask(mask_at, e)
-            new_rows(rows_at, 2, e, 1)
-            da3_from_banks(e, 2, PACK)
-            from_masked(e, 1, 0, 1)
-            from_masked(e, 1, 1, 2)
-            woven_from_masked(rows_at, 0, e, 0)
-
-        gate_runs = room(15, [P, 2, RUN], F32, "gate_runs")
-        load(gate_runs[:], gate[0:1, :].rearrange("o (r p j) -> p (o r) j", r=2, j=RUN))
+        gate_runs = held.tile([P, E, LINE], F32, name="gate_runs")[:]
+        load(gate_runs, gate[0:1, :].rearrange("o (e p i) -> p (o e) i", e=E, i=LINE))
         offsets = held.tile([P, E * C // 16], U16, name="offsets")
         nc.sync.dma_start(offsets[:], offs)
-        load_dy(0, 0, 0)
-        load_dy(2, 0, 1)
-        load_w2(1, 0, 0)
-        load_w2(3, 0, 1)
-        load_dy(8, 0, 2)
-        load_w2(6, 1, 0)
-        load_dy(5, 0, 3)
-        load_w2(7, 1, 1)
-        load_dy(4, 1, 0)
+        for c in range(PASSES):
+            for t in range(PACK):
+                dy[c, t] = load(room(DY[c * PACK + t], [P, T], F32, "dy"), dy_rows[c, t])
+        load_w2(FRESH[0], 0, 0)
+        load_w2(FRESH[1], 0, 1)
+        load_w2(FRESH[2], 1, 0)
+        load_saved(FRESH[3], 0, 0)
 
-        ident = small([P, P], F32, "ident")
-        make_identity(nc, ident[:])
-        gates[0] = room(26, [P, PAIR], F32, "gates", 2)[:]
-        gates[1] = room(24, [P, PAIR], F32, "gates", 2)[:]
-        gate_cols = small([P, 2, BLOCKS], F32, "gate_cols")
-        spread_gates(0, 0)
-        spread_gates(1, 2)
-        for e in range(2, E):
-            turn_gates(e)
+        ident = room(IDENT, [P, P], F32, "ident")
+        make_identity(nc, ident)
+        for pair in range(2):
+            gates[pair] = room(GATES[pair], [P, PAIR], F32, "gates")
+        for e in range(2):
+            spread_gates(e, 4 + e)
+            spread_gates(e + 2, 6 + e)
+            nc.vector.tensor_copy(gates_out(e), gates_in(e))
+            nc.scalar.copy(out=gates_out(e + 2), in_=gates_in(e + 2))
 
-        planes = [room(9, [P, PACK, PAIR], F32, "planes"), room(11, [P, PACK, PAIR], F32, "planes")]
+        for c, lo, hi, kib in PIECES_V + PIECES_S:
+            planes[c, lo, hi] = room(kib, [P, PACK, hi - lo], F32, "planes")
         for t in range(PACK):
-            for pair in range(2):
-                gather(planes[pair][:, t, :], 0, t, 2 * pair, 2)
-        for e in range(2):
-            for c in range(PASSES):
-                round_w2(15 + e, e, c)
-        load_w2(0, 2, 0)
-        for t in range(1, PACK):
-            load_dy(t, 1, t)
-        load_a1_apart(8, 0)
-        load_w2(5, 2, 1)
-        quantize_w2(codes(25, 0, PAIR, "w2_q0"), 0)
+            nc.vector.tensor_tensor(planes[0, 0, PAIR][:, t, :], dy[0, t].indirect(slots(0, PAIR)), gates[0], MULT)
+            nc.scalar.activation(planes[0, PAIR, T][:, t, :], dy[0, t].indirect(slots(PAIR, T)), COPY)
+        late = room(G_ROUND[0], [P, 2, PACK * C], BF16, "g_late")
+        for e in range(2, E):
+            nc.gpsimd.tensor_tensor(woven(late[:, e - 2, :]), by_lines(unit(0, e)), over_rows(gates_out(e)), MULT)
+        for t in range(PACK):
+            for c, lo, hi, kib in PIECES_V[1:]:
+                nc.vector.tensor_copy(planes[c, lo, hi][:, t, :], dy[c, t].indirect(slots(lo, hi)))
+            for c, lo, hi, kib in PIECES_S[1:]:
+                nc.scalar.activation(planes[c, lo, hi][:, t, :], dy[c, t].indirect(slots(lo, hi)), COPY)
+        load_w2(DY[0], 1, 1)
+        load_saved(DY[1], 1, 0)
+        load_w13(DY[2], 0)
+        load_w2(DY[3], 2, 0)
+        load_saved(DY[4], 0, 1)
+        load_w2(DY[5], 2, 1)
+        load_saved(DY[6], 1, 1)
+        load_w13(DY[2] + 4, 1)
+        load_w2(82, 3, 0)
 
-        first_pass = room(6, [P, E, PACK * C], BF16, "first_pass")
-        for e in range(E):
-            weave(first_pass[:, e, :], planes[e // 2][:, :, e % 2 * C : (e % 2 + 1) * C])
-        round_w2(17, 2, 0)
-        load_w2(10, 3, 0)
-        load_w2(9, 3, 1)
-        load_saved(11, a3_raw, a3_rows, 0)
-        load_a1_apart(12, 1)
-        load_w13(0, 0)
-        g_q[0, 0] = codes(25, 2, C, "g00")
-        quantize(g_q[0, 0], first_pass[:, 0, :], E5M2X4)
+        gate_on_vector(MASKED, 0)
+        round_w2(0, 0, nc.vector.tensor_copy)
+        g_b[0, 0] = room(98, [P, PACK * C], BF16, "g_b")
+        nc.vector.tensor_copy(woven(g_b[0, 0]), by_lines(unit(0, 0)))
+        round_w2(0, 1)
+        g_b[1, 0] = room(FRESH[1], [P, PACK * C], BF16, "g_b")
+        nc.scalar.copy(out=woven(g_b[1, 0]), in_=by_lines(unit(0, 1)))
+        quantize_g(0, 1)
+        quantize_g(0, 0)
+        quantize_w2(0, 0, 1)
+        quantize_w2(0, 1, 2)
+        first_product(0)
+        both = codes(G_WORDS + 12, FRESH[1] + 4, PAIR, "g_q_late")
+        quantize(both, late.rearrange("p e x -> p (e x)"), E5M2X4)
+        g_q[2, 0], g_q[3, 0] = part(both, 0, C), part(both, C, PAIR)
+        load_saved(FRESH[0], 0, 2)
+        load_w2(90, 3, 1)
 
-        own = room(13, [P, PACK, PAIR], F32, "own")
-        for t in range(PACK - 1):
-            gather(own[:, t, :], 1, t, 0, 2)
-        for e in range(2):
-            gather(own[:, PACK - 1, e * C : (e + 1) * C], 1, PACK - 1, e, 1)
-        gb01 = room(26, [P, PACK * C], BF16, "gb01")
-        weave(gb01[:], own[:, :, 0:C])
-        gb11 = room(22, [P, PACK * C], BF16, "gb11", 3)
-        weave(gb11[:], own[:, :, C:])
-        round_w2(17, 2, 1)
-        quantize_w2(codes(24, 0, PAIR, "w2_q1", (26, 2)), 1)
-        load_saved(16, a3_raw, a3_rows, 1)
-        g_b = codes(15, 0, PAIR, "g_b", (26, 2.5))
-        g_q[2, 0], g_q[3, 0] = part(g_b, 0, C), part(g_b, C, PAIR)
-        quantize(g_b, flat(first_pass[:, 2:E, :]), E5M2X4)
-        g_q[0, 1] = codes(24, 2, C, "g01")
-        quantize(g_q[0, 1], gb01[:], E5M2X4)
-        first_product(0, (0, 1, 2, 3))
-        g_q[1, 0] = codes(25, 3, C, "g10", (26, 3))
-        quantize(g_q[1, 0], first_pass[:, 1, :], E5M2X4)
-        g_q[1, 1] = codes(24, 3, C, "g11")
-        quantize(g_q[1, 1], gb11[:], E5M2X4)
-        load_w13(7, 1)
-        load_a1_apart(13, 2)
-        load_saved(14, a3_raw, a3_rows, 2)
-        load_a1(6, 3)
-        load_saved(5, a3_raw, a3_rows, 3)
+        result = room(RESULT, [P, T], F32, "result")
+        for e in range(E - 1):
+            mask(e)
+            derivative(nc.gpsimd, e, 1, range(BLOCKS))
+            spread_gates(e + 1, 0)
+            gate_on_vector(G_ROUND[e % 2], e + 1)
+            round_w2(e + 1, 0)
+            round_w2(e + 1, 1)
+            if e == 0:
+                quantize_g(1, 0)
+            else:
+                put_back(e - 1, 1, DY[7] + 2 * e, 0, C, nc.vector.tensor_copy)
+            quantize_w2(e + 1, 0, 2)
+            quantize_g(e + 1, 1)
+            first_product(e + 1)
+            derivative(nc.vector, e, 0, range(BLOCKS))
+            round_w13(e)
+            quantize_da(e, 1, 0, C)
+            quantize_w13(e)
+            quantize_da(e, 0, 0, C)
+            if e == 0:
+                load_saved(FRESH[2], 1, 2)
+                load_w13(DY[0], 2)
+                load_saved(FRESH[3], 0, 3)
+                load_w13(DY[0] + 4, 3)
+                load_saved(DY[1], 1, 3)
 
-        window(0, 23, 22)
-        first_product(1, (0, 1, 2, 3), (1, 0))
-        round_w2(19, 3, 0)
-        round_w2(19, 3, 1)
-        weave_da(9, 0, 0, 1)
-        pick_and_turn(8, 2, 0, ((22, 2), (22, 2.5)))
-        pick_and_turn(8, 2, 1, ((21, 0), (21, 1)))
-        turn_back(2)
-        gb21 = join(25, 0, 2)
-
-        window(1, 20, 18)
-        weave_da(21, 1, 1, 1)
-        pick_and_turn(12, 3, 0, ((18, 2), (18, 2.5)))
-        pick_and_turn(12, 3, 1, ((11, 0), (23, 3.75)))
-        turn_back(3)
-        gb31 = join(24, 2, 3)
-        w1_first = round_w13(18, 3, 0, (0,))
-        w3_first = round_w13(24, 0, 0, (1,))
-        quantize_w2(codes(20, 0, PAIR, "w2_q2"), 2)
-        quantize_w2(codes(20, 2, PAIR, "w2_q3"), 3)
-        quantize_da(16, 0, 0, 1)
-        quantize_da(16, 1, 0, 0)
-        g_q[2, 1] = codes(16, 2, C, "g21", (23, 3.75))
-        quantize(g_q[2, 1], gb21[:], E5M2X4)
-        first_product(2, (0, 1, 2, 3), (1, 0))
-        w13_second = round_w13(25, 0, 1, (0, 1))
-        quantize_da(16, 3, 1, 1)
-        g_q[3, 1] = codes(22, 0, C, "g31")
-        quantize(g_q[3, 1], gb31[:], E5M2X4)
-        first_product(3, (4, 5, 6, 7), (1, 0))
-        quantize_w13(21, 1, 0, (0,), w1_first)
-        quantize_w13(21, 2, 0, (1,), w3_first)
-        quantize_da(7, 0, 1, 0)
-
-        mask(24, 2)
-        new_rows(22, 2, 2, 0)
-        new_rows(18, 0, 2, 1)
-        da3_from_banks(2, 0, 1)
-        mask(19, 3)
-        da3_from_banks(2, 1, PACK)
-        from_masked(2, 0, 0, 1)
-        from_masked(2, 0, 1, 2)
-        from_masked(2, 0, 2, PACK)
-        woven_from_masked(10, 0, 3, 1)
-        result = room(12, [P, T], F32, "result", 3)
-        second_product(0, 0, (0, 1))
-        second_product(1, 4, (1, 0))
-        put_back(8, 0, 0, CUTS[0])
-        weave_da(7, 0, 2, 0)
-        weave_da(22, 3, 2, 1)
-        quantize_da(6, 1, 2, 0)
-        quantize_w13(6, 0, 1, (0, 1), w13_second, (22, 2))
-        quantize_da(1, 0, 3, 1, (22, 2.25))
-        quantize_da(6, 2, 2, 1)
-        woven_from_masked(10, 0, 3, 0)
-        put_back(18, 0, CUTS[0], PAIR)
-        second_product(2, 2, (0, 1))
-        put_back(8, 2, PAIR, CUTS[1])
-        quantize_da(1, 1, 3, 0)
-        put_back(19, 0, CUTS[1], 3 * C)
-        second_product(3, 3, (1, 0))
-        put_back(2, 0, 3 * C, E * C)
+        e = E - 1
+        mask(e)
+        round_w13(e)
+        put_back(e - 1, 1, DY[7] + 2 * e, 0, C, nc.vector.tensor_copy)
+        derivative(nc.gpsimd, e, 1, range(2))
+        derivative(nc.vector, e, 0, range(2))
+        quantize_w13(e)
+        quantize_da(e, 1, 0, HALF)
+        quantize_da(e, 0, 0, HALF)
+        put_back(e, 5, DY[7], 0, HALF, nc.scalar.copy)
+        derivative(nc.vector, e, 1, range(2, BLOCKS))
+        derivative(nc.vector, e, 0, range(2, BLOCKS))
+        quantize_da(e, 1, HALF, C)
+        quantize_da(e, 0, HALF, C)
+        put_back(e, 6, DY[7] + 1, HALF, C, nc.scalar.copy)
         nc.sync.dma_start(out[:, 0:PAIR], result[:, 0:PAIR])
         nc.scalar.dma_start(out[:, PAIR:T], result[:, PAIR:T])

@@ -22,6 +22,7 @@ E4M3X4 = mybir.dt.float8_e4m3fn_x4
 E5M2X4 = mybir.dt.float8_e5m2_x4
 MULT = mybir.AluOpType.mult
 IS_GT = mybir.AluOpType.is_gt
+MAX = mybir.AluOpType.max
 COPY = mybir.ActivationFunctionType.Copy
 
 FLOPS = 2 * N * H * E * C + 2 * 2 * H * K * E * C
@@ -30,7 +31,7 @@ BYTES = 4 * (N * T + 2 * H * E * C + E * N * H + 2 * E * H * K + E * C + K * T) 
 DY = [8 * i for i in range(8)]
 IDENT = 65
 PIECES_V = ((0, 0, PAIR, 66), (1, 0, C, 98), (1, C, C + HALF, 106))
-PIECES_S = ((0, PAIR, T, 82), (1, C + HALF, T, 110))
+PIECES_S = ((0, PAIR, T, 82), (1, C + HALF, 3 * C, 110), (1, 3 * C, T, 0))
 FRESH = [130, 138, 146, 154]
 GATES = [162, 166]
 RESULT = 170
@@ -65,7 +66,7 @@ def tile_moe_bdx_glu_relu_kernel(tc, dyT, a1, a3, w2, w1, w3, gate, offs, out):
         dy, planes, gates, gate_bank = {}, {}, {}, {}
         w2_raw, w2_b, w2_q, g_b, g_q = {}, {}, {}, {}, {}
         saved, w13_raw, w13_b, w13_q = {}, {}, {}, {}
-        dh, masked, da_b, da_q = {}, {}, {}, {}
+        dh, masked, da3_q = {}, {}, {}
 
         def load(dst, src):
             nc.sync.dma_start(dst, src)
@@ -122,49 +123,45 @@ def tile_moe_bdx_glu_relu_kernel(tc, dyT, a1, a3, w2, w1, w3, gate, offs, out):
         def gates_in(e):
             return gate_bank[e].rearrange("q i s -> q s i")
 
-        def gate_on_vector(kib, e):
-            g_b[e, 1] = room(kib, [P, PACK * C], BF16, "g_b")
-            cuts = (0, HALF, C) if e == 1 else (0, C)
-            for lo, hi in zip(cuts, cuts[1:]):
-                nc.vector.tensor_tensor(
-                    woven(g_b[e, 1][:, lo * PACK : hi * PACK]),
-                    by_lines(gathered(1, e * C + lo, e * C + hi)),
-                    over_rows(gates_in(e)[:, lo // LINE : hi // LINE, :]),
-                    MULT,
-                )
+        def gate_second_pass(engine, gates_of, e, lo, hi):
+            engine.tensor_tensor(
+                woven(g_b[e, 1][:, lo * PACK : hi * PACK]),
+                by_lines(gathered(1, e * C + lo, e * C + hi)),
+                over_rows(gates_of(e)[:, lo // LINE : hi // LINE, :]),
+                MULT,
+            )
 
-        def quantize_g(e, c):
+        def quantize_g(e, c, words_at):
             place = 2 * e + c if e < 2 else e + 2
-            g_q[e, c] = codes(G_WORDS + 2 * place, G_SCALES + 0.5 * place, C, "g_q")
+            g_q[e, c] = codes(words_at, G_SCALES + 0.5 * place, C, "g_q")
             quantize(g_q[e, c], g_b[e, c], E5M2X4)
 
         def round_w2(e, c, copy=nc.scalar.copy):
             if c == 0:
-                w2_b[e] = room(W2_ROUND[e % 2], [P, PASSES * PACK * H], BF16, "w2_b")
+                w2_b[e] = room((188, W2_ROUND[1], W2_ROUND[0], 189)[e], [P, PASSES * PACK * H], BF16, "w2_b")
             copy(
                 out=w2_b[e][:, c * PACK * H : (c + 1) * PACK * H].rearrange("p (t m u k) -> p m u t k", t=PACK, u=2, k=2),
                 in_=w2_raw[e, c].rearrange("p (u k) (m t) -> p m u t k", t=PACK, k=2),
             )
 
-        def quantize_w2(e, lo, hi):
-            if lo == 0:
-                w2_q[e] = codes(W2_CODES[e % 2], W2_CODES[e % 2] + 4, PASSES * H, "w2_q")
-            quantize(part(w2_q[e], lo * H, hi * H), w2_b[e][:, lo * PACK * H : hi * PACK * H], E4M3X4)
+        def quantize_w2(e, scales_at):
+            w2_q[e] = codes(W2_CODES[e % 2], scales_at, PASSES * H, "w2_q")
+            quantize(w2_q[e], w2_b[e], E4M3X4)
 
-        def round_w13(e):
-            w13_b[e] = room((79, 163)[e % 2], [P, 2, PACK * K], BF16, "w13_b")
+        def round_w13(e, kib):
+            w13_b[e] = room(kib, [P, 2, PACK * K], BF16, "w13_b")
             for n in range(2):
                 nc.scalar.copy(out=woven(w13_b[e][:, n, :]), in_=by_lines(w13_raw[e, n]))
 
-        def quantize_w13(e):
-            w13_q[e] = codes(81, 162, 2 * K, "w13_q")
+        def quantize_w13(e, words_at):
+            w13_q[e] = codes(words_at, 64 + 0.25 * e, 2 * K, "w13_q")
             quantize(w13_q[e], w13_b[e].rearrange("p n x -> p (n x)"), E4M3X4)
 
         def first_product(e):
             for b in range(BLOCKS):
                 dh[e, b] = bank(b, [P, PACK, P], "dh")
-                for t in range(PACK):
-                    for c in range(PASSES):
+                for c in range(PASSES):
+                    for t in range(PACK):
                         words, scales = part(w2_q[e], c * H + t * P, c * H + (t + 1) * P)
                         moving, moving_scales = part(g_q[e, c], b * P, (b + 1) * P)
                         nc.tensor.matmul_mx(
@@ -173,38 +170,44 @@ def tile_moe_bdx_glu_relu_kernel(tc, dyT, a1, a3, w2, w1, w3, gate, offs, out):
                             lhsT_scale=scales,
                             rhs=moving.bitcast(E5M2X4),
                             rhs_scale=moving_scales,
-                            start=(c == 0),
-                            stop=(c == PASSES - 1),
+                            start=(c == 0 and t == 0),
+                            stop=(c == PASSES - 1 and t == PACK - 1),
                         )
 
-        def mask(e):
-            for b in range(BLOCKS):
-                masked[e, b] = room(MASKED + 2 * b, [P, PACK, P], F32, "masked")
-                nc.vector.scalar_tensor_tensor(
-                    masked[e, b], saved[0, e][:, :, b * P : (b + 1) * P], 0.0, dh[e, b], op0=IS_GT, op1=MULT
-                )
+        def saved_cols(n, e, lo, hi):
+            return saved[n, e][:, :, lo * P : hi * P]
 
-        def derivative(engine, e, n, blocks):
-            if (e, n) not in da_b:
-                da_b[e, n] = room(70 - 4 * n, [P, PACK * C], BF16, "da_b")
-            for b in blocks:
-                engine.tensor_tensor(
-                    woven(da_b[e, n][:, b * PACK * P : (b + 1) * PACK * P]),
-                    by_lines(saved[1 - n, e][:, :, b * P : (b + 1) * P]),
-                    by_lines(masked[e, b]),
-                    MULT,
-                )
+        def mask(e, b):
+            if b % 2 == 0:
+                masked[e, b // 2] = room((MASKED, 74)[e % 2] + 2 * b, [P, PACK, HALF], F32, "masked")
+            dst = masked[e, b // 2][:, :, b % 2 * P : (b % 2 + 1) * P]
+            nc.vector.scalar_tensor_tensor(dst, saved_cols(0, e, b, b + 1), 0.0, dh[e, b], op0=IS_GT, op1=MULT)
 
-        def quantize_da(e, n, lo, hi):
-            if lo == 0:
-                da_q[e, n] = codes(74 + 2 * n, 78 + 0.5 * n, C, "da_q")
-            quantize(part(da_q[e, n], lo, hi), da_b[e, n][:, lo * PACK : hi * PACK], E5M2X4)
+        def make_da3(dst, e, b):
+            nc.vector.scalar_tensor_tensor(
+                dst.rearrange("p (s t) -> p s t", t=PACK),
+                saved_cols(0, e, b, b + 1).rearrange("p t s -> p s t"),
+                0.0,
+                dh[e, b].rearrange("p t s -> p s t"),
+                op0=MAX,
+                op1=MULT,
+            )
 
-        def put_back(e, b, kib, lo, hi, copy):
-            sums = bank(b, [P, hi - lo], "dx")
-            for n in (1, 0):
+        def make_da1(engine, dst, e, h):
+            engine.tensor_tensor(woven(dst), by_lines(saved_cols(1, e, 2 * h, 2 * h + 2)), by_lines(masked[e, h]), MULT)
+
+        def quantize_da(src, words_at, scales_at):
+            dst = codes(words_at, scales_at, src.shape[1] // PACK, "da_q")
+            quantize(dst, src, E5M2X4)
+            return dst
+
+        def blocks(x, lo, hi):
+            return x[:, lo * PACK * P : hi * PACK * P]
+
+        def second_product(e, b, da1_q, da3_q):
+            sums = bank(b, [P, da1_q[0].shape[1]], "dx")
+            for n, (moving, moving_scales) in ((1, da3_q), (0, da1_q)):
                 words, scales = part(w13_q[e], n * K, (n + 1) * K)
-                moving, moving_scales = part(da_q[e, n], lo, hi)
                 nc.tensor.matmul_mx(
                     out=sums,
                     lhsT=words.bitcast(E4M3X4),
@@ -214,12 +217,15 @@ def tile_moe_bdx_glu_relu_kernel(tc, dyT, a1, a3, w2, w1, w3, gate, offs, out):
                     start=(n == 1),
                     stop=(n == 0),
                 )
+            return sums
+
+        def put_back(e, sums, kib, lo, hi, copy=nc.scalar.copy):
             dx = room(kib, [P, hi - lo], F32, "dx")
-            copy(out=dx, in_=sums)
+            copy(dx, sums)
             for at in range(lo, hi, HALF):
                 nc.scalar.activation(result.indirect(slots(e * C + at, e * C + at + HALF)), dx[:, at - lo : at - lo + HALF], COPY)
 
-        gate_runs = held.tile([P, E, LINE], F32, name="gate_runs")[:]
+        gate_runs = room(82, [P, E, LINE], F32, "gate_runs")
         load(gate_runs, gate[0:1, :].rearrange("o (e p i) -> p (o e) i", e=E, i=LINE))
         offsets = held.tile([P, E * C // 16], U16, name="offsets")
         nc.sync.dma_start(offsets[:], offs)
@@ -228,101 +234,170 @@ def tile_moe_bdx_glu_relu_kernel(tc, dyT, a1, a3, w2, w1, w3, gate, offs, out):
                 dy[c, t] = load(room(DY[c * PACK + t], [P, T], F32, "dy"), dy_rows[c, t])
         load_w2(FRESH[0], 0, 0)
         load_w2(FRESH[1], 0, 1)
-        load_w2(FRESH[2], 1, 0)
         load_saved(FRESH[3], 0, 0)
+        load_w2(FRESH[2], 1, 0)
 
         ident = room(IDENT, [P, P], F32, "ident")
         make_identity(nc, ident)
         for pair in range(2):
             gates[pair] = room(GATES[pair], [P, PAIR], F32, "gates")
-        for e in range(2):
+        for e, copy in ((2, nc.scalar.copy), (0, nc.vector.tensor_copy), (1, nc.scalar.copy)):
             spread_gates(e, 4 + e)
-            spread_gates(e + 2, 6 + e)
-            nc.vector.tensor_copy(gates_out(e), gates_in(e))
-            nc.scalar.copy(out=gates_out(e + 2), in_=gates_in(e + 2))
+            copy(gates_out(e), gates_in(e))
+        spread_gates(3, 7)
 
-        for c, lo, hi, kib in PIECES_V + PIECES_S:
+        def gather_on_scalar(piece, t):
+            c, lo, hi, kib = piece
+            if t == 0:
+                planes[c, lo, hi] = room(kib, [P, PACK, hi - lo], F32, "planes")
+            nc.scalar.activation(planes[c, lo, hi][:, t, :], dy[c, t].indirect(slots(lo, hi)), COPY)
+
+        for c, lo, hi, kib in PIECES_V:
             planes[c, lo, hi] = room(kib, [P, PACK, hi - lo], F32, "planes")
         for t in range(PACK):
             nc.vector.tensor_tensor(planes[0, 0, PAIR][:, t, :], dy[0, t].indirect(slots(0, PAIR)), gates[0], MULT)
-            nc.scalar.activation(planes[0, PAIR, T][:, t, :], dy[0, t].indirect(slots(PAIR, T)), COPY)
+            gather_on_scalar(PIECES_S[0], t)
+        nc.vector.tensor_copy(gates_out(3), gates_in(3))
         late = room(G_ROUND[0], [P, 2, PACK * C], BF16, "g_late")
         for e in range(2, E):
             nc.gpsimd.tensor_tensor(woven(late[:, e - 2, :]), by_lines(unit(0, e)), over_rows(gates_out(e)), MULT)
+        g_b[0, 0] = room(122, [P, PACK * C], BF16, "g_b")
         for t in range(PACK):
             for c, lo, hi, kib in PIECES_V[1:]:
                 nc.vector.tensor_copy(planes[c, lo, hi][:, t, :], dy[c, t].indirect(slots(lo, hi)))
-            for c, lo, hi, kib in PIECES_S[1:]:
-                nc.scalar.activation(planes[c, lo, hi][:, t, :], dy[c, t].indirect(slots(lo, hi)), COPY)
+            gather_on_scalar(PIECES_S[1], t)
+        nc.scalar.copy(out=woven(g_b[0, 0]), in_=by_lines(unit(0, 0)))
         load_w2(DY[0], 1, 1)
-        load_saved(DY[1], 1, 0)
-        load_w13(DY[2], 0)
         load_w2(DY[3], 2, 0)
-        load_saved(DY[4], 0, 1)
-        load_w2(DY[5], 2, 1)
-        load_saved(DY[6], 1, 1)
-        load_w13(DY[2] + 4, 1)
-        load_w2(82, 3, 0)
+        load_w13(DY[2], 0)
+        load_saved(DY[1], 1, 0)
+        load_saved(82, 0, 1)
+        load_saved(90, 1, 1)
 
-        gate_on_vector(MASKED, 0)
-        round_w2(0, 0, nc.vector.tensor_copy)
-        g_b[0, 0] = room(98, [P, PACK * C], BF16, "g_b")
-        nc.vector.tensor_copy(woven(g_b[0, 0]), by_lines(unit(0, 0)))
-        round_w2(0, 1)
-        g_b[1, 0] = room(FRESH[1], [P, PACK * C], BF16, "g_b")
+        g_b[0, 1] = room(MASKED, [P, PACK * C], BF16, "g_b")
+        gate_second_pass(nc.vector, gates_in, 0, 0, C)
+        round_w2(0, 0)
+        g_b[1, 0] = room(FRESH[0], [P, PACK * C], BF16, "g_b")
         nc.scalar.copy(out=woven(g_b[1, 0]), in_=by_lines(unit(0, 1)))
-        quantize_g(0, 1)
-        quantize_g(0, 0)
-        quantize_w2(0, 0, 1)
-        quantize_w2(0, 1, 2)
+        quantize_g(0, 0, 98)
+        quantize_g(0, 1, G_WORDS)
+        round_w2(0, 1, nc.vector.tensor_copy)
+        quantize_w2(0, W2_CODES[0] + 4)
         first_product(0)
-        both = codes(G_WORDS + 12, FRESH[1] + 4, PAIR, "g_q_late")
+        both = codes(G_WORDS + 12, 188, PAIR, "g_q_late")
         quantize(both, late.rearrange("p e x -> p (e x)"), E5M2X4)
         g_q[2, 0], g_q[3, 0] = part(both, 0, C), part(both, C, PAIR)
-        load_saved(FRESH[0], 0, 2)
-        load_w2(90, 3, 1)
+        round_w2(1, 0)
+        round_w2(1, 1)
+        for t in range(PACK):
+            gather_on_scalar(PIECES_S[2], t)
+        load_w2(FRESH[1], 2, 1)
+        load_w2(FRESH[2], 3, 0)
+        load_saved(DY[4], 0, 2)
+        load_saved(DY[5], 1, 2)
+        load_w13(DY[6], 1)
+        load_w2(DY[7], 3, 1)
 
         result = room(RESULT, [P, T], F32, "result")
-        for e in range(E - 1):
-            mask(e)
-            derivative(nc.gpsimd, e, 1, range(BLOCKS))
-            spread_gates(e + 1, 0)
-            gate_on_vector(G_ROUND[e % 2], e + 1)
-            round_w2(e + 1, 0)
-            round_w2(e + 1, 1)
-            if e == 0:
-                quantize_g(1, 0)
-            else:
-                put_back(e - 1, 1, DY[7] + 2 * e, 0, C, nc.vector.tensor_copy)
-            quantize_w2(e + 1, 0, 2)
-            quantize_g(e + 1, 1)
-            first_product(e + 1)
-            derivative(nc.vector, e, 0, range(BLOCKS))
-            round_w13(e)
-            quantize_da(e, 1, 0, C)
-            quantize_w13(e)
-            quantize_da(e, 0, 0, C)
-            if e == 0:
-                load_saved(FRESH[2], 1, 2)
-                load_w13(DY[0], 2)
-                load_saved(FRESH[3], 0, 3)
-                load_w13(DY[0] + 4, 3)
-                load_saved(DY[1], 1, 3)
+        a1_at = (FRESH[3], 82, DY[4])
+        turns = (66, 70)
 
-        e = E - 1
-        mask(e)
-        round_w13(e)
-        put_back(e - 1, 1, DY[7] + 2 * e, 0, C, nc.vector.tensor_copy)
-        derivative(nc.gpsimd, e, 1, range(2))
-        derivative(nc.vector, e, 0, range(2))
-        quantize_w13(e)
-        quantize_da(e, 1, 0, HALF)
-        quantize_da(e, 0, 0, HALF)
-        put_back(e, 5, DY[7], 0, HALF, nc.scalar.copy)
-        derivative(nc.vector, e, 1, range(2, BLOCKS))
-        derivative(nc.vector, e, 0, range(2, BLOCKS))
-        quantize_da(e, 1, HALF, C)
-        quantize_da(e, 0, HALF, C)
-        put_back(e, 6, DY[7] + 1, HALF, C, nc.scalar.copy)
+        def all_masks(e):
+            for b in range(BLOCKS):
+                mask(e, b)
+
+        def all_da3(e, da3):
+            for b in range(BLOCKS):
+                make_da3(blocks(da3, b, b + 1), e, b)
+
+        def half(x, h):
+            return blocks(x, 2 * h, 2 * h + 2)
+
+        g_b[1, 1] = room(G_ROUND[0], [P, PACK * C], BF16, "g_b")
+        for lo in range(0, C, HALF):
+            gate_second_pass(nc.gpsimd, gates_out, 1, lo, lo + HALF)
+        da3 = room(turns[0], [P, PACK * C], BF16, "da3")
+        for b in range(BLOCKS):
+            mask(0, b)
+            make_da3(blocks(da3, b, b + 1), 0, b)
+        quantize_g(1, 0, a1_at[0] + 2)
+        quantize_w2(1, a1_at[0] + 7)
+        quantize_g(1, 1, a1_at[0])
+        first_product(1)
+        da3_q[0] = quantize_da(da3, W2_ROUND[1] + 4, 105)
+        round_w2(2, 0)
+        round_w13(0, 205)
+        round_w2(2, 1)
+        load_w13(FRESH[1], 2)
+        load_w13(FRESH[1] + 4, 3)
+
+        g_b[2, 1] = room(W2_ROUND[1], [P, PACK * C], BF16, "g_b")
+        gate_second_pass(nc.vector, gates_in, 2, 0, C)
+        da1 = room(turns[0], [P, PACK * C], BF16, "da1")
+        for h in range(2):
+            make_da1(nc.gpsimd, half(da1, h), 0, h)
+        load_saved(DY[1], 0, 3)
+        da3 = room(turns[1], [P, PACK * C], BF16, "da3")
+        all_masks(1)
+        early = room(122, [P, PACK * HALF], BF16, "da1_half")
+        make_da1(nc.gpsimd, early, 1, 0)
+        all_da3(1, da3)
+        quantize_w13(0, a1_at[1] + 2)
+        sums = second_product(0, 4, quantize_da(da1, a1_at[1] + 4, 100), da3_q[0])
+        quantize_w2(2, a1_at[1] + 7)
+        quantize_g(2, 1, a1_at[1])
+        first_product(2)
+        early_q = quantize_da(early, a1_at[1] + 6, 100.5)
+        da3_q[1] = quantize_da(da3, W2_ROUND[0] + 4, 105.5)
+        round_w2(3, 0)
+        round_w13(1, 207)
+        load_saved(FRESH[2], 1, 3)
+        put_back(0, sums, 126, 0, C)
+        round_w2(3, 1)
+        round_w13(2, 209)
+        round_w13(3, 211)
+
+        g_b[3, 1] = room(W2_ROUND[0], [P, PACK * C], BF16, "g_b")
+        gate_second_pass(nc.vector, gates_in, 3, 0, HALF)
+        rest = room(turns[1], [P, PACK * HALF], BF16, "da1_half")
+        make_da1(nc.gpsimd, rest, 1, 1)
+        da3 = room(turns[0], [P, PACK * C], BF16, "da3")
+        all_masks(2)
+        gate_second_pass(nc.vector, gates_in, 3, HALF, C)
+        da1 = room(122, [P, PACK * C], BF16, "da1")
+        for h in range(2):
+            make_da1(nc.gpsimd, half(da1, h), 2, h)
+        all_da3(2, da3)
+        quantize_w13(1, a1_at[2] + 2)
+        rest_q = quantize_da(rest, a1_at[2] + 6, 100.75)
+        sums = [second_product(1, 5 + h, (early_q, rest_q)[h], part(da3_q[1], h * HALF, (h + 1) * HALF)) for h in range(2)]
+        quantize_w2(3, a1_at[2] + 7)
+        quantize_g(3, 1, a1_at[2])
+        first_product(3)
+        for h in range(2):
+            put_back(1, sums[h], FRESH[1] + 4 + h, h * HALF, (h + 1) * HALF)
+        quantize_w13(2, a1_at[2] + 3)
+        quantize_w13(3, 193)
+        da1_q = quantize_da(da1, a1_at[2] + 4, 100)
+        da3_q[2] = quantize_da(da3, 189, 105)
+        put_back(2, second_product(2, 4, da1_q, da3_q[2]), 126, 0, C)
+
+        da = [room(at, [P, 2, PACK * HALF], BF16, "da_last") for at in turns]
+
+        def last_da3(b):
+            make_da3(blocks(da[b // 2][:, 1, :], b % 2, b % 2 + 1), 3, b)
+
+        def finish(h, copy):
+            dst = quantize_da(da[h].rearrange("p n x -> p (n x)"), 101 + 2 * h, 128.5 + 0.5 * h)
+            put_back(3, second_product(3, 6 + h, part(dst, 0, HALF), part(dst, HALF, C)), DY[3] + h, h * HALF, (h + 1) * HALF, copy)
+
+        all_masks(3)
+        make_da1(nc.gpsimd, da[0][:, 0, :], 3, 0)
+        for b in range(BLOCKS - 1):
+            last_da3(b)
+        finish(0, nc.scalar.copy)
+        last_da3(BLOCKS - 1)
+        make_da1(nc.vector, da[1][:, 0, :], 3, 1)
+        finish(1, nc.vector.tensor_copy)
         nc.sync.dma_start(out[:, 0:PAIR], result[:, 0:PAIR])
         nc.scalar.dma_start(out[:, PAIR:T], result[:, PAIR:T])

@@ -11,6 +11,7 @@ PAIR = 2 * C
 BLOCKS = C // P
 LINE = 4
 HALF = C // 2
+REACH = 3 * HALF // 4
 KB = 1024
 
 F32 = mybir.dt.float32
@@ -23,6 +24,7 @@ E5M2X4 = mybir.dt.float8_e5m2_x4
 MULT = mybir.AluOpType.mult
 IS_GT = mybir.AluOpType.is_gt
 MAX = mybir.AluOpType.max
+ADD = mybir.AluOpType.add
 COPY = mybir.ActivationFunctionType.Copy
 
 FLOPS = 2 * N * H * E * C + 2 * 2 * H * K * E * C
@@ -38,7 +40,6 @@ RESULT = 170
 MASKED = 178
 G_WORDS = 186
 G_SCALES = 202
-G_ROUND = [205, 209]
 W2_ROUND = [213, 221]
 W2_CODES = [229, 234]
 
@@ -77,6 +78,10 @@ def tile_moe_bdx_glu_relu_kernel(tc, dyT, a1, a3, w2, w1, w3, gate, offs, out):
 
         def load_saved(kib, n, e):
             saved[n, e] = load(room(kib, [P, PACK, C], F32, "saved"), saved_rows[n][:, :, e * C : (e + 1) * C])
+
+        def load_a3_half(kib, e, h):
+            lo = e * C + h * HALF
+            saved[1, e, h] = load(room(kib, [P, PACK, HALF], F32, "saved_half"), saved_rows[1][:, :, lo : lo + HALF])
 
         def load_w13(kib, e):
             for n in range(2):
@@ -131,14 +136,13 @@ def tile_moe_bdx_glu_relu_kernel(tc, dyT, a1, a3, w2, w1, w3, gate, offs, out):
                 MULT,
             )
 
-        def quantize_g(e, c, words_at):
-            place = 2 * e + c if e < 2 else e + 2
-            g_q[e, c] = codes(words_at, G_SCALES + 0.5 * place, C, "g_q")
+        def quantize_g(e, c, words_at, scales_at):
+            g_q[e, c] = codes(words_at, scales_at, C, "g_q")
             quantize(g_q[e, c], g_b[e, c], E5M2X4)
 
         def round_w2(e, c, copy=nc.scalar.copy):
             if c == 0:
-                w2_b[e] = room((188, W2_ROUND[1], W2_ROUND[0], 189)[e], [P, PASSES * PACK * H], BF16, "w2_b")
+                w2_b[e] = room((188, W2_ROUND[1], W2_ROUND[0], 189.5)[e], [P, (PASSES if e < E - 1 else 1) * PACK * H], BF16, "w2_b")
             copy(
                 out=w2_b[e][:, c * PACK * H : (c + 1) * PACK * H].rearrange("p (t m u k) -> p m u t k", t=PACK, u=2, k=2),
                 in_=w2_raw[e, c].rearrange("p (u k) (m t) -> p m u t k", t=PACK, k=2),
@@ -177,6 +181,9 @@ def tile_moe_bdx_glu_relu_kernel(tc, dyT, a1, a3, w2, w1, w3, gate, offs, out):
         def saved_cols(n, e, lo, hi):
             return saved[n, e][:, :, lo * P : hi * P]
 
+        def a3_half(e, h):
+            return saved[1, e, h] if e % 2 else saved_cols(1, e, 2 * h, 2 * h + 2)
+
         def mask(e, b):
             if b % 2 == 0:
                 masked[e, b // 2] = room((MASKED, 74)[e % 2] + 2 * b, [P, PACK, HALF], F32, "masked")
@@ -193,8 +200,10 @@ def tile_moe_bdx_glu_relu_kernel(tc, dyT, a1, a3, w2, w1, w3, gate, offs, out):
                 op1=MULT,
             )
 
-        def make_da1(engine, dst, e, h):
-            engine.tensor_tensor(woven(dst), by_lines(saved_cols(1, e, 2 * h, 2 * h + 2)), by_lines(masked[e, h]), MULT)
+        def make_da1(engine, dst, e, h, lo=0, hi=HALF):
+            engine.tensor_tensor(
+                woven(dst[:, lo * PACK : hi * PACK]), by_lines(a3_half(e, h)[:, :, lo:hi]), by_lines(masked[e, h][:, :, lo:hi]), MULT
+            )
 
         def quantize_da(src, words_at, scales_at):
             dst = codes(words_at, scales_at, src.shape[1] // PACK, "da_q")
@@ -258,48 +267,54 @@ def tile_moe_bdx_glu_relu_kernel(tc, dyT, a1, a3, w2, w1, w3, gate, offs, out):
             nc.vector.tensor_tensor(planes[0, 0, PAIR][:, t, :], dy[0, t].indirect(slots(0, PAIR)), gates[0], MULT)
             gather_on_scalar(PIECES_S[0], t)
         nc.vector.tensor_copy(gates_out(3), gates_in(3))
-        late = room(G_ROUND[0], [P, 2, PACK * C], BF16, "g_late")
+        late = room(122, [P, 2, PACK * C], BF16, "g_late")
         for e in range(2, E):
             nc.gpsimd.tensor_tensor(woven(late[:, e - 2, :]), by_lines(unit(0, e)), over_rows(gates_out(e)), MULT)
-        g_b[0, 0] = room(122, [P, PACK * C], BF16, "g_b")
+        g_b[0, 0] = room(205, [P, PACK * C], BF16, "g_b")
         for t in range(PACK):
             for c, lo, hi, kib in PIECES_V[1:]:
-                nc.vector.tensor_copy(planes[c, lo, hi][:, t, :], dy[c, t].indirect(slots(lo, hi)))
+                if lo > 0 and t == PACK - 1:
+                    nc.scalar.activation(planes[c, lo, hi][:, t, :], dy[c, t].indirect(slots(lo, hi)), COPY)
+                else:
+                    nc.vector.tensor_copy(planes[c, lo, hi][:, t, :], dy[c, t].indirect(slots(lo, hi)))
             gather_on_scalar(PIECES_S[1], t)
         nc.scalar.copy(out=woven(g_b[0, 0]), in_=by_lines(unit(0, 0)))
         load_w2(DY[0], 1, 1)
-        load_w2(DY[3], 2, 0)
-        load_w13(DY[2], 0)
         load_saved(DY[1], 1, 0)
         load_saved(82, 0, 1)
-        load_saved(90, 1, 1)
+        load_w2(DY[3], 2, 0)
+        load_a3_half(90, 1, 0)
+        load_w13(DY[2], 0)
 
         g_b[0, 1] = room(MASKED, [P, PACK * C], BF16, "g_b")
         gate_second_pass(nc.vector, gates_in, 0, 0, C)
         round_w2(0, 0)
         g_b[1, 0] = room(FRESH[0], [P, PACK * C], BF16, "g_b")
         nc.scalar.copy(out=woven(g_b[1, 0]), in_=by_lines(unit(0, 1)))
-        quantize_g(0, 0, 98)
-        quantize_g(0, 1, G_WORDS)
+        quantize_g(0, 0, 98, G_SCALES)
+        quantize_g(0, 1, G_WORDS, G_SCALES + 0.5)
         round_w2(0, 1, nc.vector.tensor_copy)
         quantize_w2(0, W2_CODES[0] + 4)
         first_product(0)
         both = codes(G_WORDS + 12, 188, PAIR, "g_q_late")
         quantize(both, late.rearrange("p e x -> p (e x)"), E5M2X4)
         g_q[2, 0], g_q[3, 0] = part(both, 0, C), part(both, C, PAIR)
+        quantize_g(1, 0, 203, 189)
         round_w2(1, 0)
         round_w2(1, 1)
         for t in range(PACK):
             gather_on_scalar(PIECES_S[2], t)
         load_w2(FRESH[1], 2, 1)
-        load_w2(FRESH[2], 3, 0)
-        load_saved(DY[4], 0, 2)
-        load_saved(DY[5], 1, 2)
-        load_w13(DY[6], 1)
+        load_a3_half(94, 1, 1)
+        load_saved(FRESH[2], 0, 2)
+        load_saved(DY[4], 1, 2)
+        load_w13(DY[5], 1)
+        load_w2(DY[6], 3, 0)
         load_w2(DY[7], 3, 1)
+        load_w13(DY[5] + 4, 2)
 
         result = room(RESULT, [P, T], F32, "result")
-        a1_at = (FRESH[3], 82, DY[4])
+        a1_at = (FRESH[3], 82, FRESH[2])
         turns = (66, 70)
 
         def all_masks(e):
@@ -313,23 +328,20 @@ def tile_moe_bdx_glu_relu_kernel(tc, dyT, a1, a3, w2, w1, w3, gate, offs, out):
         def half(x, h):
             return blocks(x, 2 * h, 2 * h + 2)
 
-        g_b[1, 1] = room(G_ROUND[0], [P, PACK * C], BF16, "g_b")
+        g_b[1, 1] = room(128, [P, PACK * C], BF16, "g_b")
         for lo in range(0, C, HALF):
             gate_second_pass(nc.gpsimd, gates_out, 1, lo, lo + HALF)
         da3 = room(turns[0], [P, PACK * C], BF16, "da3")
         for b in range(BLOCKS):
             mask(0, b)
             make_da3(blocks(da3, b, b + 1), 0, b)
-        quantize_g(1, 0, a1_at[0] + 2)
         quantize_w2(1, a1_at[0] + 7)
-        quantize_g(1, 1, a1_at[0])
+        quantize_g(1, 1, a1_at[0], G_SCALES + 0.5)
         first_product(1)
         da3_q[0] = quantize_da(da3, W2_ROUND[1] + 4, 105)
         round_w2(2, 0)
         round_w13(0, 205)
         round_w2(2, 1)
-        load_w13(FRESH[1], 2)
-        load_w13(FRESH[1] + 4, 3)
 
         g_b[2, 1] = room(W2_ROUND[1], [P, PACK * C], BF16, "g_b")
         gate_second_pass(nc.vector, gates_in, 2, 0, C)
@@ -337,25 +349,26 @@ def tile_moe_bdx_glu_relu_kernel(tc, dyT, a1, a3, w2, w1, w3, gate, offs, out):
         for h in range(2):
             make_da1(nc.gpsimd, half(da1, h), 0, h)
         load_saved(DY[1], 0, 3)
+        load_w13(DY[2], 3)
+        load_a3_half(DY[3], 3, 0)
+        load_a3_half(DY[3] + 4, 3, 1)
         da3 = room(turns[1], [P, PACK * C], BF16, "da3")
         all_masks(1)
         early = room(122, [P, PACK * HALF], BF16, "da1_half")
-        make_da1(nc.gpsimd, early, 1, 0)
+        make_da1(nc.gpsimd, early, 1, 0, 0, REACH)
         all_da3(1, da3)
         quantize_w13(0, a1_at[1] + 2)
+        make_da1(nc.vector, early, 1, 0, REACH, HALF)
         sums = second_product(0, 4, quantize_da(da1, a1_at[1] + 4, 100), da3_q[0])
         quantize_w2(2, a1_at[1] + 7)
-        quantize_g(2, 1, a1_at[1])
+        quantize_g(2, 1, a1_at[1], G_SCALES)
         first_product(2)
         early_q = quantize_da(early, a1_at[1] + 6, 100.5)
         da3_q[1] = quantize_da(da3, W2_ROUND[0] + 4, 105.5)
-        round_w2(3, 0)
         round_w13(1, 207)
-        load_saved(FRESH[2], 1, 3)
-        put_back(0, sums, 126, 0, C)
-        round_w2(3, 1)
+        round_w2(3, 0)
+        put_back(0, sums, FRESH[1], 0, C)
         round_w13(2, 209)
-        round_w13(3, 211)
 
         g_b[3, 1] = room(W2_ROUND[0], [P, PACK * C], BF16, "g_b")
         gate_second_pass(nc.vector, gates_in, 3, 0, HALF)
@@ -365,38 +378,48 @@ def tile_moe_bdx_glu_relu_kernel(tc, dyT, a1, a3, w2, w1, w3, gate, offs, out):
         all_masks(2)
         gate_second_pass(nc.vector, gates_in, 3, HALF, C)
         da1 = room(122, [P, PACK * C], BF16, "da1")
-        for h in range(2):
-            make_da1(nc.gpsimd, half(da1, h), 2, h)
+        make_da1(nc.gpsimd, half(da1, 0), 2, 0)
+        make_da1(nc.gpsimd, half(da1, 1), 2, 1, 0, REACH)
         all_da3(2, da3)
         quantize_w13(1, a1_at[2] + 2)
+        make_da1(nc.vector, half(da1, 1), 2, 1, REACH, HALF)
         rest_q = quantize_da(rest, a1_at[2] + 6, 100.75)
         sums = [second_product(1, 5 + h, (early_q, rest_q)[h], part(da3_q[1], h * HALF, (h + 1) * HALF)) for h in range(2)]
-        quantize_w2(3, a1_at[2] + 7)
-        quantize_g(3, 1, a1_at[2])
+        quantize_g(3, 1, a1_at[2], G_SCALES + 0.5)
+        w2_q[3] = codes(W2_CODES[1], a1_at[2] + 4, PASSES * H, "w2_q")
+        quantize(part(w2_q[3], 0, H), w2_b[3], E4M3X4)
+        last_b = room(a1_at[2] + 7, [P, PACK * H], BF16, "w2_last")
+        src = w2_raw[3, 1].rearrange("p (u k) (m t) -> p m u t k", t=PACK, k=2)
+        dst = last_b.rearrange("p (t m u k) -> p m u t k", t=PACK, u=2, k=2)
+        nc.scalar.copy(out=dst[:, 0 : P // 2], in_=src[:, 0 : P // 2])
+        nc.vector.tensor_copy(dst[:, P // 2 : P], src[:, P // 2 : P])
+        da1_q = quantize_da(da1, 190, 100)
+        quantize(part(w2_q[3], H, 2 * H), last_b, E4M3X4)
         first_product(3)
         for h in range(2):
-            put_back(1, sums[h], FRESH[1] + 4 + h, h * HALF, (h + 1) * HALF)
+            put_back(1, sums[h], DY[5] + 4 + h, h * HALF, (h + 1) * HALF)
         quantize_w13(2, a1_at[2] + 3)
-        quantize_w13(3, 193)
-        da1_q = quantize_da(da1, a1_at[2] + 4, 100)
-        da3_q[2] = quantize_da(da3, 189, 105)
+        da3_q[2] = quantize_da(da3, a1_at[2] + 7, 105)
         put_back(2, second_product(2, 4, da1_q, da3_q[2]), 126, 0, C)
 
-        da = [room(at, [P, 2, PACK * HALF], BF16, "da_last") for at in turns]
+        w13_b[3] = room(turns[0], [P, 2, PACK * K], BF16, "w13_b")
+        for n in range(2):
+            nc.gpsimd.tensor_scalar(woven(w13_b[3][:, n, :]), by_lines(w13_raw[3, n]), 1.0, 0.0, MULT, ADD)
+        da = [room(at, [P, 2, PACK * HALF], BF16, "da_last") for at in (122, turns[1])]
 
         def last_da3(b):
             make_da3(blocks(da[b // 2][:, 1, :], b % 2, b % 2 + 1), 3, b)
 
         def finish(h, copy):
             dst = quantize_da(da[h].rearrange("p n x -> p (n x)"), 101 + 2 * h, 128.5 + 0.5 * h)
-            put_back(3, second_product(3, 6 + h, part(dst, 0, HALF), part(dst, HALF, C)), DY[3] + h, h * HALF, (h + 1) * HALF, copy)
+            put_back(3, second_product(3, 6 + h, part(dst, 0, HALF), part(dst, HALF, C)), DY[7] + h, h * HALF, (h + 1) * HALF, copy)
 
         all_masks(3)
         make_da1(nc.gpsimd, da[0][:, 0, :], 3, 0)
-        for b in range(BLOCKS - 1):
+        for b in range(BLOCKS):
             last_da3(b)
+        quantize_w13(3, 192)
         finish(0, nc.scalar.copy)
-        last_da3(BLOCKS - 1)
         make_da1(nc.vector, da[1][:, 0, :], 3, 1)
         finish(1, nc.vector.tensor_copy)
         nc.sync.dma_start(out[:, 0:PAIR], result[:, 0:PAIR])

@@ -83,8 +83,8 @@ def tile_moe_bdx_glu_relu_kernel(tc, dyT, a1, a3, w2, w1, w3, gate, offs, out):
             lo = e * C + h * HALF
             saved[1, e, h] = load(room(kib, [P, PACK, HALF], F32, "saved_half"), saved_rows[1][:, :, lo : lo + HALF])
 
-        def load_w13(kib, e):
-            for n in range(2):
+        def load_w13(kib, e, which=(0, 1)):
+            for n in which:
                 w13_raw[e, n] = load(room(kib + 2 * n, [P, PACK, K], F32, "w13_raw"), w13_rows[n][e])
 
         def codes(words_at, scales_at, width, name):
@@ -235,7 +235,7 @@ def tile_moe_bdx_glu_relu_kernel(tc, dyT, a1, a3, w2, w1, w3, gate, offs, out):
                 nc.scalar.activation(result.indirect(slots(e * C + at, e * C + at + HALF)), dx[:, at - lo : at - lo + HALF], COPY)
 
         gate_runs = room(82, [P, E, LINE], F32, "gate_runs")
-        load(gate_runs, gate[0:1, :].rearrange("o (e p i) -> p (o e) i", e=E, i=LINE))
+        nc.scalar.dma_start(gate_runs, gate[0:1, :].rearrange("o (e p i) -> p (o e) i", e=E, i=LINE))
         offsets = held.tile([P, E * C // 16], U16, name="offsets")
         nc.sync.dma_start(offsets[:], offs)
         for c in range(PASSES):
@@ -349,8 +349,9 @@ def tile_moe_bdx_glu_relu_kernel(tc, dyT, a1, a3, w2, w1, w3, gate, offs, out):
         for h in range(2):
             make_da1(nc.gpsimd, half(da1, h), 0, h)
         load_saved(DY[1], 0, 3)
-        load_w13(DY[2], 3)
+        load_w13(DY[2], 3, (0,))
         load_a3_half(DY[3], 3, 0)
+        load_w13(DY[2], 3, (1,))
         load_a3_half(DY[3] + 4, 3, 1)
         da3 = room(turns[1], [P, PACK * C], BF16, "da3")
         all_masks(1)
@@ -400,12 +401,13 @@ def tile_moe_bdx_glu_relu_kernel(tc, dyT, a1, a3, w2, w1, w3, gate, offs, out):
             put_back(1, sums[h], DY[5] + 4 + h, h * HALF, (h + 1) * HALF)
         quantize_w13(2, a1_at[2] + 3)
         da3_q[2] = quantize_da(da3, a1_at[2] + 7, 105)
-        put_back(2, second_product(2, 4, da1_q, da3_q[2]), 126, 0, C)
+        sums = second_product(2, 4, da1_q, da3_q[2])
 
         w13_b[3] = room(turns[0], [P, 2, PACK * K], BF16, "w13_b")
-        for n in range(2):
-            nc.gpsimd.tensor_scalar(woven(w13_b[3][:, n, :]), by_lines(w13_raw[3, n]), 1.0, 0.0, MULT, ADD)
-        da = [room(at, [P, 2, PACK * HALF], BF16, "da_last") for at in (122, turns[1])]
+        nc.gpsimd.tensor_scalar(woven(w13_b[3][:, 0, :]), by_lines(w13_raw[3, 0]), 1.0, 0.0, MULT, ADD)
+        nc.scalar.copy(out=woven(w13_b[3][:, 1, :]), in_=by_lines(w13_raw[3, 1]))
+        put_back(2, sums, DY[2] + 2, 0, C)
+        da = [room(at, [P, 2, PACK * HALF], BF16, "da_last") for at in (122, turns[0])]
 
         def last_da3(b):
             make_da3(blocks(da[b // 2][:, 1, :], b % 2, b % 2 + 1), 3, b)
@@ -416,11 +418,14 @@ def tile_moe_bdx_glu_relu_kernel(tc, dyT, a1, a3, w2, w1, w3, gate, offs, out):
 
         all_masks(3)
         make_da1(nc.gpsimd, da[0][:, 0, :], 3, 0)
-        for b in range(BLOCKS):
-            last_da3(b)
+        last_da3(0)
+        last_da3(1)
         quantize_w13(3, 192)
         finish(0, nc.scalar.copy)
-        make_da1(nc.vector, da[1][:, 0, :], 3, 1)
+        make_da1(nc.gpsimd, da[1][:, 0, :], 3, 1, 0, P)
+        last_da3(2)
+        last_da3(3)
+        make_da1(nc.vector, da[1][:, 0, :], 3, 1, P, HALF)
         finish(1, nc.vector.tensor_copy)
         nc.sync.dma_start(out[:, 0:PAIR], result[:, 0:PAIR])
         nc.scalar.dma_start(out[:, PAIR:T], result[:, PAIR:T])

from contextlib import ExitStack

import concourse.mybir as mybir
from concourse.masks import make_identity

E, C, T, K, H, N = 4, 512, 2048, 128, 512, 1024
P = 128
PACK = 4
PASSES = N // (P * PACK)
PAIR = 2 * C
BLOCKS = C // P
LINE = 4
HALF = C // 2
REACH = 3 * HALF // 4
KB = 1024

F32 = mybir.dt.float32
BF16 = mybir.dt.bfloat16
U32 = mybir.dt.uint32
U16 = mybir.dt.uint16
U8 = mybir.dt.uint8
E4M3X4 = mybir.dt.float8_e4m3fn_x4
E5M2X4 = mybir.dt.float8_e5m2_x4
MULT = mybir.AluOpType.mult
IS_GT = mybir.AluOpType.is_gt
MAX = mybir.AluOpType.max
ADD = mybir.AluOpType.add
COPY = mybir.ActivationFunctionType.Copy

FLOPS = 2 * N * H * E * C + 2 * 2 * H * K * E * C
BYTES = 4 * (N * T + 2 * H * E * C + E * N * H + 2 * E * H * K + E * C + K * T) + 2 * P * (E * C // 16)

DY = [8 * i for i in range(8)]
IDENT = 65
PIECES_V = ((0, 0, PAIR, 66), (1, 0, C, 98), (1, C, C + HALF, 106))
PIECES_S = ((0, PAIR, T, 82), (1, C + HALF, 3 * C, 110), (1, 3 * C, T, 0))
FRESH = [130, 138, 146, 154]
GATES = [162, 166]
RESULT = 170
MASKED = 178
G_WORDS = 186
G_SCALES = 202
W2_ROUND = [213, 221]
W2_CODES = [229, 234]


def tile_moe_bdx_glu_relu_kernel(tc, dyT, a1, a3, w2, w1, w3, gate, offs, out):
    nc = tc.nc

    dy_rows = dyT.rearrange("(c p t) w -> c t p w", c=PASSES, t=PACK)
    w2_rows = w2.rearrange("e (c p j) i -> e c p j i", c=PASSES, j=PACK)
    saved_rows = [a.rearrange("(p t) s -> p t s", t=PACK) for a in (a1, a3)]
    w13_rows = [w.rearrange("e (p j) k -> e p j k", j=PACK) for w in (w1, w3)]

    with ExitStack() as ctx:
        held = ctx.enter_context(tc.tile_pool(name="held", bufs=1))
        rooms = ctx.enter_context(tc.tile_pool(name="rooms", bufs=1))
        psum = ctx.enter_context(tc.psum_pool(name="psum", bufs=1))

        def room(kib, shape, dtype, name):
            at = int(kib * KB)
            return rooms.tile(shape, dtype, tag="%s_at%d" % (name, at), offset=at, align_bytes=64, name=name)[:]

        def bank(b, shape, name):
            return psum.tile(shape, F32, tag="bank%d" % b, name=name)[:]

        dy, planes, gates, gate_bank = {}, {}, {}, {}
        w2_raw, w2_b, w2_q, g_b, g_q = {}, {}, {}, {}, {}
        saved, w13_raw, w13_b, w13_q = {}, {}, {}, {}
        dh, masked, da3_q = {}, {}, {}

        def load(dst, src):
            nc.sync.dma_start(dst, src)
            return dst

        def load_w2(kib, e, c):
            w2_raw[e, c] = load(room(kib, [P, PACK, H], F32, "w2_raw"), w2_rows[e, c])

        def load_saved(kib, n, e):
            saved[n, e] = load(room(kib, [P, PACK, C], F32, "saved"), saved_rows[n][:, :, e * C : (e + 1) * C])

        def load_a3_half(kib, e, h):
            lo = e * C + h * HALF
            saved[1, e, h] = load(room(kib, [P, PACK, HALF], F32, "saved_half"), saved_rows[1][:, :, lo : lo + HALF])

        def load_w13(kib, e, which=(0, 1)):
            for n in which:
                w13_raw[e, n] = load(room(kib + 2 * n, [P, PACK, K], F32, "w13_raw"), w13_rows[n][e])

        def codes(words_at, scales_at, width, name):
            return room(words_at, [P, width], U32, name), room(scales_at, [P, width], U8, name + "_s")

        def part(pair, lo, hi):
            return pair[0][:, lo:hi], pair[1][:, lo:hi]

        def quantize(dst, src, dtype):
            nc.vector.quantize_mx(out=dst[0].bitcast(dtype), scales=dst[1], in_=src)

        def woven(x):
            return x.rearrange("p (s i t) -> p s t i", i=LINE, t=PACK)

        def by_lines(x):
            return x.rearrange("p t (s i) -> p s t i", i=LINE)

        def slots(lo, hi):
            return offsets[:, lo // 16 : hi // 16]

        def gathered(c, lo, hi):
            for key, tile in planes.items():
                if key[0] == c and key[1] <= lo and hi <= key[2]:
                    return tile[:, :, lo - key[1] : hi - key[1]]

        def unit(c, e):
            return gathered(c, e * C, (e + 1) * C)

        def over_rows(x):
            return x.unsqueeze(2).to_broadcast([P, x.shape[1], PACK, LINE])

        def spread_gates(e, b):
            gate_bank[e] = bank(b, [P, LINE, P], "spread")
            for i in range(LINE):
                nc.tensor.transpose(gate_bank[e][:, i, :], gate_runs[:, e, i : i + 1].to_broadcast([P, P]), ident)

        def gates_out(e):
            lo = e % 2 * C
            return gates[e // 2][:, lo : lo + C].rearrange("q (s i) -> q s i", i=LINE)

        def gates_in(e):
            return gate_bank[e].rearrange("q i s -> q s i")

        def gate_second_pass(engine, gates_of, e, lo, hi):
            engine.tensor_tensor(
                woven(g_b[e, 1][:, lo * PACK : hi * PACK]),
                by_lines(gathered(1, e * C + lo, e * C + hi)),
                over_rows(gates_of(e)[:, lo // LINE : hi // LINE, :]),
                MULT,
            )

        def quantize_g(e, c, words_at, scales_at):
            g_q[e, c] = codes(words_at, scales_at, C, "g_q")
            quantize(g_q[e, c], g_b[e, c], E5M2X4)

        def round_w2(e, c, copy=nc.scalar.copy):
            if c == 0:
                w2_b[e] = room((188, W2_ROUND[1], W2_ROUND[0], 189.5)[e], [P, (PASSES if e < E - 1 else 1) * PACK * H], BF16, "w2_b")
            copy(
                out=w2_b[e][:, c * PACK * H : (c + 1) * PACK * H].rearrange("p (t m u k) -> p m u t k", t=PACK, u=2, k=2),
                in_=w2_raw[e, c].rearrange("p (u k) (m t) -> p m u t k", t=PACK, k=2),
            )

        def quantize_w2(e, scales_at):
            w2_q[e] = codes(W2_CODES[e % 2], scales_at, PASSES * H, "w2_q")
            quantize(w2_q[e], w2_b[e], E4M3X4)

        def round_w13(e, kib):
            w13_b[e] = room(kib, [P, 2, PACK * K], BF16, "w13_b")
            for n in range(2):
                nc.scalar.copy(out=woven(w13_b[e][:, n, :]), in_=by_lines(w13_raw[e, n]))

        def quantize_w13(e, words_at):
            w13_q[e] = codes(words_at, 64 + 0.25 * e, 2 * K, "w13_q")
            quantize(w13_q[e], w13_b[e].rearrange("p n x -> p (n x)"), E4M3X4)

        def first_product(e):
            for b in range(BLOCKS):
                dh[e, b] = bank(b, [P, PACK, P], "dh")
                for c in range(PASSES):
                    for t in range(PACK):
                        words, scales = part(w2_q[e], c * H + t * P, c * H + (t + 1) * P)
                        moving, moving_scales = part(g_q[e, c], b * P, (b + 1) * P)
                        nc.tensor.matmul_mx(
                            out=dh[e, b][:, t, :],
                            lhsT=words.bitcast(E4M3X4),
                            lhsT_scale=scales,
                            rhs=moving.bitcast(E5M2X4),
                            rhs_scale=moving_scales,
                            start=(c == 0 and t == 0),
                            stop=(c == PASSES - 1 and t == PACK - 1),
                        )

        def saved_cols(n, e, lo, hi):
            return saved[n, e][:, :, lo * P : hi * P]

        def a3_half(e, h):
            return saved[1, e, h] if e % 2 else saved_cols(1, e, 2 * h, 2 * h + 2)

        def mask(e, b):
            if b % 2 == 0:
                masked[e, b // 2] = room((MASKED, 74)[e % 2] + 2 * b, [P, PACK, HALF], F32, "masked")
            dst = masked[e, b // 2][:, :, b % 2 * P : (b % 2 + 1) * P]
            nc.vector.scalar_tensor_tensor(dst, saved_cols(0, e, b, b + 1), 0.0, dh[e, b], op0=IS_GT, op1=MULT)

        def make_da3(dst, e, b):
            nc.vector.scalar_tensor_tensor(
                dst.rearrange("p (s t) -> p s t", t=PACK),
                saved_cols(0, e, b, b + 1).rearrange("p t s -> p s t"),
                0.0,
                dh[e, b].rearrange("p t s -> p s t"),
                op0=MAX,
                op1=MULT,
            )

        def make_da1(engine, dst, e, h, lo=0, hi=HALF):
            engine.tensor_tensor(
                woven(dst[:, lo * PACK : hi * PACK]), by_lines(a3_half(e, h)[:, :, lo:hi]), by_lines(masked[e, h][:, :, lo:hi]), MULT
            )

        def quantize_da(src, words_at, scales_at):
            dst = codes(words_at, scales_at, src.shape[1] // PACK, "da_q")
            quantize(dst, src, E5M2X4)
            return dst

        def blocks(x, lo, hi):
            return x[:, lo * PACK * P : hi * PACK * P]

        def second_product(e, b, da1_q, da3_q):
            sums = bank(b, [P, da1_q[0].shape[1]], "dx")
            for n, (moving, moving_scales) in ((1, da3_q), (0, da1_q)):
                words, scales = part(w13_q[e], n * K, (n + 1) * K)
                nc.tensor.matmul_mx(
                    out=sums,
                    lhsT=words.bitcast(E4M3X4),
                    lhsT_scale=scales,
                    rhs=moving.bitcast(E5M2X4),
                    rhs_scale=moving_scales,
                    start=(n == 1),
                    stop=(n == 0),
                )
            return sums

        def put_back(e, sums, kib, lo, hi, copy=nc.scalar.copy):
            dx = room(kib, [P, hi - lo], F32, "dx")
            copy(dx, sums)
            for at in range(lo, hi, HALF):
                nc.scalar.activation(result.indirect(slots(e * C + at, e * C + at + HALF)), dx[:, at - lo : at - lo + HALF], COPY)

        gate_runs = room(82, [P, E, LINE], F32, "gate_runs")
        nc.scalar.dma_start(gate_runs, gate[0:1, :].rearrange("o (e p i) -> p (o e) i", e=E, i=LINE))
        offsets = held.tile([P, E * C // 16], U16, name="offsets")
        nc.sync.dma_start(offsets[:], offs)
        for c in range(PASSES):
            for t in range(PACK):
                dy[c, t] = load(room(DY[c * PACK + t], [P, T], F32, "dy"), dy_rows[c, t])
        load_w2(FRESH[0], 0, 0)
        load_w2(FRESH[1], 0, 1)
        load_saved(FRESH[3], 0, 0)
        load_w2(FRESH[2], 1, 0)

        ident = room(IDENT, [P, P], F32, "ident")
        make_identity(nc, ident)
        for pair in range(2):
            gates[pair] = room(GATES[pair], [P, PAIR], F32, "gates")
        for e, copy in ((2, nc.scalar.copy), (0, nc.vector.tensor_copy), (1, nc.scalar.copy)):
            spread_gates(e, 4 + e)
            copy(gates_out(e), gates_in(e))
        spread_gates(3, 7)

        def gather_on_scalar(piece, t):
            c, lo, hi, kib = piece
            if t == 0:
                planes[c, lo, hi] = room(kib, [P, PACK, hi - lo], F32, "planes")
            nc.scalar.activation(planes[c, lo, hi][:, t, :], dy[c, t].indirect(slots(lo, hi)), COPY)

        for c, lo, hi, kib in PIECES_V:
            planes[c, lo, hi] = room(kib, [P, PACK, hi - lo], F32, "planes")
        for t in range(PACK):
            nc.vector.tensor_tensor(planes[0, 0, PAIR][:, t, :], dy[0, t].indirect(slots(0, PAIR)), gates[0], MULT)
            gather_on_scalar(PIECES_S[0], t)
        nc.vector.tensor_copy(gates_out(3), gates_in(3))
        late = room(122, [P, 2, PACK * C], BF16, "g_late")
        for e in range(2, E):
            nc.gpsimd.tensor_tensor(woven(late[:, e - 2, :]), by_lines(unit(0, e)), over_rows(gates_out(e)), MULT)
        g_b[0, 0] = room(205, [P, PACK * C], BF16, "g_b")
        for t in range(PACK):
            for c, lo, hi, kib in PIECES_V[1:]:
                if lo > 0 and t == PACK - 1:
                    nc.scalar.activation(planes[c, lo, hi][:, t, :], dy[c, t].indirect(slots(lo, hi)), COPY)
                else:
                    nc.vector.tensor_copy(planes[c, lo, hi][:, t, :], dy[c, t].indirect(slots(lo, hi)))
            gather_on_scalar(PIECES_S[1], t)
        nc.scalar.copy(out=woven(g_b[0, 0]), in_=by_lines(unit(0, 0)))
        load_w2(DY[0], 1, 1)
        load_saved(DY[1], 1, 0)
        load_saved(82, 0, 1)
        load_w2(DY[3], 2, 0)
        load_a3_half(90, 1, 0)
        load_w13(DY[2], 0)

        g_b[0, 1] = room(MASKED, [P, PACK * C], BF16, "g_b")
        gate_second_pass(nc.vector, gates_in, 0, 0, C)
        round_w2(0, 0)
        g_b[1, 0] = room(FRESH[0], [P, PACK * C], BF16, "g_b")
        nc.scalar.copy(out=woven(g_b[1, 0]), in_=by_lines(unit(0, 1)))
        quantize_g(0, 0, 98, G_SCALES)
        quantize_g(0, 1, G_WORDS, G_SCALES + 0.5)
        round_w2(0, 1, nc.vector.tensor_copy)
        quantize_w2(0, W2_CODES[0] + 4)
        first_product(0)
        both = codes(G_WORDS + 12, 188, PAIR, "g_q_late")
        quantize(both, late.rearrange("p e x -> p (e x)"), E5M2X4)
        g_q[2, 0], g_q[3, 0] = part(both, 0, C), part(both, C, PAIR)
        quantize_g(1, 0, 203, 189)
        round_w2(1, 0)
        round_w2(1, 1)
        for t in range(PACK):
            gather_on_scalar(PIECES_S[2], t)
        load_w2(FRESH[1], 2, 1)
        load_a3_half(94, 1, 1)
        load_saved(FRESH[2], 0, 2)
        load_saved(DY[4], 1, 2)
        load_w13(DY[5], 1)
        load_w2(DY[6], 3, 0)
        load_w2(DY[7], 3, 1)
        load_w13(DY[5] + 4, 2)

        result = room(RESULT, [P, T], F32, "result")
        a1_at = (FRESH[3], 82, FRESH[2])
        turns = (66, 70)

        def all_masks(e):
            for b in range(BLOCKS):
                mask(e, b)

        def all_da3(e, da3):
            for b in range(BLOCKS):
                make_da3(blocks(da3, b, b + 1), e, b)

        def half(x, h):
            return blocks(x, 2 * h, 2 * h + 2)

        g_b[1, 1] = room(128, [P, PACK * C], BF16, "g_b")
        for lo in range(0, C, HALF):
            gate_second_pass(nc.gpsimd, gates_out, 1, lo, lo + HALF)
        da3 = room(turns[0], [P, PACK * C], BF16, "da3")
        for b in range(BLOCKS):
            mask(0, b)
            make_da3(blocks(da3, b, b + 1), 0, b)
        quantize_w2(1, a1_at[0] + 7)
        quantize_g(1, 1, a1_at[0], G_SCALES + 0.5)
        first_product(1)
        da3_q[0] = quantize_da(da3, W2_ROUND[1] + 4, 105)
        round_w2(2, 0)
        round_w13(0, 205)
        round_w2(2, 1)

        g_b[2, 1] = room(W2_ROUND[1], [P, PACK * C], BF16, "g_b")
        gate_second_pass(nc.vector, gates_in, 2, 0, C)
        da1 = room(turns[0], [P, PACK * C], BF16, "da1")
        for h in range(2):
            make_da1(nc.gpsimd, half(da1, h), 0, h)
        load_saved(DY[1], 0, 3)
        load_w13(DY[2], 3, (0,))
        load_a3_half(DY[3], 3, 0)
        load_w13(DY[2], 3, (1,))
        load_a3_half(DY[3] + 4, 3, 1)
        da3 = room(turns[1], [P, PACK * C], BF16, "da3")
        all_masks(1)
        early = room(122, [P, PACK * HALF], BF16, "da1_half")
        make_da1(nc.gpsimd, early, 1, 0, 0, REACH)
        all_da3(1, da3)
        quantize_w13(0, a1_at[1] + 2)
        make_da1(nc.vector, early, 1, 0, REACH, HALF)
        sums = second_product(0, 4, quantize_da(da1, a1_at[1] + 4, 100), da3_q[0])
        quantize_w2(2, a1_at[1] + 7)
        quantize_g(2, 1, a1_at[1], G_SCALES)
        first_product(2)
        early_q = quantize_da(early, a1_at[1] + 6, 100.5)
        da3_q[1] = quantize_da(da3, W2_ROUND[0] + 4, 105.5)
        round_w13(1, 207)
        round_w2(3, 0)
        put_back(0, sums, FRESH[1], 0, C)
        round_w13(2, 209)

        g_b[3, 1] = room(W2_ROUND[0], [P, PACK * C], BF16, "g_b")
        gate_second_pass(nc.vector, gates_in, 3, 0, HALF)
        rest = room(turns[1], [P, PACK * HALF], BF16, "da1_half")
        make_da1(nc.gpsimd, rest, 1, 1)
        da3 = room(turns[0], [P, PACK * C], BF16, "da3")
        all_masks(2)
        gate_second_pass(nc.vector, gates_in, 3, HALF, C)
        da1 = room(122, [P, PACK * C], BF16, "da1")
        make_da1(nc.gpsimd, half(da1, 0), 2, 0)
        make_da1(nc.gpsimd, half(da1, 1), 2, 1, 0, REACH)
        all_da3(2, da3)
        quantize_w13(1, a1_at[2] + 2)
        make_da1(nc.vector, half(da1, 1), 2, 1, REACH, HALF)
        rest_q = quantize_da(rest, a1_at[2] + 6, 100.75)
        sums = [second_product(1, 5 + h, (early_q, rest_q)[h], part(da3_q[1], h * HALF, (h + 1) * HALF)) for h in range(2)]
        quantize_g(3, 1, a1_at[2], G_SCALES + 0.5)
        w2_q[3] = codes(W2_CODES[1], a1_at[2] + 4, PASSES * H, "w2_q")
        quantize(part(w2_q[3], 0, H), w2_b[3], E4M3X4)
        last_b = room(a1_at[2] + 7, [P, PACK * H], BF16, "w2_last")
        src = w2_raw[3, 1].rearrange("p (u k) (m t) -> p m u t k", t=PACK, k=2)
        dst = last_b.rearrange("p (t m u k) -> p m u t k", t=PACK, u=2, k=2)
        nc.scalar.copy(out=dst[:, 0 : P // 2], in_=src[:, 0 : P // 2])
        nc.vector.tensor_copy(dst[:, P // 2 : P], src[:, P // 2 : P])
        da1_q = quantize_da(da1, 190, 100)
        quantize(part(w2_q[3], H, 2 * H), last_b, E4M3X4)
        first_product(3)
        for h in range(2):
            put_back(1, sums[h], DY[5] + 4 + h, h * HALF, (h + 1) * HALF)
        quantize_w13(2, a1_at[2] + 3)
        da3_q[2] = quantize_da(da3, a1_at[2] + 7, 105)
        sums = second_product(2, 4, da1_q, da3_q[2])

        w13_b[3] = room(turns[0], [P, 2, PACK * K], BF16, "w13_b")
        nc.gpsimd.tensor_scalar(woven(w13_b[3][:, 0, :]), by_lines(w13_raw[3, 0]), 1.0, 0.0, MULT, ADD)
        nc.scalar.copy(out=woven(w13_b[3][:, 1, :]), in_=by_lines(w13_raw[3, 1]))
        put_back(2, sums, DY[2] + 2, 0, C)
        da = [room(at, [P, 2, PACK * HALF], BF16, "da_last") for at in (122, turns[0])]

        def last_da3(b):
            make_da3(blocks(da[b // 2][:, 1, :], b % 2, b % 2 + 1), 3, b)

        def finish(h, copy):
            dst = quantize_da(da[h].rearrange("p n x -> p (n x)"), 101 + 2 * h, 128.5 + 0.5 * h)
            put_back(3, second_product(3, 6 + h, part(dst, 0, HALF), part(dst, HALF, C)), DY[7] + h, h * HALF, (h + 1) * HALF, copy)

        all_masks(3)
        make_da1(nc.gpsimd, da[0][:, 0, :], 3, 0)
        last_da3(0)
        last_da3(1)
        quantize_w13(3, 192)
        finish(0, nc.scalar.copy)
        make_da1(nc.gpsimd, da[1][:, 0, :], 3, 1, 0, P)
        last_da3(2)
        last_da3(3)
        make_da1(nc.vector, da[1][:, 0, :], 3, 1, P, HALF)
        finish(1, nc.vector.tensor_copy)
        nc.sync.dma_start(out[:, 0:PAIR], result[:, 0:PAIR])
        nc.scalar.dma_start(out[:, PAIR:T], result[:, PAIR:T])
